import numpy as np
import ml_dtypes


def mxq(x, axis, fmt="e4m3"):
    dtype, down = {"e4m3": (ml_dtypes.float8_e4m3fn, 7), "e5m2": (ml_dtypes.float8_e5m2, 14)}[fmt]
    v = np.moveaxis(np.asarray(x, np.float32).astype(ml_dtypes.bfloat16).astype(np.float64), axis, -1)
    blocks = v.reshape(v.shape[:-1] + (-1, 32))
    amax = np.abs(blocks).max(-1, keepdims=True)
    byte = np.maximum(np.where(amax > 0, np.frexp(amax)[1] - 1 + 127, 0) - down, 1)
    scale = np.exp2(byte - 127.0)
    codes = (blocks / scale).astype(np.float32).astype(dtype).astype(np.float64)
    return np.moveaxis((codes * scale).reshape(v.shape), -1, axis)


WIDE = False


def mx_kscale(k):
    if not WIDE:
        return np.ones(k)
    levels = np.array([10, -10, 5, -5, 0])
    if k % 512:
        return np.exp2(np.random.permutation(np.resize(levels, k // 32))).repeat(32)
    a = np.empty((k // 512, 16))
    for p in range(k // 512):
        a[p, :8] = np.random.permutation(np.resize(levels, 8))
        for g in range(8):
            far = levels[np.abs(levels - a[p, g]) >= 10]
            a[p, g + 8] = far[np.random.randint(len(far))]
    return np.exp2(a.ravel()).repeat(32)


def f64(x):
    return np.asarray(x).astype(np.float64)


def striped(idx):
    return np.tile(idx.reshape(-1, 16).T, (8, 1)).astype(np.uint16)


def unstriped(offs):
    return offs[:16].T.reshape(-1).astype(np.int64)


def pack_weight(w):
    k, n = w.shape
    w = f64(np.asarray(w, np.float32).astype(ml_dtypes.bfloat16)).reshape(k // 32, 32, n)
    amax = np.abs(w).max(1)
    byte = np.clip(np.where(amax > 0, np.frexp(amax)[1] - 1 + 127 - 7, 1), 1, 254)
    scaled = (w * np.exp2(127.0 - byte)[:, None, :]).reshape(k, n).astype(np.float32)
    words = np.ascontiguousarray(scaled.reshape(k // 512, 128, 4, n).transpose(0, 1, 3, 2)).astype(ml_dtypes.float8_e4m3fn).view(np.uint8)
    return words, np.ascontiguousarray(byte.astype(np.uint8).reshape(k // 512, 16, n))


def unpack_weight(words, scales):
    g, p, n, _ = words.shape
    vals = np.ascontiguousarray(words).view(ml_dtypes.float8_e4m3fn).astype(np.float64) * np.repeat(np.exp2(scales.astype(np.float64) - 127.0), 8, axis=1)[..., None]
    return vals.transpose(0, 1, 3, 2).reshape(g * 512, n)


def sigmoid(v):
    return 1.0 / (1.0 + np.exp(-np.maximum(v, -700.0)))


K, T, S, V, U = 512, 1024, 512, 512, 256


def setup_inputs():
    n = np.random.standard_normal
    s = mx_kscale(K)[:, None]
    packed_xT = pack_weight(n((K, T)) * s)
    return {
        "x_words": packed_xT[0],
        "x_scales": packed_xT[1],
        "hT": (n((K, V)) / np.sqrt(K) / s).astype(np.float32),
        "gT": (n((K, V)) / np.sqrt(K) / s).astype(np.float32),
        "offs": striped(np.random.permutation(T)[:S]),
        "win": striped(np.random.permutation(S)[:U]),
        "los": striped(np.random.permutation(S)[:U]),
    }


def reference(x_words, x_scales, hT, gT, offs, win, los):
    hTq = mxq(f64(hT), 0, "e4m3")
    xq = unpack_weight(x_words, x_scales)[:, unstriped(offs)]
    gTq = mxq(f64(gT), 0, "e4m3")
    z = gTq.T @ xq
    dd = (hTq.T @ xq) - z
    return sigmoid(-0.5 * (dd[:, unstriped(win)] - dd[:, unstriped(los)]))

@@ -1,0 +1,117 @@
+from contextlib import ExitStack
+
+import concourse.mybir as mybir
+
+K, T, S, V, U = 512, 1024, 512, 512, 256
+FLOPS = 2 * 2 * K * V * S
+
+F32 = mybir.dt.float32
+BF16 = mybir.dt.bfloat16
+I32 = mybir.dt.int32
+U32 = mybir.dt.uint32
+U16 = mybir.dt.uint16
+U8 = mybir.dt.uint8
+FP8X4 = mybir.dt.float8_e4m3fn_x4
+ACT = mybir.ActivationFunctionType
+ALU = mybir.AluOpType
+
+P = 128
+PACK = 4
+TILES = V // P
+VECTOR_CASTS = 2
+
+
+def tile_picked_ydpo_dpo_p_kernel(tc, x_words, x_scales, hT, gT, offs, win, los, out):
+    nc = tc.nc
+    with ExitStack() as ctx:
+        keep = ctx.enter_context(tc.tile_pool(name="keep", bufs=1))
+        psum = ctx.enter_context(tc.psum_pool(name="psum", bufs=1))
+
+        offs_sb = keep.tile([P, S // 16], U16, name="offs_sb")
+        win_sb = keep.tile([P, U // 16], U16, name="win_sb")
+        los_sb = keep.tile([P, U // 16], U16, name="los_sb")
+        table_words = keep.tile([P, T], I32, name="table_words", align_bytes=64)
+        table_scales = keep.tile([P, T], U8, name="table_scales", align_bytes=64)
+        h_raw = [keep.tile([P, PACK, P], F32, name="h_raw%d" % i, align_bytes=64) for i in range(TILES)]
+        g_raw = [keep.tile([P, PACK, P], F32, name="g_raw%d" % i, tag="g_raw%d" % i, align_bytes=64) for i in range(TILES)]
+
+        nc.vector.memset(table_scales[:].bitcast(I32), 0)
+        nc.sync.dma_start(offs_sb[:], offs)
+        for q in range(4):
+            nc.scalar.dma_start(
+                out=table_scales[32 * q : 32 * q + 4, :].bitcast(I32),
+                in_=x_scales[0, 4 * q : 4 * q + 4, :].bitcast(I32),
+            )
+        nc.sync.dma_start(out=table_words[:], in_=x_words[0].rearrange("p n r -> p (n r)").bitcast(I32))
+        h_rows = hT.rearrange("(p j) t -> p j t", j=PACK)
+        g_rows = gT.rearrange("(p j) t -> p j t", j=PACK)
+        for i in range(TILES):
+            nc.sync.dma_start(out=h_raw[i][:], in_=h_rows[:, :, P * i : P * (i + 1)])
+            nc.sync.dma_start(out=g_raw[i][:], in_=g_rows[:, :, P * i : P * (i + 1)])
+            if i == 1:
+                nc.sync.dma_start(win_sb[:], win)
+                nc.sync.dma_start(los_sb[:], los)
+
+        warm_in = keep.tile([P, 1], F32, name="warm_in")
+        warm_out = keep.tile([P, 1], F32, name="warm_out")
+        nc.vector.memset(warm_in[:], 0.0)
+        nc.scalar.activation(warm_out[:], warm_in[:], ACT.Sigmoid)
+
+        x_scale = keep.tile([P, S], U8, name="x_scale", align_bytes=64)
+        x_code = keep.tile([P, S], U32, name="x_code", align_bytes=64)
+        nc.vector.tensor_copy(x_scale[:], table_scales[:].indirect(offs_sb[:]))
+        nc.vector.tensor_copy(x_code[:], table_words[:].bitcast(U32).indirect(offs_sb[:]))
+
+        acc = [psum.tile([P, S], F32, name="acc%d" % i) for i in range(TILES)]
+        dd = []
+        margin = [keep.tile([P, U], F32, name="margin%d" % i, align_bytes=64) for i in range(TILES)]
+
+        def multiply(i):
+            grouped = keep.tile([P, 2, P * PACK], BF16, name="grouped%d" % i, tag="grouped%d" % i, align_bytes=64)
+            h_dst = grouped[:, 0, :].rearrange("p (c i j) -> p c j i", i=4, j=PACK)
+            g_dst = grouped[:, 1, :].rearrange("p (c i j) -> p c j i", i=4, j=PACK)
+            h_src = h_raw[i][:].rearrange("p j (c i) -> p c j i", i=4)
+            g_src = g_raw[i][:].rearrange("p j (c i) -> p c j i", i=4)
+            nc.scalar.copy(h_dst, h_src)
+            if i < VECTOR_CASTS:
+                nc.vector.tensor_scalar(g_dst, g_src, -1.0, None, ALU.mult)
+            else:
+                nc.scalar.activation(g_dst, g_src, ACT.Copy, scale=-1.0)
+            codes = keep.tile([P, 2 * P], U32, name="codes%d" % i, align_bytes=64)
+            scales = keep.tile([P, 2 * P], U8, name="scales%d" % i, align_bytes=64)
+            nc.vector.quantize_mx(out=codes[:].bitcast(FP8X4), scales=scales[:], in_=grouped[:].rearrange("p a n -> p (a n)"))
+            for a in range(2):
+                nc.tensor.matmul_mx(
+                    out=acc[i][:],
+                    lhsT=codes[:, P * a : P * (a + 1)].bitcast(FP8X4),
+                    lhsT_scale=scales[:, P * a : P * (a + 1)],
+                    rhs=x_code[:].bitcast(FP8X4),
+                    rhs_scale=x_scale[:],
+                    start=(a == 0),
+                    stop=(a == 1),
+                )
+
+        def evacuate(i):
+            tag = "g_raw%d" % (i + 1) if 1 <= i < TILES - 1 else "dd%d" % i
+            dd.append(keep.tile([P, S], F32, name="dd%d" % i, tag=tag, align_bytes=64))
+            nc.scalar.copy(dd[i][:], acc[i][:])
+
+        def pick(i):
+            tag = "grouped%d" % (i + 1) if i + 1 < TILES else "rejected"
+            rejected = keep.tile([P, U], F32, name="rejected%d" % i, tag=tag, align_bytes=64)
+            nc.vector.tensor_copy(rejected[:], dd[i][:].indirect(los_sb[:]))
+            nc.vector.tensor_tensor(margin[i][:], dd[i][:].indirect(win_sb[:]), rejected[:], ALU.subtract)
+
+        def finish(i):
+            weight = h_raw[TILES - 1 - i // 2][:].rearrange("p j t -> p (j t)")[:, U * (i % 2) : U * (i % 2 + 1)]
+            nc.scalar.activation(weight, margin[i][:], ACT.Sigmoid, scale=-0.5)
+            nc.sync.dma_start(out=out[P * i : P * (i + 1), :], in_=weight)
+
+        multiply(0)
+        for i in range(TILES):
+            if i + 1 < TILES:
+                multiply(i + 1)
+            evacuate(i)
+            pick(i)
+        for i in range(TILES):
+            finish(i)

@@ -18,7 +18,6 @@ ALU = mybir.AluOpType
 P = 128
 PACK = 4
 TILES = V // P
-VECTOR_CASTS = 2
 
 
 def tile_picked_ydpo_dpo_p_kernel(tc, x_words, x_scales, hT, gT, offs, win, los, out):
@@ -37,8 +36,9 @@ def tile_picked_ydpo_dpo_p_kernel(tc, x_words, x_scales, hT, gT, offs, win, los,
 
         nc.vector.memset(table_scales[:].bitcast(I32), 0)
         nc.sync.dma_start(offs_sb[:], offs)
+        nc.sync.dma_start(los_sb[:], los)
         for q in range(4):
-            nc.scalar.dma_start(
+            nc.sync.dma_start(
                 out=table_scales[32 * q : 32 * q + 4, :].bitcast(I32),
                 in_=x_scales[0, 4 * q : 4 * q + 4, :].bitcast(I32),
             )
@@ -50,11 +50,10 @@ def tile_picked_ydpo_dpo_p_kernel(tc, x_words, x_scales, hT, gT, offs, win, los,
             nc.sync.dma_start(out=g_raw[i][:], in_=g_rows[:, :, P * i : P * (i + 1)])
             if i == 1:
                 nc.sync.dma_start(win_sb[:], win)
-                nc.sync.dma_start(los_sb[:], los)
 
         warm_in = keep.tile([P, 1], F32, name="warm_in")
         warm_out = keep.tile([P, 1], F32, name="warm_out")
-        nc.vector.memset(warm_in[:], 0.0)
+        nc.gpsimd.memset(warm_in[:], 0.0)
         nc.scalar.activation(warm_out[:], warm_in[:], ACT.Sigmoid)
 
         x_scale = keep.tile([P, S], U8, name="x_scale", align_bytes=64)
@@ -63,6 +62,7 @@ def tile_picked_ydpo_dpo_p_kernel(tc, x_words, x_scales, hT, gT, offs, win, los,
         nc.vector.tensor_copy(x_code[:], table_words[:].bitcast(U32).indirect(offs_sb[:]))
 
         acc = [psum.tile([P, S], F32, name="acc%d" % i) for i in range(TILES)]
+        acc_late = psum.tile([P, S], F32, name="acc_late")
         dd = []
         margin = [keep.tile([P, U], F32, name="margin%d" % i, align_bytes=64) for i in range(TILES)]
 
@@ -73,39 +73,60 @@ def tile_picked_ydpo_dpo_p_kernel(tc, x_words, x_scales, hT, gT, offs, win, los,
             h_src = h_raw[i][:].rearrange("p j (c i) -> p c j i", i=4)
             g_src = g_raw[i][:].rearrange("p j (c i) -> p c j i", i=4)
             nc.scalar.copy(h_dst, h_src)
-            if i < VECTOR_CASTS:
+            if i == 1:
                 nc.vector.tensor_scalar(g_dst, g_src, -1.0, None, ALU.mult)
             else:
                 nc.scalar.activation(g_dst, g_src, ACT.Copy, scale=-1.0)
-            codes = keep.tile([P, 2 * P], U32, name="codes%d" % i, align_bytes=64)
+            codes = keep.tile([P, 2 * P], U32, name="codes%d" % i, tag="codes%d" % i, align_bytes=64)
             scales = keep.tile([P, 2 * P], U8, name="scales%d" % i, align_bytes=64)
-            nc.vector.quantize_mx(out=codes[:].bitcast(FP8X4), scales=scales[:], in_=grouped[:].rearrange("p a n -> p (a n)"))
+            if i == 0:
+                for a in range(2):
+                    nc.vector.quantize_mx(
+                        out=codes[:, P * a : P * (a + 1)].bitcast(FP8X4), scales=scales[:, P * a : P * (a + 1)], in_=grouped[:, a, :]
+                    )
+                parts = [(acc[0][:, : S // 2], slice(0, S // 2)), (acc_late[:, : S // 2], slice(S // 2, S))]
+            else:
+                nc.vector.quantize_mx(out=codes[:].bitcast(FP8X4), scales=scales[:], in_=grouped[:].rearrange("p a n -> p (a n)"))
+                parts = [(acc[i][:], slice(0, S))]
             for a in range(2):
-                nc.tensor.matmul_mx(
-                    out=acc[i][:],
-                    lhsT=codes[:, P * a : P * (a + 1)].bitcast(FP8X4),
-                    lhsT_scale=scales[:, P * a : P * (a + 1)],
-                    rhs=x_code[:].bitcast(FP8X4),
-                    rhs_scale=x_scale[:],
-                    start=(a == 0),
-                    stop=(a == 1),
-                )
+                for bank, cols in parts:
+                    nc.tensor.matmul_mx(
+                        out=bank,
+                        lhsT=codes[:, P * a : P * (a + 1)].bitcast(FP8X4),
+                        lhsT_scale=scales[:, P * a : P * (a + 1)],
+                        rhs=x_code[:, cols].bitcast(FP8X4),
+                        rhs_scale=x_scale[:, cols],
+                        start=(a == 0),
+                        stop=(a == 1),
+                    )
 
         def evacuate(i):
             tag = "g_raw%d" % (i + 1) if 1 <= i < TILES - 1 else "dd%d" % i
             dd.append(keep.tile([P, S], F32, name="dd%d" % i, tag=tag, align_bytes=64))
-            nc.scalar.copy(dd[i][:], acc[i][:])
+            if i == 0:
+                nc.scalar.copy(dd[0][:, : S // 2], acc[0][:, : S // 2])
+                nc.vector.tensor_copy(dd[0][:, S // 2 :], acc_late[:, : S // 2])
+            else:
+                nc.scalar.copy(dd[i][:], acc[i][:])
+
+        def pair_ranges(i):
+            return [(0, U // 2), (U // 2, U)] if i == TILES - 1 else [(0, U)]
 
         def pick(i):
-            tag = "grouped%d" % (i + 1) if i + 1 < TILES else "rejected"
+            tag = "grouped1" if i == 0 else "rejected%d" % i
             rejected = keep.tile([P, U], F32, name="rejected%d" % i, tag=tag, align_bytes=64)
-            nc.vector.tensor_copy(rejected[:], dd[i][:].indirect(los_sb[:]))
-            nc.vector.tensor_tensor(margin[i][:], dd[i][:].indirect(win_sb[:]), rejected[:], ALU.subtract)
+            for r0, r1 in pair_ranges(i):
+                nc.vector.tensor_copy(rejected[:, r0:r1], dd[i][:].indirect(los_sb[:, r0 // 16 : r1 // 16]))
+            for r0, r1 in pair_ranges(i):
+                nc.vector.tensor_tensor(
+                    margin[i][:, r0:r1], dd[i][:].indirect(win_sb[:, r0 // 16 : r1 // 16]), rejected[:, r0:r1], ALU.subtract
+                )
 
         def finish(i):
-            weight = h_raw[TILES - 1 - i // 2][:].rearrange("p j t -> p (j t)")[:, U * (i % 2) : U * (i % 2 + 1)]
-            nc.scalar.activation(weight, margin[i][:], ACT.Sigmoid, scale=-0.5)
-            nc.sync.dma_start(out=out[P * i : P * (i + 1), :], in_=weight)
+            weight = weights[i]
+            for r0, r1 in pair_ranges(i):
+                nc.scalar.activation(weight[:, r0:r1], margin[i][:, r0:r1], ACT.Sigmoid, scale=-0.5)
+                nc.sync.dma_start(out=out[P * i : P * (i + 1), r0:r1], in_=weight[:, r0:r1])
 
         multiply(0)
         for i in range(TILES):
@@ -113,5 +134,9 @@ def tile_picked_ydpo_dpo_p_kernel(tc, x_words, x_scales, hT, gT, offs, win, los,
                 multiply(i + 1)
             evacuate(i)
             pick(i)
+        early = keep.tile([P, 2 * U], F32, name="early", tag="grouped3", align_bytes=64)
+        late = keep.tile([P, U], F32, name="late", tag="codes3", align_bytes=64)
+        last = keep.tile([P, U], F32, name="last", align_bytes=64)
+        weights = [early[:, :U], early[:, U:], late[:], last[:]]
         for i in range(TILES):
             finish(i)

@@ -18,6 +18,11 @@ ALU = mybir.AluOpType
 P = 128
 PACK = 4
 TILES = V // P
+HALVES = ((0, U // 2), (U // 2, U))
+HALVED = (0, 1, 2, 3)
+APART = (0, 1, 2, 3)
+GSUB = ()
+VCAST = (1,)
 
 
 def tile_picked_ydpo_dpo_p_kernel(tc, x_words, x_scales, hT, gT, offs, win, los, out):
@@ -61,8 +66,7 @@ def tile_picked_ydpo_dpo_p_kernel(tc, x_words, x_scales, hT, gT, offs, win, los,
         nc.vector.tensor_copy(x_scale[:], table_scales[:].indirect(offs_sb[:]))
         nc.vector.tensor_copy(x_code[:], table_words[:].bitcast(U32).indirect(offs_sb[:]))
 
-        acc = [psum.tile([P, S], F32, name="acc%d" % i) for i in range(TILES)]
-        acc_late = psum.tile([P, S], F32, name="acc_late")
+        banks = []
         dd = []
         margin = [keep.tile([P, U], F32, name="margin%d" % i, align_bytes=64) for i in range(TILES)]
 
@@ -73,60 +77,69 @@ def tile_picked_ydpo_dpo_p_kernel(tc, x_words, x_scales, hT, gT, offs, win, los,
             h_src = h_raw[i][:].rearrange("p j (c i) -> p c j i", i=4)
             g_src = g_raw[i][:].rearrange("p j (c i) -> p c j i", i=4)
             nc.scalar.copy(h_dst, h_src)
-            if i == 1:
+            if i in VCAST:
                 nc.vector.tensor_scalar(g_dst, g_src, -1.0, None, ALU.mult)
             else:
                 nc.scalar.activation(g_dst, g_src, ACT.Copy, scale=-1.0)
             codes = keep.tile([P, 2 * P], U32, name="codes%d" % i, tag="codes%d" % i, align_bytes=64)
             scales = keep.tile([P, 2 * P], U8, name="scales%d" % i, align_bytes=64)
-            if i == 0:
+            if i in APART:
                 for a in range(2):
                     nc.vector.quantize_mx(
                         out=codes[:, P * a : P * (a + 1)].bitcast(FP8X4), scales=scales[:, P * a : P * (a + 1)], in_=grouped[:, a, :]
                     )
-                parts = [(acc[0][:, : S // 2], slice(0, S // 2)), (acc_late[:, : S // 2], slice(S // 2, S))]
             else:
                 nc.vector.quantize_mx(out=codes[:].bitcast(FP8X4), scales=scales[:], in_=grouped[:].rearrange("p a n -> p (a n)"))
-                parts = [(acc[i][:], slice(0, S))]
-            for a in range(2):
-                for bank, cols in parts:
-                    nc.tensor.matmul_mx(
-                        out=bank,
-                        lhsT=codes[:, P * a : P * (a + 1)].bitcast(FP8X4),
-                        lhsT_scale=scales[:, P * a : P * (a + 1)],
-                        rhs=x_code[:, cols].bitcast(FP8X4),
-                        rhs_scale=x_scale[:, cols],
-                        start=(a == 0),
-                        stop=(a == 1),
-                    )
+            ranges = [slice(0, S // 2), slice(S // 2, S)] if i in HALVED else [slice(0, S)]
+            parts = []
+            for n, cols in enumerate(ranges):
+                bank = psum.tile([P, S], F32, name="acc%d_%d" % (i, n))
+                parts.append((bank[:, : cols.stop - cols.start], cols))
+            banks.append(parts)
+            order = [(a, b) for a in range(2) for b in parts] if i in APART else [(a, b) for b in parts for a in range(2)]
+            for a, (bank, cols) in order:
+                nc.tensor.matmul_mx(
+                    out=bank,
+                    lhsT=codes[:, P * a : P * (a + 1)].bitcast(FP8X4),
+                    lhsT_scale=scales[:, P * a : P * (a + 1)],
+                    rhs=x_code[:, cols].bitcast(FP8X4),
+                    rhs_scale=x_scale[:, cols],
+                    start=(a == 0),
+                    stop=(a == 1),
+                )
 
         def evacuate(i):
-            tag = "g_raw%d" % (i + 1) if 1 <= i < TILES - 1 else "dd%d" % i
+            tag = "g_raw%d" % (i + 1) if i < TILES - 1 else "dd%d" % i
             dd.append(keep.tile([P, S], F32, name="dd%d" % i, tag=tag, align_bytes=64))
-            if i == 0:
-                nc.scalar.copy(dd[0][:, : S // 2], acc[0][:, : S // 2])
-                nc.vector.tensor_copy(dd[0][:, S // 2 :], acc_late[:, : S // 2])
-            else:
-                nc.scalar.copy(dd[i][:], acc[i][:])
+            for n, (bank, cols) in enumerate(banks[i]):
+                if i < 0:
+                    nc.vector.tensor_copy(dd[i][:, cols], bank)
+                else:
+                    nc.scalar.copy(dd[i][:, cols], bank)
 
         def pair_ranges(i):
-            return [(0, U // 2), (U // 2, U)] if i == TILES - 1 else [(0, U)]
+            return [(0, 128), (128, U)] if i == TILES - 1 else [(0, U)]
 
         def pick(i):
-            tag = "grouped1" if i == 0 else "rejected%d" % i
-            rejected = keep.tile([P, U], F32, name="rejected%d" % i, tag=tag, align_bytes=64)
-            for r0, r1 in pair_ranges(i):
+            rejected = keep.tile([P, U], F32, name="rejected%d" % i, align_bytes=64)
+            for r0, r1 in HALVES:
                 nc.vector.tensor_copy(rejected[:, r0:r1], dd[i][:].indirect(los_sb[:, r0 // 16 : r1 // 16]))
-            for r0, r1 in pair_ranges(i):
-                nc.vector.tensor_tensor(
-                    margin[i][:, r0:r1], dd[i][:].indirect(win_sb[:, r0 // 16 : r1 // 16]), rejected[:, r0:r1], ALU.subtract
-                )
+            if i in GSUB:
+                preferred = keep.tile([P, U], F32, name="preferred%d" % i, align_bytes=64)
+                nc.vector.tensor_copy(preferred[:], dd[i][:].indirect(win_sb[:]))
+                nc.gpsimd.tensor_tensor(margin[i][:], preferred[:], rejected[:], ALU.subtract)
+            else:
+                for r0, r1 in HALVES:
+                    nc.vector.tensor_tensor(
+                        margin[i][:, r0:r1], dd[i][:].indirect(win_sb[:, r0 // 16 : r1 // 16]), rejected[:, r0:r1], ALU.subtract
+                    )
 
         def finish(i):
             weight = weights[i]
             for r0, r1 in pair_ranges(i):
                 nc.scalar.activation(weight[:, r0:r1], margin[i][:, r0:r1], ACT.Sigmoid, scale=-0.5)
-                nc.sync.dma_start(out=out[P * i : P * (i + 1), r0:r1], in_=weight[:, r0:r1])
+                queue = nc.sync if r0 > 0 else nc.sync
+                queue.dma_start(out=out[P * i : P * (i + 1), r0:r1], in_=weight[:, r0:r1])
 
         multiply(0)
         for i in range(TILES):

@@ -20,9 +20,9 @@ PACK = 4
 TILES = V // P
 HALVES = ((0, U // 2), (U // 2, U))
 HALVED = (0, 1, 2, 3)
-APART = (0, 1, 2, 3)
+APART = (0, 2, 3)
 GSUB = ()
-VCAST = (1,)
+VCAST = ()
 
 
 def tile_picked_ydpo_dpo_p_kernel(tc, x_words, x_scales, hT, gT, offs, win, los, out):
@@ -40,7 +40,10 @@ def tile_picked_ydpo_dpo_p_kernel(tc, x_words, x_scales, hT, gT, offs, win, los,
         g_raw = [keep.tile([P, PACK, P], F32, name="g_raw%d" % i, tag="g_raw%d" % i, align_bytes=64) for i in range(TILES)]
 
         nc.vector.memset(table_scales[:].bitcast(I32), 0)
+        h_rows = hT.rearrange("(p j) t -> p j t", j=PACK)
+        g_rows = gT.rearrange("(p j) t -> p j t", j=PACK)
         nc.sync.dma_start(offs_sb[:], offs)
+        nc.sync.dma_start(out=h_raw[1][:], in_=h_rows[:, :, P : 2 * P])
         nc.sync.dma_start(los_sb[:], los)
         for q in range(4):
             nc.sync.dma_start(
@@ -48,10 +51,9 @@ def tile_picked_ydpo_dpo_p_kernel(tc, x_words, x_scales, hT, gT, offs, win, los,
                 in_=x_scales[0, 4 * q : 4 * q + 4, :].bitcast(I32),
             )
         nc.sync.dma_start(out=table_words[:], in_=x_words[0].rearrange("p n r -> p (n r)").bitcast(I32))
-        h_rows = hT.rearrange("(p j) t -> p j t", j=PACK)
-        g_rows = gT.rearrange("(p j) t -> p j t", j=PACK)
         for i in range(TILES):
-            nc.sync.dma_start(out=h_raw[i][:], in_=h_rows[:, :, P * i : P * (i + 1)])
+            if i != 1:
+                nc.sync.dma_start(out=h_raw[i][:], in_=h_rows[:, :, P * i : P * (i + 1)])
             nc.sync.dma_start(out=g_raw[i][:], in_=g_rows[:, :, P * i : P * (i + 1)])
             if i == 1:
                 nc.sync.dma_start(win_sb[:], win)

@@ -18,11 +18,11 @@ ALU = mybir.AluOpType
 P = 128
 PACK = 4
 TILES = V // P
-HALVES = ((0, U // 2), (U // 2, U))
-HALVED = (0, 1, 2, 3)
-APART = (0, 2, 3)
-GSUB = ()
-VCAST = ()
+PAIR_HALVES = ((0, U // 2), (U // 2, U))
+QUARTERS = tuple(slice(c, c + S // 4) for c in range(0, S, S // 4))
+HALVES = (slice(0, S // 2), slice(S // 2, S))
+WHOLE = (slice(0, S),)
+PIECES = (QUARTERS, HALVES, WHOLE, WHOLE)
 
 
 def tile_picked_ydpo_dpo_p_kernel(tc, x_words, x_scales, hT, gT, offs, win, los, out):
@@ -36,26 +36,26 @@ def tile_picked_ydpo_dpo_p_kernel(tc, x_words, x_scales, hT, gT, offs, win, los,
         los_sb = keep.tile([P, U // 16], U16, name="los_sb")
         table_words = keep.tile([P, T], I32, name="table_words", align_bytes=64)
         table_scales = keep.tile([P, T], U8, name="table_scales", align_bytes=64)
-        h_raw = [keep.tile([P, PACK, P], F32, name="h_raw%d" % i, align_bytes=64) for i in range(TILES)]
+        h_raw = [keep.tile([P, PACK, P], F32, name="h_raw%d" % i, tag="h_raw%d" % i, align_bytes=64) for i in range(TILES)]
         g_raw = [keep.tile([P, PACK, P], F32, name="g_raw%d" % i, tag="g_raw%d" % i, align_bytes=64) for i in range(TILES)]
 
         nc.vector.memset(table_scales[:].bitcast(I32), 0)
         h_rows = hT.rearrange("(p j) t -> p j t", j=PACK)
         g_rows = gT.rearrange("(p j) t -> p j t", j=PACK)
         nc.sync.dma_start(offs_sb[:], offs)
-        nc.sync.dma_start(out=h_raw[1][:], in_=h_rows[:, :, P : 2 * P])
-        nc.sync.dma_start(los_sb[:], los)
+        nc.sync.dma_start(out=h_raw[0][:], in_=h_rows[:, :, :P])
         for q in range(4):
             nc.sync.dma_start(
                 out=table_scales[32 * q : 32 * q + 4, :].bitcast(I32),
                 in_=x_scales[0, 4 * q : 4 * q + 4, :].bitcast(I32),
             )
+        nc.sync.dma_start(out=g_raw[0][:], in_=g_rows[:, :, :P])
         nc.sync.dma_start(out=table_words[:], in_=x_words[0].rearrange("p n r -> p (n r)").bitcast(I32))
-        for i in range(TILES):
-            if i != 1:
-                nc.sync.dma_start(out=h_raw[i][:], in_=h_rows[:, :, P * i : P * (i + 1)])
+        for i in range(1, TILES):
+            nc.sync.dma_start(out=h_raw[i][:], in_=h_rows[:, :, P * i : P * (i + 1)])
             nc.sync.dma_start(out=g_raw[i][:], in_=g_rows[:, :, P * i : P * (i + 1)])
             if i == 1:
+                nc.sync.dma_start(los_sb[:], los)
                 nc.sync.dma_start(win_sb[:], win)
 
         warm_in = keep.tile([P, 1], F32, name="warm_in")
@@ -65,93 +65,106 @@ def tile_picked_ydpo_dpo_p_kernel(tc, x_words, x_scales, hT, gT, offs, win, los,
 
         x_scale = keep.tile([P, S], U8, name="x_scale", align_bytes=64)
         x_code = keep.tile([P, S], U32, name="x_code", align_bytes=64)
-        nc.vector.tensor_copy(x_scale[:], table_scales[:].indirect(offs_sb[:]))
-        nc.vector.tensor_copy(x_code[:], table_words[:].bitcast(U32).indirect(offs_sb[:]))
-
-        banks = []
+        grouped = [
+            keep.tile([P, 2 * P * PACK], BF16, name="grouped%d" % i, tag="grouped%d" % i, align_bytes=64) for i in range(TILES)
+        ]
+        codes = [keep.tile([P, 2 * P], U32, name="codes%d" % i, tag="codes%d" % i, align_bytes=64) for i in range(TILES)]
+        scales = [keep.tile([P, 2 * P], U8, name="scales%d" % i, align_bytes=64) for i in range(TILES)]
+        banks = [[psum.tile([P, S], F32, name="acc%d_%d" % (i, n)) for n in range(len(PIECES[i]))] for i in range(TILES)]
+        rejected = []
+        margin = []
         dd = []
-        margin = [keep.tile([P, U], F32, name="margin%d" % i, align_bytes=64) for i in range(TILES)]
+
+        def cast(i, side, engine):
+            raw = (h_raw, g_raw)[side][i]
+            dst = grouped[i][:, P * PACK * side : P * PACK * (side + 1)].rearrange("p (c i j) -> p c j i", i=4, j=PACK)
+            src = raw[:].rearrange("p j (c i) -> p c j i", i=4)
+            if side == 0 and engine == "vector":
+                nc.vector.tensor_copy(dst, src)
+            elif side == 0:
+                nc.scalar.copy(dst, src)
+            elif engine == "vector":
+                nc.vector.tensor_scalar(dst, src, -1.0, None, ALU.mult)
+            else:
+                nc.scalar.activation(dst, src, ACT.Copy, scale=-1.0)
+
+        def quantize(i, first, last):
+            nc.vector.quantize_mx(
+                out=codes[i][:, P * first : P * last].bitcast(FP8X4),
+                scales=scales[i][:, P * first : P * last],
+                in_=grouped[i][:, P * PACK * first : P * PACK * last],
+            )
 
         def multiply(i):
-            grouped = keep.tile([P, 2, P * PACK], BF16, name="grouped%d" % i, tag="grouped%d" % i, align_bytes=64)
-            h_dst = grouped[:, 0, :].rearrange("p (c i j) -> p c j i", i=4, j=PACK)
-            g_dst = grouped[:, 1, :].rearrange("p (c i j) -> p c j i", i=4, j=PACK)
-            h_src = h_raw[i][:].rearrange("p j (c i) -> p c j i", i=4)
-            g_src = g_raw[i][:].rearrange("p j (c i) -> p c j i", i=4)
-            nc.scalar.copy(h_dst, h_src)
-            if i in VCAST:
-                nc.vector.tensor_scalar(g_dst, g_src, -1.0, None, ALU.mult)
-            else:
-                nc.scalar.activation(g_dst, g_src, ACT.Copy, scale=-1.0)
-            codes = keep.tile([P, 2 * P], U32, name="codes%d" % i, tag="codes%d" % i, align_bytes=64)
-            scales = keep.tile([P, 2 * P], U8, name="scales%d" % i, align_bytes=64)
-            if i in APART:
-                for a in range(2):
-                    nc.vector.quantize_mx(
-                        out=codes[:, P * a : P * (a + 1)].bitcast(FP8X4), scales=scales[:, P * a : P * (a + 1)], in_=grouped[:, a, :]
+            for n, cols in enumerate(PIECES[i]):
+                for side in range(2):
+                    nc.tensor.matmul_mx(
+                        out=banks[i][n][:, : cols.stop - cols.start],
+                        lhsT=codes[i][:, P * side : P * (side + 1)].bitcast(FP8X4),
+                        lhsT_scale=scales[i][:, P * side : P * (side + 1)],
+                        rhs=x_code[:, cols].bitcast(FP8X4),
+                        rhs_scale=x_scale[:, cols],
+                        start=(side == 0),
+                        stop=(side == 1),
                     )
-            else:
-                nc.vector.quantize_mx(out=codes[:].bitcast(FP8X4), scales=scales[:], in_=grouped[:].rearrange("p a n -> p (a n)"))
-            ranges = [slice(0, S // 2), slice(S // 2, S)] if i in HALVED else [slice(0, S)]
-            parts = []
-            for n, cols in enumerate(ranges):
-                bank = psum.tile([P, S], F32, name="acc%d_%d" % (i, n))
-                parts.append((bank[:, : cols.stop - cols.start], cols))
-            banks.append(parts)
-            order = [(a, b) for a in range(2) for b in parts] if i in APART else [(a, b) for b in parts for a in range(2)]
-            for a, (bank, cols) in order:
-                nc.tensor.matmul_mx(
-                    out=bank,
-                    lhsT=codes[:, P * a : P * (a + 1)].bitcast(FP8X4),
-                    lhsT_scale=scales[:, P * a : P * (a + 1)],
-                    rhs=x_code[:, cols].bitcast(FP8X4),
-                    rhs_scale=x_scale[:, cols],
-                    start=(a == 0),
-                    stop=(a == 1),
-                )
 
         def evacuate(i):
-            tag = "g_raw%d" % (i + 1) if i < TILES - 1 else "dd%d" % i
-            dd.append(keep.tile([P, S], F32, name="dd%d" % i, tag=tag, align_bytes=64))
-            for n, (bank, cols) in enumerate(banks[i]):
-                if i < 0:
-                    nc.vector.tensor_copy(dd[i][:, cols], bank)
-                else:
-                    nc.scalar.copy(dd[i][:, cols], bank)
+            dd.append(keep.tile([P, S], F32, name="dd%d" % i, tag=("h_raw1", "h_raw3", "g_raw3", "dd3")[i], align_bytes=64))
+            for n, cols in enumerate(PIECES[i]):
+                nc.scalar.copy(dd[i][:, cols], banks[i][n][:, : cols.stop - cols.start])
 
-        def pair_ranges(i):
-            return [(0, 128), (128, U)] if i == TILES - 1 else [(0, U)]
+        def pick_rejected(i):
+            for r0, r1 in PAIR_HALVES:
+                nc.vector.tensor_copy(rejected[i][:, r0:r1], dd[i][:].indirect(los_sb[:, r0 // 16 : r1 // 16]))
 
-        def pick(i):
-            rejected = keep.tile([P, U], F32, name="rejected%d" % i, align_bytes=64)
-            for r0, r1 in HALVES:
-                nc.vector.tensor_copy(rejected[:, r0:r1], dd[i][:].indirect(los_sb[:, r0 // 16 : r1 // 16]))
-            if i in GSUB:
-                preferred = keep.tile([P, U], F32, name="preferred%d" % i, align_bytes=64)
-                nc.vector.tensor_copy(preferred[:], dd[i][:].indirect(win_sb[:]))
-                nc.gpsimd.tensor_tensor(margin[i][:], preferred[:], rejected[:], ALU.subtract)
-            else:
-                for r0, r1 in HALVES:
-                    nc.vector.tensor_tensor(
-                        margin[i][:, r0:r1], dd[i][:].indirect(win_sb[:, r0 // 16 : r1 // 16]), rejected[:, r0:r1], ALU.subtract
-                    )
+        def pick_preferred(i, half):
+            r0, r1 = PAIR_HALVES[half]
+            nc.vector.tensor_tensor(
+                margin[i][:, r0:r1], dd[i][:].indirect(win_sb[:, r0 // 16 : r1 // 16]), rejected[i][:, r0:r1], ALU.subtract
+            )
 
-        def finish(i):
-            weight = weights[i]
-            for r0, r1 in pair_ranges(i):
+        def finish(i, weight):
+            for r0, r1 in PAIR_HALVES if i == TILES - 1 else ((0, U),):
                 nc.scalar.activation(weight[:, r0:r1], margin[i][:, r0:r1], ACT.Sigmoid, scale=-0.5)
-                queue = nc.sync if r0 > 0 else nc.sync
-                queue.dma_start(out=out[P * i : P * (i + 1), r0:r1], in_=weight[:, r0:r1])
+                nc.sync.dma_start(out=out[P * i : P * (i + 1), r0:r1], in_=weight[:, r0:r1])
 
+        def gather_words():
+            for cols in PIECES[0]:
+                nc.vector.tensor_copy(
+                    x_code[:, cols], table_words[:].bitcast(U32).indirect(offs_sb[:, cols.start // 16 : cols.stop // 16])
+                )
+
+        nc.vector.tensor_copy(x_scale[:], table_scales[:].indirect(offs_sb[:]))
+        cast(0, 0, "scalar")
+        cast(0, 1, "scalar")
+        quantize(0, 0, 2)
+        gather_words()
         multiply(0)
+        cast(1, 0, "scalar")
+        evacuate(0)
+        cast(1, 1, "vector")
+        cast(2, 0, "vector")
+        quantize(1, 0, 2)
+        multiply(1)
+        cast(2, 1, "vector")
+        quantize(2, 0, 2)
+        multiply(2)
+        cast(3, 0, "scalar")
         for i in range(TILES):
-            if i + 1 < TILES:
-                multiply(i + 1)
-            evacuate(i)
-            pick(i)
+            if i > 0:
+                evacuate(i)
+            if i == 1:
+                cast(3, 1, "scalar")
+                quantize(3, 0, 2)
+                multiply(3)
+            tag = "g_raw2" if i == 0 else "rejected%d" % i
+            rejected.append(keep.tile([P, U], F32, name="rejected%d" % i, tag=tag, align_bytes=64))
+            margin.append(keep.tile([P, U], F32, name="margin%d" % i, align_bytes=64))
+            pick_rejected(i)
+            pick_preferred(i, 0)
+            pick_preferred(i, 1)
         early = keep.tile([P, 2 * U], F32, name="early", tag="grouped3", align_bytes=64)
         late = keep.tile([P, U], F32, name="late", tag="codes3", align_bytes=64)
         last = keep.tile([P, U], F32, name="last", align_bytes=64)
-        weights = [early[:, :U], early[:, U:], late[:], last[:]]
-        for i in range(TILES):
-            finish(i)
+        for i, weight in enumerate([early[:, :U], early[:, U:], late[:], last[:]]):
+            finish(i, weight)

@@ -85,6 +85,9 @@ def tile_picked_ydpo_dpo_p_kernel(tc, x_words, x_scales, hT, gT, offs, win, los,
                 nc.scalar.copy(dst, src)
             elif engine == "vector":
                 nc.vector.tensor_scalar(dst, src, -1.0, None, ALU.mult)
+            elif engine == "gpsimd":
+                plain = grouped[i][:, P * PACK * side : P * PACK * (side + 1)].rearrange("p (t j) -> p t j", j=PACK)
+                nc.gpsimd.tensor_scalar(plain, raw[:].rearrange("p j t -> p t j"), -1.0, 0.0, ALU.mult, ALU.add)
             else:
                 nc.scalar.activation(dst, src, ACT.Copy, scale=-1.0)
 
@@ -146,9 +149,7 @@ def tile_picked_ydpo_dpo_p_kernel(tc, x_words, x_scales, hT, gT, offs, win, los,
         cast(2, 0, "vector")
         quantize(1, 0, 2)
         multiply(1)
-        cast(2, 1, "vector")
-        quantize(2, 0, 2)
-        multiply(2)
+        cast(2, 1, "gpsimd")
         cast(3, 0, "scalar")
         for i in range(TILES):
             if i > 0:
@@ -157,10 +158,14 @@ def tile_picked_ydpo_dpo_p_kernel(tc, x_words, x_scales, hT, gT, offs, win, los,
                 cast(3, 1, "scalar")
                 quantize(3, 0, 2)
                 multiply(3)
-            tag = "g_raw2" if i == 0 else "rejected%d" % i
+            tag = "h_raw2" if i == 0 else "rejected%d" % i
             rejected.append(keep.tile([P, U], F32, name="rejected%d" % i, tag=tag, align_bytes=64))
-            margin.append(keep.tile([P, U], F32, name="margin%d" % i, align_bytes=64))
+            tag = "g_raw2" if i == 0 else "margin%d" % i
+            margin.append(keep.tile([P, U], F32, name="margin%d" % i, tag=tag, align_bytes=64))
             pick_rejected(i)
+            if i == 0:
+                quantize(2, 0, 2)
+                multiply(2)
             pick_preferred(i, 0)
             pick_preferred(i, 1)
         early = keep.tile([P, 2 * U], F32, name="early", tag="grouped3", align_bytes=64)

@@ -22,13 +22,14 @@ PAIR_HALVES = ((0, U // 2), (U // 2, U))
 QUARTERS = tuple(slice(c, c + S // 4) for c in range(0, S, S // 4))
 HALVES = (slice(0, S // 2), slice(S // 2, S))
 WHOLE = (slice(0, S),)
-PIECES = (QUARTERS, HALVES, WHOLE, WHOLE)
+PIECES = (QUARTERS, HALVES, WHOLE, HALVES)
 
 
 def tile_picked_ydpo_dpo_p_kernel(tc, x_words, x_scales, hT, gT, offs, win, los, out):
     nc = tc.nc
     with ExitStack() as ctx:
         keep = ctx.enter_context(tc.tile_pool(name="keep", bufs=1))
+        held = ctx.enter_context(tc.tile_pool(name="held", bufs=1))
         psum = ctx.enter_context(tc.psum_pool(name="psum", bufs=1))
 
         offs_sb = keep.tile([P, S // 16], U16, name="offs_sb")
@@ -37,7 +38,8 @@ def tile_picked_ydpo_dpo_p_kernel(tc, x_words, x_scales, hT, gT, offs, win, los,
         table_words = keep.tile([P, T], I32, name="table_words", align_bytes=64)
         table_scales = keep.tile([P, T], U8, name="table_scales", align_bytes=64)
         h_raw = [keep.tile([P, PACK, P], F32, name="h_raw%d" % i, tag="h_raw%d" % i, align_bytes=64) for i in range(TILES)]
-        g_raw = [keep.tile([P, PACK, P], F32, name="g_raw%d" % i, tag="g_raw%d" % i, align_bytes=64) for i in range(TILES)]
+        g_raw = [keep.tile([P, PACK, P], F32, name="g_raw%d" % i, tag="g_raw%d" % i, align_bytes=64) for i in range(TILES - 1)]
+        g_raw.append(held.tile([P, PACK, P], F32, name="g_raw3", offset=0))
 
         nc.vector.memset(table_scales[:].bitcast(I32), 0)
         h_rows = hT.rearrange("(p j) t -> p j t", j=PACK)
@@ -70,7 +72,13 @@ def tile_picked_ydpo_dpo_p_kernel(tc, x_words, x_scales, hT, gT, offs, win, los,
         ]
         codes = [keep.tile([P, 2 * P], U32, name="codes%d" % i, tag="codes%d" % i, align_bytes=64) for i in range(TILES)]
         scales = [keep.tile([P, 2 * P], U8, name="scales%d" % i, align_bytes=64) for i in range(TILES)]
-        banks = [[psum.tile([P, S], F32, name="acc%d_%d" % (i, n)) for n in range(len(PIECES[i]))] for i in range(TILES)]
+        banks = [
+            [
+                psum.tile([P, S], F32, name="acc%d_%d" % (i, n), tag="bank%d" % ((0, 4, 6, 0)[i] + n))
+                for n in range(len(PIECES[i]))
+            ]
+            for i in range(TILES)
+        ]
         rejected = []
         margin = []
         dd = []
@@ -79,15 +87,15 @@ def tile_picked_ydpo_dpo_p_kernel(tc, x_words, x_scales, hT, gT, offs, win, los,
             raw = (h_raw, g_raw)[side][i]
             dst = grouped[i][:, P * PACK * side : P * PACK * (side + 1)].rearrange("p (c i j) -> p c j i", i=4, j=PACK)
             src = raw[:].rearrange("p j (c i) -> p c j i", i=4)
-            if side == 0 and engine == "vector":
+            if engine == "gpsimd":
+                plain = grouped[i][:, P * PACK * side : P * PACK * (side + 1)].rearrange("p (t j) -> p t j", j=PACK)
+                nc.gpsimd.tensor_scalar(plain, raw[:].rearrange("p j t -> p t j"), 1.0 - 2.0 * side, 0.0, ALU.mult, ALU.add)
+            elif side == 0 and engine == "vector":
                 nc.vector.tensor_copy(dst, src)
             elif side == 0:
                 nc.scalar.copy(dst, src)
             elif engine == "vector":
                 nc.vector.tensor_scalar(dst, src, -1.0, None, ALU.mult)
-            elif engine == "gpsimd":
-                plain = grouped[i][:, P * PACK * side : P * PACK * (side + 1)].rearrange("p (t j) -> p t j", j=PACK)
-                nc.gpsimd.tensor_scalar(plain, raw[:].rearrange("p j t -> p t j"), -1.0, 0.0, ALU.mult, ALU.add)
             else:
                 nc.scalar.activation(dst, src, ACT.Copy, scale=-1.0)
 
@@ -112,7 +120,10 @@ def tile_picked_ydpo_dpo_p_kernel(tc, x_words, x_scales, hT, gT, offs, win, los,
                     )
 
         def evacuate(i):
-            dd.append(keep.tile([P, S], F32, name="dd%d" % i, tag=("h_raw1", "h_raw3", "g_raw3", "dd3")[i], align_bytes=64))
+            if i == 2:
+                dd.append(held.tile([P, S], F32, name="dd2", offset=1024))
+            else:
+                dd.append(keep.tile([P, S], F32, name="dd%d" % i, tag="h_raw1" if i == 0 else "dd%d" % i, align_bytes=64))
             for n, cols in enumerate(PIECES[i]):
                 nc.scalar.copy(dd[i][:, cols], banks[i][n][:, : cols.stop - cols.start])
 
@@ -123,13 +134,16 @@ def tile_picked_ydpo_dpo_p_kernel(tc, x_words, x_scales, hT, gT, offs, win, los,
         def pick_preferred(i, half):
             r0, r1 = PAIR_HALVES[half]
             nc.vector.tensor_tensor(
-                margin[i][:, r0:r1], dd[i][:].indirect(win_sb[:, r0 // 16 : r1 // 16]), rejected[i][:, r0:r1], ALU.subtract
+                margin[2 * i + half][:], dd[i][:].indirect(win_sb[:, r0 // 16 : r1 // 16]), rejected[i][:, r0:r1], ALU.subtract
             )
 
         def finish(i, weight):
-            for r0, r1 in PAIR_HALVES if i == TILES - 1 else ((0, U),):
-                nc.scalar.activation(weight[:, r0:r1], margin[i][:, r0:r1], ACT.Sigmoid, scale=-0.5)
-                nc.sync.dma_start(out=out[P * i : P * (i + 1), r0:r1], in_=weight[:, r0:r1])
+            for half, (r0, r1) in enumerate(PAIR_HALVES):
+                nc.scalar.activation(weight[:, r0:r1], margin[2 * i + half][:], ACT.Sigmoid, scale=-0.5)
+                if i == TILES - 1:
+                    nc.sync.dma_start(out=out[P * i : P * (i + 1), r0:r1], in_=weight[:, r0:r1])
+            if i < TILES - 1:
+                nc.sync.dma_start(out=out[P * i : P * (i + 1), :], in_=weight)
 
         def gather_words():
             for cols in PIECES[0]:
@@ -146,27 +160,30 @@ def tile_picked_ydpo_dpo_p_kernel(tc, x_words, x_scales, hT, gT, offs, win, los,
         cast(1, 0, "scalar")
         evacuate(0)
         cast(1, 1, "vector")
-        cast(2, 0, "vector")
         quantize(1, 0, 2)
         multiply(1)
+        cast(2, 0, "vector")
         cast(2, 1, "gpsimd")
-        cast(3, 0, "scalar")
         for i in range(TILES):
             if i > 0:
                 evacuate(i)
             if i == 1:
-                cast(3, 1, "scalar")
-                quantize(3, 0, 2)
-                multiply(3)
-            tag = "h_raw2" if i == 0 else "rejected%d" % i
-            rejected.append(keep.tile([P, U], F32, name="rejected%d" % i, tag=tag, align_bytes=64))
-            tag = "g_raw2" if i == 0 else "margin%d" % i
-            margin.append(keep.tile([P, U], F32, name="margin%d" % i, tag=tag, align_bytes=64))
-            pick_rejected(i)
-            if i == 0:
                 quantize(2, 0, 2)
                 multiply(2)
+                cast(3, 0, "scalar")
+                cast(3, 1, "scalar")
+            tag = ("h_raw2", "g_raw2", "rejected2", "rejected3")[i]
+            rejected.append(keep.tile([P, U], F32, name="rejected%d" % i, tag=tag, align_bytes=64))
+            margin.append(keep.tile([P, U // 2], F32, name="margin%d_0" % i, align_bytes=64))
+            if i == 1:
+                margin.append(held.tile([P, U // 2], F32, name="margin1_1", offset=0))
+            else:
+                margin.append(keep.tile([P, U // 2], F32, name="margin%d_1" % i, align_bytes=64))
+            pick_rejected(i)
             pick_preferred(i, 0)
+            if i == 1:
+                quantize(3, 0, 2)
+                multiply(3)
             pick_preferred(i, 1)
         early = keep.tile([P, 2 * U], F32, name="early", tag="grouped3", align_bytes=64)
         late = keep.tile([P, U], F32, name="late", tag="codes3", align_bytes=64)

@@ -48,8 +48,8 @@ def tile_picked_ydpo_dpo_p_kernel(tc, x_words, x_scales, hT, gT, offs, win, los,
         nc.sync.dma_start(out=h_raw[0][:], in_=h_rows[:, :, :P])
         for q in range(4):
             nc.sync.dma_start(
-                out=table_scales[32 * q : 32 * q + 4, :].bitcast(I32),
-                in_=x_scales[0, 4 * q : 4 * q + 4, :].bitcast(I32),
+                out=table_scales[q:P:32, :].bitcast(I32),
+                in_=x_scales[0, q:16:4, :].bitcast(I32),
             )
         nc.sync.dma_start(out=g_raw[0][:], in_=g_rows[:, :, :P])
         nc.sync.dma_start(out=table_words[:], in_=x_words[0].rearrange("p n r -> p (n r)").bitcast(I32))
@@ -68,7 +68,7 @@ def tile_picked_ydpo_dpo_p_kernel(tc, x_words, x_scales, hT, gT, offs, win, los,
         x_scale = keep.tile([P, S], U8, name="x_scale", align_bytes=64)
         x_code = keep.tile([P, S], U32, name="x_code", align_bytes=64)
         grouped = [
-            keep.tile([P, 2 * P * PACK], BF16, name="grouped%d" % i, tag="grouped%d" % i, align_bytes=64) for i in range(TILES)
+            keep.tile([P, 2 * P * PACK], BF16, name="grouped%d" % i, tag="grouped%d" % min(i, 2), align_bytes=64) for i in range(TILES)
         ]
         codes = [keep.tile([P, 2 * P], U32, name="codes%d" % i, tag="codes%d" % i, align_bytes=64) for i in range(TILES)]
         scales = [keep.tile([P, 2 * P], U8, name="scales%d" % i, align_bytes=64) for i in range(TILES)]
@@ -123,7 +123,7 @@ def tile_picked_ydpo_dpo_p_kernel(tc, x_words, x_scales, hT, gT, offs, win, los,
             if i == 2:
                 dd.append(held.tile([P, S], F32, name="dd2", offset=1024))
             else:
-                dd.append(keep.tile([P, S], F32, name="dd%d" % i, tag="h_raw1" if i == 0 else "dd%d" % i, align_bytes=64))
+                dd.append(keep.tile([P, S], F32, name="dd%d" % i, tag="h_raw2" if i == 1 else "dd%d" % i, align_bytes=64))
             for n, cols in enumerate(PIECES[i]):
                 nc.scalar.copy(dd[i][:, cols], banks[i][n][:, : cols.stop - cols.start])
 
@@ -157,22 +157,22 @@ def tile_picked_ydpo_dpo_p_kernel(tc, x_words, x_scales, hT, gT, offs, win, los,
         quantize(0, 0, 2)
         gather_words()
         multiply(0)
-        cast(1, 0, "scalar")
+        cast(1, 0, "gpsimd")
         evacuate(0)
         cast(1, 1, "vector")
         quantize(1, 0, 2)
         multiply(1)
-        cast(2, 0, "vector")
-        cast(2, 1, "gpsimd")
+        cast(2, 0, "gpsimd")
+        cast(2, 1, "scalar")
         for i in range(TILES):
             if i > 0:
                 evacuate(i)
             if i == 1:
                 quantize(2, 0, 2)
                 multiply(2)
-                cast(3, 0, "scalar")
+                cast(3, 0, "gpsimd")
                 cast(3, 1, "scalar")
-            tag = ("h_raw2", "g_raw2", "rejected2", "rejected3")[i]
+            tag = ("g_raw1", "g_raw2", "rejected2", "rejected3")[i]
             rejected.append(keep.tile([P, U], F32, name="rejected%d" % i, tag=tag, align_bytes=64))
             margin.append(keep.tile([P, U // 2], F32, name="margin%d_0" % i, align_bytes=64))
             if i == 1:
@@ -185,7 +185,7 @@ def tile_picked_ydpo_dpo_p_kernel(tc, x_words, x_scales, hT, gT, offs, win, los,
                 quantize(3, 0, 2)
                 multiply(3)
             pick_preferred(i, 1)
-        early = keep.tile([P, 2 * U], F32, name="early", tag="grouped3", align_bytes=64)
+        early = keep.tile([P, 2 * U], F32, name="early", tag="grouped2", align_bytes=64)
         late = keep.tile([P, U], F32, name="late", tag="codes3", align_bytes=64)
         last = keep.tile([P, U], F32, name="last", align_bytes=64)
         for i, weight in enumerate([early[:, :U], early[:, U:], late[:], last[:]]):

@@ -22,7 +22,7 @@ PAIR_HALVES = ((0, U // 2), (U // 2, U))
 QUARTERS = tuple(slice(c, c + S // 4) for c in range(0, S, S // 4))
 HALVES = (slice(0, S // 2), slice(S // 2, S))
 WHOLE = (slice(0, S),)
-PIECES = (QUARTERS, HALVES, WHOLE, HALVES)
+PIECES = (QUARTERS, HALVES, HALVES, HALVES)
 
 
 def tile_picked_ydpo_dpo_p_kernel(tc, x_words, x_scales, hT, gT, offs, win, los, out):
@@ -44,8 +44,8 @@ def tile_picked_ydpo_dpo_p_kernel(tc, x_words, x_scales, hT, gT, offs, win, los,
         nc.vector.memset(table_scales[:].bitcast(I32), 0)
         h_rows = hT.rearrange("(p j) t -> p j t", j=PACK)
         g_rows = gT.rearrange("(p j) t -> p j t", j=PACK)
-        nc.sync.dma_start(offs_sb[:], offs)
         nc.sync.dma_start(out=h_raw[0][:], in_=h_rows[:, :, :P])
+        nc.sync.dma_start(offs_sb[:], offs)
         for q in range(4):
             nc.sync.dma_start(
                 out=table_scales[q:P:32, :].bitcast(I32),
@@ -68,10 +68,21 @@ def tile_picked_ydpo_dpo_p_kernel(tc, x_words, x_scales, hT, gT, offs, win, los,
         x_scale = keep.tile([P, S], U8, name="x_scale", align_bytes=64)
         x_code = keep.tile([P, S], U32, name="x_code", align_bytes=64)
         grouped = [
-            keep.tile([P, 2 * P * PACK], BF16, name="grouped%d" % i, tag="grouped%d" % min(i, 2), align_bytes=64) for i in range(TILES)
+            keep.tile([P, 2 * P * PACK], BF16, name="grouped%d" % i, tag="grouped%d" % i, align_bytes=64)
+            for i in range(TILES - 1)
         ]
+        grouped3 = [
+            keep.tile([P, P * PACK], BF16, name="grouped3h", tag="grouped2", align_bytes=64),
+            keep.tile([P, P * PACK], BF16, name="grouped3g", align_bytes=64),
+        ]
+
+        def grouped_part(i, first, last):
+            if i == TILES - 1:
+                return grouped3[first][:]
+            return grouped[i][:, P * PACK * first : P * PACK * last]
+
         codes = [keep.tile([P, 2 * P], U32, name="codes%d" % i, tag="codes%d" % i, align_bytes=64) for i in range(TILES)]
-        scales = [keep.tile([P, 2 * P], U8, name="scales%d" % i, align_bytes=64) for i in range(TILES)]
+        scales = [keep.tile([P, 2 * P], U8, name="scales%d" % i, tag="scales%d" % i, align_bytes=64) for i in range(TILES)]
         banks = [
             [
                 psum.tile([P, S], F32, name="acc%d_%d" % (i, n), tag="bank%d" % ((0, 4, 6, 0)[i] + n))
@@ -79,16 +90,14 @@ def tile_picked_ydpo_dpo_p_kernel(tc, x_words, x_scales, hT, gT, offs, win, los,
             ]
             for i in range(TILES)
         ]
-        rejected = []
-        margin = []
         dd = []
 
         def cast(i, side, engine):
             raw = (h_raw, g_raw)[side][i]
-            dst = grouped[i][:, P * PACK * side : P * PACK * (side + 1)].rearrange("p (c i j) -> p c j i", i=4, j=PACK)
+            dst = grouped_part(i, side, side + 1).rearrange("p (c i j) -> p c j i", i=4, j=PACK)
             src = raw[:].rearrange("p j (c i) -> p c j i", i=4)
             if engine == "gpsimd":
-                plain = grouped[i][:, P * PACK * side : P * PACK * (side + 1)].rearrange("p (t j) -> p t j", j=PACK)
+                plain = grouped_part(i, side, side + 1).rearrange("p (t j) -> p t j", j=PACK)
                 nc.gpsimd.tensor_scalar(plain, raw[:].rearrange("p j t -> p t j"), 1.0 - 2.0 * side, 0.0, ALU.mult, ALU.add)
             elif side == 0 and engine == "vector":
                 nc.vector.tensor_copy(dst, src)
@@ -103,7 +112,7 @@ def tile_picked_ydpo_dpo_p_kernel(tc, x_words, x_scales, hT, gT, offs, win, los,
             nc.vector.quantize_mx(
                 out=codes[i][:, P * first : P * last].bitcast(FP8X4),
                 scales=scales[i][:, P * first : P * last],
-                in_=grouped[i][:, P * PACK * first : P * PACK * last],
+                in_=grouped_part(i, first, last),
             )
 
         def multiply(i):
@@ -127,35 +136,34 @@ def tile_picked_ydpo_dpo_p_kernel(tc, x_words, x_scales, hT, gT, offs, win, los,
             for n, cols in enumerate(PIECES[i]):
                 nc.scalar.copy(dd[i][:, cols], banks[i][n][:, : cols.stop - cols.start])
 
-        def pick_rejected(i):
+        def gather(dst, i, offsets, r0, r1):
+            nc.vector.tensor_copy(dst, dd[i][:].indirect(offsets[:, r0 // 16 : r1 // 16]))
+
+        def gather_subtract(dst, i, rejected, r0, r1):
+            nc.vector.tensor_tensor(dst, dd[i][:].indirect(win_sb[:, r0 // 16 : r1 // 16]), rejected, ALU.subtract)
+
+        def pick(i, tag):
+            rejected = keep.tile([P, U], F32, name="rejected%d" % i, tag=tag, align_bytes=64)
+            margin = keep.tile([P, U], F32, name="margin%d" % i, align_bytes=64)
             for r0, r1 in PAIR_HALVES:
-                nc.vector.tensor_copy(rejected[i][:, r0:r1], dd[i][:].indirect(los_sb[:, r0 // 16 : r1 // 16]))
+                gather(rejected[:, r0:r1], i, los_sb, r0, r1)
+            for r0, r1 in PAIR_HALVES:
+                gather_subtract(margin[:, r0:r1], i, rejected[:, r0:r1], r0, r1)
+            return margin
 
-        def pick_preferred(i, half):
-            r0, r1 = PAIR_HALVES[half]
-            nc.vector.tensor_tensor(
-                margin[2 * i + half][:], dd[i][:].indirect(win_sb[:, r0 // 16 : r1 // 16]), rejected[i][:, r0:r1], ALU.subtract
-            )
+        def finish(i, weight, margin, r0, r1):
+            nc.scalar.activation(weight, margin, ACT.Sigmoid, scale=-0.5)
+            nc.sync.dma_start(out=out[P * i : P * (i + 1), r0:r1], in_=weight)
 
-        def finish(i, weight):
-            for half, (r0, r1) in enumerate(PAIR_HALVES):
-                nc.scalar.activation(weight[:, r0:r1], margin[2 * i + half][:], ACT.Sigmoid, scale=-0.5)
-                if i == TILES - 1:
-                    nc.sync.dma_start(out=out[P * i : P * (i + 1), r0:r1], in_=weight[:, r0:r1])
-            if i < TILES - 1:
-                nc.sync.dma_start(out=out[P * i : P * (i + 1), :], in_=weight)
-
-        def gather_words():
-            for cols in PIECES[0]:
-                nc.vector.tensor_copy(
-                    x_code[:, cols], table_words[:].bitcast(U32).indirect(offs_sb[:, cols.start // 16 : cols.stop // 16])
-                )
-
+        H = U // 2
         nc.vector.tensor_copy(x_scale[:], table_scales[:].indirect(offs_sb[:]))
         cast(0, 0, "scalar")
         cast(0, 1, "scalar")
         quantize(0, 0, 2)
-        gather_words()
+        for cols in PIECES[0]:
+            nc.vector.tensor_copy(
+                x_code[:, cols], table_words[:].bitcast(U32).indirect(offs_sb[:, cols.start // 16 : cols.stop // 16])
+            )
         multiply(0)
         cast(1, 0, "gpsimd")
         evacuate(0)
@@ -164,29 +172,33 @@ def tile_picked_ydpo_dpo_p_kernel(tc, x_words, x_scales, hT, gT, offs, win, los,
         multiply(1)
         cast(2, 0, "gpsimd")
         cast(2, 1, "scalar")
-        for i in range(TILES):
-            if i > 0:
-                evacuate(i)
-            if i == 1:
-                quantize(2, 0, 2)
-                multiply(2)
-                cast(3, 0, "gpsimd")
-                cast(3, 1, "scalar")
-            tag = ("g_raw1", "g_raw2", "rejected2", "rejected3")[i]
-            rejected.append(keep.tile([P, U], F32, name="rejected%d" % i, tag=tag, align_bytes=64))
-            margin.append(keep.tile([P, U // 2], F32, name="margin%d_0" % i, align_bytes=64))
-            if i == 1:
-                margin.append(held.tile([P, U // 2], F32, name="margin1_1", offset=0))
-            else:
-                margin.append(keep.tile([P, U // 2], F32, name="margin%d_1" % i, align_bytes=64))
-            pick_rejected(i)
-            pick_preferred(i, 0)
-            if i == 1:
-                quantize(3, 0, 2)
-                multiply(3)
-            pick_preferred(i, 1)
-        early = keep.tile([P, 2 * U], F32, name="early", tag="grouped2", align_bytes=64)
-        late = keep.tile([P, U], F32, name="late", tag="codes3", align_bytes=64)
+        margin0 = pick(0, "g_raw1")
+        evacuate(1)
+        quantize(2, 0, 2)
+        multiply(2)
+        cast(3, 0, "gpsimd")
+        cast(3, 1, "scalar")
+        rejected1 = keep.tile([P, U], F32, name="rejected1", tag="g_raw2", align_bytes=64)
+        preferred1a = keep.tile([P, H], F32, name="preferred1a", align_bytes=64)
+        preferred1b = held.tile([P, H], F32, name="preferred1b", offset=0)
+        gather(rejected1[:], 1, los_sb, 0, U)
+        gather(preferred1a[:], 1, win_sb, 0, H)
+        quantize(3, 0, 1)
+        quantize(3, 1, 2)
+        multiply(3)
+        gather(preferred1b[:], 1, win_sb, H, U)
+        margin1 = keep.tile([P, U], F32, name="margin1", tag="grouped2", align_bytes=64)
+        nc.gpsimd.tensor_tensor(margin1[:, :H], preferred1a[:], rejected1[:, :H], ALU.subtract)
+        nc.gpsimd.tensor_tensor(margin1[:, H:], preferred1b[:], rejected1[:, H:], ALU.subtract)
+        evacuate(2)
+        margin2 = pick(2, "rejected2")
+        evacuate(3)
+        margin3 = pick(3, "rejected3")
+        early = keep.tile([P, 2 * U], F32, name="early", tag="codes3", align_bytes=64)
+        late = keep.tile([P, U], F32, name="late", tag="scales3", align_bytes=64)
         last = keep.tile([P, U], F32, name="last", align_bytes=64)
-        for i, weight in enumerate([early[:, :U], early[:, U:], late[:], last[:]]):
-            finish(i, weight)
+        finish(0, early[:, :U], margin0[:], 0, U)
+        finish(1, early[:, U:], margin1[:], 0, U)
+        finish(2, late[:], margin2[:], 0, U)
+        for r0, r1 in PAIR_HALVES:
+            finish(3, last[:, r0:r1], margin3[:, r0:r1], r0, r1)

@@ -17,45 +17,56 @@ ALU = mybir.AluOpType
 
 P = 128
 PACK = 4
+LINE = 4
 TILES = V // P
-PAIR_HALVES = ((0, U // 2), (U // 2, U))
+H, G = 0, 1
+SIGNS = (1.0, -1.0)
+FIRST, SECOND = slice(0, U // 2), slice(U // 2, U)
+
 QUARTERS = tuple(slice(c, c + S // 4) for c in range(0, S, S // 4))
 HALVES = (slice(0, S // 2), slice(S // 2, S))
-WHOLE = (slice(0, S),)
 PIECES = (QUARTERS, HALVES, HALVES, HALVES)
+FIRST_BANK = (0, 4, 6, 0)
+
+
+def entries(list_tile, part):
+    return list_tile[:, part.start // 16 : part.stop // 16]
 
 
 def tile_picked_ydpo_dpo_p_kernel(tc, x_words, x_scales, hT, gT, offs, win, los, out):
     nc = tc.nc
     with ExitStack() as ctx:
         keep = ctx.enter_context(tc.tile_pool(name="keep", bufs=1))
-        held = ctx.enter_context(tc.tile_pool(name="held", bufs=1))
         psum = ctx.enter_context(tc.psum_pool(name="psum", bufs=1))
+
+        def sbuf(name, columns, dtype, takes_over=None):
+            return keep.tile([P, columns], dtype, name=name, tag=takes_over or name, align_bytes=64)
 
         offs_sb = keep.tile([P, S // 16], U16, name="offs_sb")
         win_sb = keep.tile([P, U // 16], U16, name="win_sb")
         los_sb = keep.tile([P, U // 16], U16, name="los_sb")
-        table_words = keep.tile([P, T], I32, name="table_words", align_bytes=64)
-        table_scales = keep.tile([P, T], U8, name="table_scales", align_bytes=64)
-        h_raw = [keep.tile([P, PACK, P], F32, name="h_raw%d" % i, tag="h_raw%d" % i, align_bytes=64) for i in range(TILES)]
-        g_raw = [keep.tile([P, PACK, P], F32, name="g_raw%d" % i, tag="g_raw%d" % i, align_bytes=64) for i in range(TILES - 1)]
-        g_raw.append(held.tile([P, PACK, P], F32, name="g_raw3", offset=0))
+        table_words = sbuf("table_words", T, I32)
+        table_scales = sbuf("table_scales", T, U8)
+        raw = [
+            [keep.tile([P, PACK, P], F32, name="%s_raw%d" % (n, i), tag="%s_raw%d" % (n, i), align_bytes=64) for i in range(TILES)]
+            for n in "hg"
+        ]
+        rows = [a.rearrange("(p j) t -> p j t", j=PACK) for a in (hT, gT)]
+
+        def load(i, side):
+            nc.sync.dma_start(out=raw[side][i][:], in_=rows[side][:, :, P * i : P * (i + 1)])
 
         nc.vector.memset(table_scales[:].bitcast(I32), 0)
-        h_rows = hT.rearrange("(p j) t -> p j t", j=PACK)
-        g_rows = gT.rearrange("(p j) t -> p j t", j=PACK)
-        nc.sync.dma_start(out=h_raw[0][:], in_=h_rows[:, :, :P])
+
+        load(0, H)
         nc.sync.dma_start(offs_sb[:], offs)
-        for q in range(4):
-            nc.sync.dma_start(
-                out=table_scales[q:P:32, :].bitcast(I32),
-                in_=x_scales[0, q:16:4, :].bitcast(I32),
-            )
-        nc.sync.dma_start(out=g_raw[0][:], in_=g_rows[:, :, :P])
+        for r in range(4):
+            nc.sync.dma_start(out=table_scales[r:P:32, :].bitcast(I32), in_=x_scales[0, r:16:4, :].bitcast(I32))
+        load(0, G)
         nc.sync.dma_start(out=table_words[:], in_=x_words[0].rearrange("p n r -> p (n r)").bitcast(I32))
         for i in range(1, TILES):
-            nc.sync.dma_start(out=h_raw[i][:], in_=h_rows[:, :, P * i : P * (i + 1)])
-            nc.sync.dma_start(out=g_raw[i][:], in_=g_rows[:, :, P * i : P * (i + 1)])
+            load(i, H)
+            load(i, G)
             if i == 1:
                 nc.sync.dma_start(los_sb[:], los)
                 nc.sync.dma_start(win_sb[:], win)
@@ -65,140 +76,139 @@ def tile_picked_ydpo_dpo_p_kernel(tc, x_words, x_scales, hT, gT, offs, win, los,
         nc.gpsimd.memset(warm_in[:], 0.0)
         nc.scalar.activation(warm_out[:], warm_in[:], ACT.Sigmoid)
 
-        x_scale = keep.tile([P, S], U8, name="x_scale", align_bytes=64)
-        x_code = keep.tile([P, S], U32, name="x_code", align_bytes=64)
-        grouped = [
-            keep.tile([P, 2 * P * PACK], BF16, name="grouped%d" % i, tag="grouped%d" % i, align_bytes=64)
-            for i in range(TILES - 1)
-        ]
-        grouped3 = [
-            keep.tile([P, P * PACK], BF16, name="grouped3h", tag="grouped2", align_bytes=64),
-            keep.tile([P, P * PACK], BF16, name="grouped3g", align_bytes=64),
-        ]
-
-        def grouped_part(i, first, last):
-            if i == TILES - 1:
-                return grouped3[first][:]
-            return grouped[i][:, P * PACK * first : P * PACK * last]
-
-        codes = [keep.tile([P, 2 * P], U32, name="codes%d" % i, tag="codes%d" % i, align_bytes=64) for i in range(TILES)]
-        scales = [keep.tile([P, 2 * P], U8, name="scales%d" % i, tag="scales%d" % i, align_bytes=64) for i in range(TILES)]
+        x_scale = sbuf("x_scale", S, U8)
+        x_code = sbuf("x_code", S, U32)
+        grouped = [sbuf("grouped%d" % i, 2 * P * PACK, BF16) for i in range(TILES - 1)]
+        grouped_last = [sbuf("grouped3h", P * PACK, BF16), sbuf("grouped3g", P * PACK, BF16, takes_over="grouped2")]
+        codes = [sbuf("codes%d" % i, 2 * P, U32) for i in range(TILES)]
+        scales = [sbuf("scales%d" % i, 2 * P, U8) for i in range(TILES)]
         banks = [
             [
-                psum.tile([P, S], F32, name="acc%d_%d" % (i, n), tag="bank%d" % ((0, 4, 6, 0)[i] + n))
+                psum.tile([P, S], F32, name="acc%d_%d" % (i, n), tag="bank%d" % (FIRST_BANK[i] + n))
                 for n in range(len(PIECES[i]))
             ]
             for i in range(TILES)
         ]
-        dd = []
 
-        def cast(i, side, engine):
-            raw = (h_raw, g_raw)[side][i]
-            dst = grouped_part(i, side, side + 1).rearrange("p (c i j) -> p c j i", i=4, j=PACK)
-            src = raw[:].rearrange("p j (c i) -> p c j i", i=4)
-            if engine == "gpsimd":
-                plain = grouped_part(i, side, side + 1).rearrange("p (t j) -> p t j", j=PACK)
-                nc.gpsimd.tensor_scalar(plain, raw[:].rearrange("p j t -> p t j"), 1.0 - 2.0 * side, 0.0, ALU.mult, ALU.add)
-            elif side == 0 and engine == "vector":
-                nc.vector.tensor_copy(dst, src)
-            elif side == 0:
+        def side_of(i, side):
+            if i == TILES - 1:
+                return grouped_last[side][:]
+            return grouped[i][:, P * PACK * side : P * PACK * (side + 1)]
+
+        def by_lines(i, side):
+            dst = side_of(i, side).rearrange("p (c l j) -> p c j l", l=LINE, j=PACK)
+            return dst, raw[side][i][:].rearrange("p j (c l) -> p c j l", l=LINE)
+
+        def cast_on_scalar(i, side):
+            dst, src = by_lines(i, side)
+            if side == H:
                 nc.scalar.copy(dst, src)
-            elif engine == "vector":
-                nc.vector.tensor_scalar(dst, src, -1.0, None, ALU.mult)
             else:
-                nc.scalar.activation(dst, src, ACT.Copy, scale=-1.0)
+                nc.scalar.activation(dst, src, ACT.Copy, scale=SIGNS[side])
 
-        def quantize(i, first, last):
-            nc.vector.quantize_mx(
-                out=codes[i][:, P * first : P * last].bitcast(FP8X4),
-                scales=scales[i][:, P * first : P * last],
-                in_=grouped_part(i, first, last),
-            )
+        def cast_on_vector(i, side):
+            dst, src = by_lines(i, side)
+            nc.vector.tensor_scalar(dst, src, SIGNS[side], None, ALU.mult)
+
+        def cast_on_gpsimd(i, side):
+            dst = side_of(i, side).rearrange("p (t j) -> p t j", j=PACK)
+            nc.gpsimd.tensor_scalar(dst, raw[side][i][:].rearrange("p j t -> p t j"), SIGNS[side], 0.0, ALU.mult, ALU.add)
+
+        def quantize_both(i):
+            nc.vector.quantize_mx(out=codes[i][:].bitcast(FP8X4), scales=scales[i][:], in_=grouped[i][:])
+
+        def quantize_side(i, side):
+            cols = slice(P * side, P * (side + 1))
+            nc.vector.quantize_mx(out=codes[i][:, cols].bitcast(FP8X4), scales=scales[i][:, cols], in_=side_of(i, side))
 
         def multiply(i):
-            for n, cols in enumerate(PIECES[i]):
-                for side in range(2):
+            for bank, cols in zip(banks[i], PIECES[i]):
+                for side in (H, G):
                     nc.tensor.matmul_mx(
-                        out=banks[i][n][:, : cols.stop - cols.start],
+                        out=bank[:, : cols.stop - cols.start],
                         lhsT=codes[i][:, P * side : P * (side + 1)].bitcast(FP8X4),
                         lhsT_scale=scales[i][:, P * side : P * (side + 1)],
                         rhs=x_code[:, cols].bitcast(FP8X4),
                         rhs_scale=x_scale[:, cols],
-                        start=(side == 0),
-                        stop=(side == 1),
+                        start=(side == H),
+                        stop=(side == G),
                     )
 
-        def evacuate(i):
-            if i == 2:
-                dd.append(held.tile([P, S], F32, name="dd2", offset=1024))
-            else:
-                dd.append(keep.tile([P, S], F32, name="dd%d" % i, tag="h_raw2" if i == 1 else "dd%d" % i, align_bytes=64))
-            for n, cols in enumerate(PIECES[i]):
-                nc.scalar.copy(dd[i][:, cols], banks[i][n][:, : cols.stop - cols.start])
+        def evacuate(i, takes_over=None):
+            dd = sbuf("dd%d" % i, S, F32, takes_over)
+            for bank, cols in zip(banks[i], PIECES[i]):
+                nc.scalar.copy(dd[:, cols], bank[:, : cols.stop - cols.start])
+            return dd
 
-        def gather(dst, i, offsets, r0, r1):
-            nc.vector.tensor_copy(dst, dd[i][:].indirect(offsets[:, r0 // 16 : r1 // 16]))
+        def gather(dst, dd, list_tile, pairs):
+            nc.vector.tensor_copy(dst, dd[:].indirect(entries(list_tile, pairs)))
 
-        def gather_subtract(dst, i, rejected, r0, r1):
-            nc.vector.tensor_tensor(dst, dd[i][:].indirect(win_sb[:, r0 // 16 : r1 // 16]), rejected, ALU.subtract)
+        def gather_subtract(dst, dd, rejected, pairs):
+            nc.vector.tensor_tensor(dst, dd[:].indirect(entries(win_sb, pairs)), rejected[:, pairs], ALU.subtract)
 
-        def pick(i, tag):
-            rejected = keep.tile([P, U], F32, name="rejected%d" % i, tag=tag, align_bytes=64)
-            margin = keep.tile([P, U], F32, name="margin%d" % i, align_bytes=64)
-            for r0, r1 in PAIR_HALVES:
-                gather(rejected[:, r0:r1], i, los_sb, r0, r1)
-            for r0, r1 in PAIR_HALVES:
-                gather_subtract(margin[:, r0:r1], i, rejected[:, r0:r1], r0, r1)
+        def pick(i, dd, takes_over=None):
+            rejected = sbuf("rejected%d" % i, U, F32, takes_over)
+            margin = sbuf("margin%d" % i, U, F32)
+            for pairs in (FIRST, SECOND):
+                gather(rejected[:, pairs], dd, los_sb, pairs)
+            for pairs in (FIRST, SECOND):
+                gather_subtract(margin[:, pairs], dd, rejected, pairs)
             return margin
 
-        def finish(i, weight, margin, r0, r1):
+        def weigh(weight, margin):
             nc.scalar.activation(weight, margin, ACT.Sigmoid, scale=-0.5)
-            nc.sync.dma_start(out=out[P * i : P * (i + 1), r0:r1], in_=weight)
 
-        H = U // 2
+        def store(i, weight, pairs):
+            nc.sync.dma_start(out=out[P * i : P * (i + 1), pairs], in_=weight)
+
         nc.vector.tensor_copy(x_scale[:], table_scales[:].indirect(offs_sb[:]))
-        cast(0, 0, "scalar")
-        cast(0, 1, "scalar")
-        quantize(0, 0, 2)
+        cast_on_scalar(0, H)
+        cast_on_scalar(0, G)
+        quantize_both(0)
         for cols in PIECES[0]:
-            nc.vector.tensor_copy(
-                x_code[:, cols], table_words[:].bitcast(U32).indirect(offs_sb[:, cols.start // 16 : cols.stop // 16])
-            )
+            nc.vector.tensor_copy(x_code[:, cols], table_words[:].bitcast(U32).indirect(entries(offs_sb, cols)))
         multiply(0)
-        cast(1, 0, "gpsimd")
-        evacuate(0)
-        cast(1, 1, "vector")
-        quantize(1, 0, 2)
+        cast_on_gpsimd(1, H)
+        dd0 = evacuate(0)
+
+        cast_on_vector(1, G)
+        quantize_both(1)
         multiply(1)
-        cast(2, 0, "gpsimd")
-        cast(2, 1, "scalar")
-        margin0 = pick(0, "g_raw1")
-        evacuate(1)
-        quantize(2, 0, 2)
+        cast_on_gpsimd(2, H)
+        cast_on_scalar(2, G)
+        margin0 = pick(0, dd0, takes_over="g_raw1")
+
+        dd1 = evacuate(1, takes_over="h_raw2")
+        quantize_both(2)
         multiply(2)
-        cast(3, 0, "gpsimd")
-        cast(3, 1, "scalar")
-        rejected1 = keep.tile([P, U], F32, name="rejected1", tag="g_raw2", align_bytes=64)
-        preferred1a = keep.tile([P, H], F32, name="preferred1a", align_bytes=64)
-        preferred1b = held.tile([P, H], F32, name="preferred1b", offset=0)
-        gather(rejected1[:], 1, los_sb, 0, U)
-        gather(preferred1a[:], 1, win_sb, 0, H)
-        quantize(3, 0, 1)
-        quantize(3, 1, 2)
+        cast_on_scalar(3, H)
+        cast_on_gpsimd(3, G)
+
+        rejected1 = sbuf("rejected1", U, F32, takes_over="g_raw2")
+        preferred1 = sbuf("preferred1", U // 2, F32)
+        margin1_second = sbuf("margin1_second", U // 2, F32, takes_over="g_raw3")
+        gather(rejected1[:], dd1, los_sb, slice(0, U))
+        gather(preferred1[:], dd1, win_sb, FIRST)
+        quantize_side(3, H)
+        quantize_side(3, G)
         multiply(3)
-        gather(preferred1b[:], 1, win_sb, H, U)
-        margin1 = keep.tile([P, U], F32, name="margin1", tag="grouped2", align_bytes=64)
-        nc.gpsimd.tensor_tensor(margin1[:, :H], preferred1a[:], rejected1[:, :H], ALU.subtract)
-        nc.gpsimd.tensor_tensor(margin1[:, H:], preferred1b[:], rejected1[:, H:], ALU.subtract)
-        evacuate(2)
-        margin2 = pick(2, "rejected2")
-        evacuate(3)
-        margin3 = pick(3, "rejected3")
-        early = keep.tile([P, 2 * U], F32, name="early", tag="codes3", align_bytes=64)
-        late = keep.tile([P, U], F32, name="late", tag="scales3", align_bytes=64)
-        last = keep.tile([P, U], F32, name="last", align_bytes=64)
-        finish(0, early[:, :U], margin0[:], 0, U)
-        finish(1, early[:, U:], margin1[:], 0, U)
-        finish(2, late[:], margin2[:], 0, U)
-        for r0, r1 in PAIR_HALVES:
-            finish(3, last[:, r0:r1], margin3[:, r0:r1], r0, r1)
+        gather_subtract(margin1_second[:], dd1, rejected1, SECOND)
+        margin1_first = sbuf("margin1_first", U // 2, F32, takes_over="grouped2")
+        nc.gpsimd.tensor_tensor(margin1_first[:], preferred1[:], rejected1[:, FIRST], ALU.subtract)
+
+        margin2 = pick(2, evacuate(2, takes_over="h_raw3"), takes_over="grouped3h")
+        margin3 = pick(3, evacuate(3))
+
+        early = sbuf("early", 2 * U, F32, takes_over="codes3")
+        late = sbuf("late", U, F32, takes_over="scales3")
+        last = sbuf("last", U, F32)
+        weigh(early[:, :U], margin0[:])
+        store(0, early[:, :U], slice(0, U))
+        weigh(early[:, U : U + U // 2], margin1_first[:])
+        weigh(early[:, U + U // 2 :], margin1_second[:])
+        store(1, early[:, U:], slice(0, U))
+        weigh(late[:], margin2[:])
+        store(2, late[:], slice(0, U))
+        for pairs in (FIRST, SECOND):
+            weigh(last[:, pairs], margin3[:, pairs])
+            store(3, last[:, pairs], pairs)

@@ -21,6 +21,8 @@ LINE = 4
 TILES = V // P
 H, G = 0, 1
 SIGNS = (1.0, -1.0)
+SCALE_ROWS = K // 32
+QUADRANT = 32
 FIRST, SECOND = slice(0, U // 2), slice(U // 2, U)
 
 QUARTERS = tuple(slice(c, c + S // 4) for c in range(0, S, S // 4))
@@ -58,10 +60,14 @@ def tile_picked_ydpo_dpo_p_kernel(tc, x_words, x_scales, hT, gT, offs, win, los,
 
         nc.vector.memset(table_scales[:].bitcast(I32), 0)
 
-        load(0, H)
         nc.sync.dma_start(offs_sb[:], offs)
-        for r in range(4):
-            nc.sync.dma_start(out=table_scales[r:P:32, :].bitcast(I32), in_=x_scales[0, r:16:4, :].bitcast(I32))
+        load(0, H)
+        per_quadrant = SCALE_ROWS * QUADRANT // P
+        for r in range(per_quadrant):
+            nc.sync.dma_start(
+                out=table_scales[r:P:QUADRANT, :].bitcast(I32),
+                in_=x_scales[0, r:SCALE_ROWS:per_quadrant, :].bitcast(I32),
+            )
         load(0, G)
         nc.sync.dma_start(out=table_words[:], in_=x_words[0].rearrange("p n r -> p (n r)").bitcast(I32))
         for i in range(1, TILES):

@@ -24,6 +24,7 @@ SIGNS = (1.0, -1.0)
 SCALE_ROWS = K // 32
 QUADRANT = 32
 FIRST, SECOND = slice(0, U // 2), slice(U // 2, U)
+ALL = slice(0, U)
 
 QUARTERS = tuple(slice(c, c + S // 4) for c in range(0, S, S // 4))
 HALVES = (slice(0, S // 2), slice(S // 2, S))
@@ -84,10 +85,15 @@ def tile_picked_ydpo_dpo_p_kernel(tc, x_words, x_scales, hT, gT, offs, win, los,
 
         x_scale = sbuf("x_scale", S, U8)
         x_code = sbuf("x_code", S, U32)
-        grouped = [sbuf("grouped%d" % i, 2 * P * PACK, BF16) for i in range(TILES - 1)]
-        grouped_last = [sbuf("grouped3h", P * PACK, BF16), sbuf("grouped3g", P * PACK, BF16, takes_over="grouped2")]
-        codes = [sbuf("codes%d" % i, 2 * P, U32) for i in range(TILES)]
-        scales = [sbuf("scales%d" % i, 2 * P, U8) for i in range(TILES)]
+        grouped0 = sbuf("grouped0", 2 * P * PACK, BF16)
+        codes0 = sbuf("codes0", 2 * P, U32)
+        scales0 = sbuf("scales0", 2 * P, U8)
+        grouped = {(0, side): grouped0[:, P * PACK * side : P * PACK * (side + 1)] for side in (H, G)}
+        codes = {(0, side): codes0[:, P * side : P * (side + 1)] for side in (H, G)}
+        scales = {(0, side): scales0[:, P * side : P * (side + 1)] for side in (H, G)}
+        for i in range(1, TILES):
+            for side in (H, G):
+                grouped[i, side] = sbuf("grouped%d%s" % (i, "hg"[side]), P * PACK, BF16)[:]
         banks = [
             [
                 psum.tile([P, S], F32, name="acc%d_%d" % (i, n), tag="bank%d" % (FIRST_BANK[i] + n))
@@ -96,13 +102,8 @@ def tile_picked_ydpo_dpo_p_kernel(tc, x_words, x_scales, hT, gT, offs, win, los,
             for i in range(TILES)
         ]
 
-        def side_of(i, side):
-            if i == TILES - 1:
-                return grouped_last[side][:]
-            return grouped[i][:, P * PACK * side : P * PACK * (side + 1)]
-
         def by_lines(i, side):
-            dst = side_of(i, side).rearrange("p (c l j) -> p c j l", l=LINE, j=PACK)
+            dst = grouped[i, side].rearrange("p (c l j) -> p c j l", l=LINE, j=PACK)
             return dst, raw[side][i][:].rearrange("p j (c l) -> p c j l", l=LINE)
 
         def cast_on_scalar(i, side):
@@ -117,28 +118,28 @@ def tile_picked_ydpo_dpo_p_kernel(tc, x_words, x_scales, hT, gT, offs, win, los,
             nc.vector.tensor_scalar(dst, src, SIGNS[side], None, ALU.mult)
 
         def cast_on_gpsimd(i, side):
-            dst = side_of(i, side).rearrange("p (t j) -> p t j", j=PACK)
+            dst = grouped[i, side].rearrange("p (t j) -> p t j", j=PACK)
             nc.gpsimd.tensor_scalar(dst, raw[side][i][:].rearrange("p j t -> p t j"), SIGNS[side], 0.0, ALU.mult, ALU.add)
 
-        def quantize_both(i):
-            nc.vector.quantize_mx(out=codes[i][:].bitcast(FP8X4), scales=scales[i][:], in_=grouped[i][:])
+        def quantize(i, side, takes_over=None):
+            codes[i, side] = sbuf("codes%d%s" % (i, "hg"[side]), P, U32, takes_over)[:]
+            scales[i, side] = sbuf("scales%d%s" % (i, "hg"[side]), P, U8)[:]
+            nc.vector.quantize_mx(out=codes[i, side].bitcast(FP8X4), scales=scales[i, side], in_=grouped[i, side])
 
-        def quantize_side(i, side):
-            cols = slice(P * side, P * (side + 1))
-            nc.vector.quantize_mx(out=codes[i][:, cols].bitcast(FP8X4), scales=scales[i][:, cols], in_=side_of(i, side))
+        def product(i, side, bank, cols):
+            nc.tensor.matmul_mx(
+                out=bank[:, : cols.stop - cols.start],
+                lhsT=codes[i, side].bitcast(FP8X4),
+                lhsT_scale=scales[i, side],
+                rhs=x_code[:, cols].bitcast(FP8X4),
+                rhs_scale=x_scale[:, cols],
+                start=(side == H),
+                stop=(side == G),
+            )
 
-        def multiply(i):
+        def multiply(i, side):
             for bank, cols in zip(banks[i], PIECES[i]):
-                for side in (H, G):
-                    nc.tensor.matmul_mx(
-                        out=bank[:, : cols.stop - cols.start],
-                        lhsT=codes[i][:, P * side : P * (side + 1)].bitcast(FP8X4),
-                        lhsT_scale=scales[i][:, P * side : P * (side + 1)],
-                        rhs=x_code[:, cols].bitcast(FP8X4),
-                        rhs_scale=x_scale[:, cols],
-                        start=(side == H),
-                        stop=(side == G),
-                    )
+                product(i, side, bank, cols)
 
         def evacuate(i, takes_over=None):
             dd = sbuf("dd%d" % i, S, F32, takes_over)
@@ -146,20 +147,14 @@ def tile_picked_ydpo_dpo_p_kernel(tc, x_words, x_scales, hT, gT, offs, win, los,
                 nc.scalar.copy(dd[:, cols], bank[:, : cols.stop - cols.start])
             return dd
 
-        def gather(dst, dd, list_tile, pairs):
-            nc.vector.tensor_copy(dst, dd[:].indirect(entries(list_tile, pairs)))
+        def fetch_rejected(i, dd, parts):
+            rejected = sbuf("rejected%d" % i, U, F32)
+            for pairs in parts:
+                nc.scalar.activation(rejected[:, pairs], dd[:].indirect(entries(los_sb, pairs)), ACT.Copy)
+            return rejected
 
         def gather_subtract(dst, dd, rejected, pairs):
             nc.vector.tensor_tensor(dst, dd[:].indirect(entries(win_sb, pairs)), rejected[:, pairs], ALU.subtract)
-
-        def pick(i, dd, takes_over=None):
-            rejected = sbuf("rejected%d" % i, U, F32, takes_over)
-            margin = sbuf("margin%d" % i, U, F32)
-            for pairs in (FIRST, SECOND):
-                gather(rejected[:, pairs], dd, los_sb, pairs)
-            for pairs in (FIRST, SECOND):
-                gather_subtract(margin[:, pairs], dd, rejected, pairs)
-            return margin
 
         def weigh(weight, margin):
             nc.scalar.activation(weight, margin, ACT.Sigmoid, scale=-0.5)
@@ -170,51 +165,59 @@ def tile_picked_ydpo_dpo_p_kernel(tc, x_words, x_scales, hT, gT, offs, win, los,
         nc.vector.tensor_copy(x_scale[:], table_scales[:].indirect(offs_sb[:]))
         cast_on_scalar(0, H)
         cast_on_scalar(0, G)
-        quantize_both(0)
+        nc.vector.quantize_mx(out=codes0[:].bitcast(FP8X4), scales=scales0[:], in_=grouped0[:])
         for cols in PIECES[0]:
             nc.vector.tensor_copy(x_code[:, cols], table_words[:].bitcast(U32).indirect(entries(offs_sb, cols)))
-        multiply(0)
+        for bank, cols in zip(banks[0], PIECES[0]):
+            for side in (H, G):
+                product(0, side, bank, cols)
         cast_on_gpsimd(1, H)
         dd0 = evacuate(0)
+        rejected0 = fetch_rejected(0, dd0, (ALL,))
 
-        cast_on_vector(1, G)
-        quantize_both(1)
-        multiply(1)
-        cast_on_gpsimd(2, H)
-        cast_on_scalar(2, G)
-        margin0 = pick(0, dd0, takes_over="g_raw1")
+        def finish_sides(i):
+            cast_on_vector(i, G)
+            quantize(i, H, takes_over="g_raw%d" % i)
+            multiply(i, H)
+            quantize(i, G)
+            multiply(i, G)
 
-        dd1 = evacuate(1, takes_over="h_raw2")
-        quantize_both(2)
-        multiply(2)
-        cast_on_scalar(3, H)
-        cast_on_gpsimd(3, G)
+        finish_sides(1)
+        dd1 = evacuate(1)
+        rejected1 = fetch_rejected(1, dd1, (ALL,))
+        cast_on_vector(2, H)
+        finish_sides(2)
+        margin0_first = sbuf("margin0_first", U // 2, F32, takes_over="grouped2g")
+        gather_subtract(margin0_first[:], dd0, rejected0, FIRST)
+        dd2 = evacuate(2)
+        rejected2 = fetch_rejected(2, dd2, (ALL,))
+        cast_on_vector(3, H)
+        margin0_second = sbuf("margin0_second", U // 2, F32, takes_over="h_raw3")
+        gather_subtract(margin0_second[:], dd0, rejected0, SECOND)
+        finish_sides(3)
+        dd3 = sbuf("dd3", S, F32)
+        nc.scalar.copy(dd3[:, HALVES[0]], banks[3][0][:, : S // 2])
+        nc.vector.tensor_copy(dd3[:, HALVES[1]], banks[3][1][:, : S // 2])
+        rejected3 = fetch_rejected(3, dd3, (FIRST, SECOND))
+        margin1 = sbuf("margin1", U, F32, takes_over="grouped3g")
+        gather_subtract(margin1[:], dd1, rejected1, ALL)
+        margin2 = sbuf("margin2", U, F32, takes_over="scales3g")
+        gather_subtract(margin2[:], dd2, rejected2, ALL)
+        margin3 = sbuf("margin3", U, F32)
+        for pairs in (FIRST, SECOND):
+            gather_subtract(margin3[:, pairs], dd3, rejected3, pairs)
 
-        rejected1 = sbuf("rejected1", U, F32, takes_over="g_raw2")
-        preferred1 = sbuf("preferred1", U // 2, F32)
-        margin1_second = sbuf("margin1_second", U // 2, F32, takes_over="g_raw3")
-        gather(rejected1[:], dd1, los_sb, slice(0, U))
-        gather(preferred1[:], dd1, win_sb, FIRST)
-        quantize_side(3, H)
-        quantize_side(3, G)
-        multiply(3)
-        gather_subtract(margin1_second[:], dd1, rejected1, SECOND)
-        margin1_first = sbuf("margin1_first", U // 2, F32, takes_over="grouped2")
-        nc.gpsimd.tensor_tensor(margin1_first[:], preferred1[:], rejected1[:, FIRST], ALU.subtract)
-
-        margin2 = pick(2, evacuate(2, takes_over="h_raw3"), takes_over="grouped3h")
-        margin3 = pick(3, evacuate(3))
-
-        early = sbuf("early", 2 * U, F32, takes_over="codes3")
-        late = sbuf("late", U, F32, takes_over="scales3")
+        weight0 = sbuf("weight0", U, F32, takes_over="codes2g")
+        weigh(weight0[:, FIRST], margin0_first[:])
+        weigh(weight0[:, SECOND], margin0_second[:])
+        store(0, weight0[:], ALL)
+        weight1 = sbuf("weight1", U, F32, takes_over="codes3g")
+        weigh(weight1[:], margin1[:])
+        store(1, weight1[:], ALL)
+        weight2 = sbuf("weight2", U, F32)
+        weigh(weight2[:], margin2[:])
+        store(2, weight2[:], ALL)
         last = sbuf("last", U, F32)
-        weigh(early[:, :U], margin0[:])
-        store(0, early[:, :U], slice(0, U))
-        weigh(early[:, U : U + U // 2], margin1_first[:])
-        weigh(early[:, U + U // 2 :], margin1_second[:])
-        store(1, early[:, U:], slice(0, U))
-        weigh(late[:], margin2[:])
-        store(2, late[:], slice(0, U))
         for pairs in (FIRST, SECOND):
             weigh(last[:, pairs], margin3[:, pairs])
             store(3, last[:, pairs], pairs)

@@ -173,36 +173,42 @@ def tile_picked_ydpo_dpo_p_kernel(tc, x_words, x_scales, hT, gT, offs, win, los,
                 product(0, side, bank, cols)
         cast_on_gpsimd(1, H)
         dd0 = evacuate(0)
-        rejected0 = fetch_rejected(0, dd0, (ALL,))
 
-        def finish_sides(i):
+        def both_sides(i):
             cast_on_vector(i, G)
             quantize(i, H, takes_over="g_raw%d" % i)
             multiply(i, H)
             quantize(i, G)
             multiply(i, G)
 
-        finish_sides(1)
+        rejected0 = fetch_rejected(0, dd0, (FIRST, SECOND))
+        both_sides(1)
         dd1 = evacuate(1)
         rejected1 = fetch_rejected(1, dd1, (ALL,))
         cast_on_vector(2, H)
-        finish_sides(2)
-        margin0_first = sbuf("margin0_first", U // 2, F32, takes_over="grouped2g")
-        gather_subtract(margin0_first[:], dd0, rejected0, FIRST)
+        both_sides(2)
         dd2 = evacuate(2)
-        rejected2 = fetch_rejected(2, dd2, (ALL,))
+
         cast_on_vector(3, H)
-        margin0_second = sbuf("margin0_second", U // 2, F32, takes_over="h_raw3")
+        margin0_first = sbuf("margin0_first", U // 2, F32, takes_over="h_raw3")
+        gather_subtract(margin0_first[:], dd0, rejected0, FIRST)
+        quantize(3, H)
+        multiply(3, H)
+        cast_on_vector(3, G)
+        margin0_second = sbuf("margin0_second", U // 2, F32, takes_over="g_raw3")
         gather_subtract(margin0_second[:], dd0, rejected0, SECOND)
-        finish_sides(3)
-        dd3 = sbuf("dd3", S, F32)
-        nc.scalar.copy(dd3[:, HALVES[0]], banks[3][0][:, : S // 2])
-        nc.vector.tensor_copy(dd3[:, HALVES[1]], banks[3][1][:, : S // 2])
+        quantize(3, G)
+        multiply(3, G)
+        held = sbuf("held", 2 * U, F32, takes_over="grouped3g")
+        margin1, rejected2 = held[:, :U], held[:, U:]
+        gather_subtract(margin1, dd1, rejected1, ALL)
+        for pairs in (FIRST, SECOND):
+            nc.vector.tensor_copy(rejected2[:, pairs], dd2[:].indirect(entries(los_sb, pairs)))
+        margin2 = sbuf("margin2", U, F32)
+        for pairs in (FIRST, SECOND):
+            gather_subtract(margin2[:, pairs], dd2, rejected2, pairs)
+        dd3 = evacuate(3)
         rejected3 = fetch_rejected(3, dd3, (FIRST, SECOND))
-        margin1 = sbuf("margin1", U, F32, takes_over="grouped3g")
-        gather_subtract(margin1[:], dd1, rejected1, ALL)
-        margin2 = sbuf("margin2", U, F32, takes_over="scales3g")
-        gather_subtract(margin2[:], dd2, rejected2, ALL)
         margin3 = sbuf("margin3", U, F32)
         for pairs in (FIRST, SECOND):
             gather_subtract(margin3[:, pairs], dd3, rejected3, pairs)
@@ -212,9 +218,9 @@ def tile_picked_ydpo_dpo_p_kernel(tc, x_words, x_scales, hT, gT, offs, win, los,
         weigh(weight0[:, SECOND], margin0_second[:])
         store(0, weight0[:], ALL)
         weight1 = sbuf("weight1", U, F32, takes_over="codes3g")
-        weigh(weight1[:], margin1[:])
+        weigh(weight1[:], margin1)
         store(1, weight1[:], ALL)
-        weight2 = sbuf("weight2", U, F32)
+        weight2 = sbuf("weight2", U, F32, takes_over="scales3g")
         weigh(weight2[:], margin2[:])
         store(2, weight2[:], ALL)
         last = sbuf("last", U, F32)

@@ -117,10 +117,6 @@ def tile_picked_ydpo_dpo_p_kernel(tc, x_words, x_scales, hT, gT, offs, win, los,
             dst, src = by_lines(i, side)
             nc.vector.tensor_scalar(dst, src, SIGNS[side], None, ALU.mult)
 
-        def cast_on_gpsimd(i, side):
-            dst = grouped[i, side].rearrange("p (t j) -> p t j", j=PACK)
-            nc.gpsimd.tensor_scalar(dst, raw[side][i][:].rearrange("p j t -> p t j"), SIGNS[side], 0.0, ALU.mult, ALU.add)
-
         def quantize(i, side, takes_over=None):
             codes[i, side] = sbuf("codes%d%s" % (i, "hg"[side]), P, U32, takes_over)[:]
             scales[i, side] = sbuf("scales%d%s" % (i, "hg"[side]), P, U8)[:]
@@ -171,8 +167,8 @@ def tile_picked_ydpo_dpo_p_kernel(tc, x_words, x_scales, hT, gT, offs, win, los,
         for bank, cols in zip(banks[0], PIECES[0]):
             for side in (H, G):
                 product(0, side, bank, cols)
-        cast_on_gpsimd(1, H)
-        dd0 = evacuate(0)
+        cast_on_scalar(1, H)
+        dd0 = evacuate(0, takes_over="h_raw1")
 
         def both_sides(i):
             cast_on_vector(i, G)
@@ -192,15 +188,10 @@ def tile_picked_ydpo_dpo_p_kernel(tc, x_words, x_scales, hT, gT, offs, win, los,
         cast_on_vector(3, H)
         margin0_first = sbuf("margin0_first", U // 2, F32, takes_over="h_raw3")
         gather_subtract(margin0_first[:], dd0, rejected0, FIRST)
-        quantize(3, H)
-        multiply(3, H)
-        cast_on_vector(3, G)
-        margin0_second = sbuf("margin0_second", U // 2, F32, takes_over="g_raw3")
-        gather_subtract(margin0_second[:], dd0, rejected0, SECOND)
-        quantize(3, G)
-        multiply(3, G)
-        held = sbuf("held", 2 * U, F32, takes_over="grouped3g")
-        margin1, rejected2 = held[:, :U], held[:, U:]
+        both_sides(3)
+        held = sbuf("held", 2 * U + U // 2, F32, takes_over="grouped3g")
+        margin1, rejected2, margin0_second = held[:, :U], held[:, U : 2 * U], held[:, 2 * U :]
+        gather_subtract(margin0_second, dd0, rejected0, SECOND)
         gather_subtract(margin1, dd1, rejected1, ALL)
         for pairs in (FIRST, SECOND):
             nc.vector.tensor_copy(rejected2[:, pairs], dd2[:].indirect(entries(los_sb, pairs)))
@@ -213,14 +204,14 @@ def tile_picked_ydpo_dpo_p_kernel(tc, x_words, x_scales, hT, gT, offs, win, los,
         for pairs in (FIRST, SECOND):
             gather_subtract(margin3[:, pairs], dd3, rejected3, pairs)
 
-        weight0 = sbuf("weight0", U, F32, takes_over="codes2g")
+        weight0 = sbuf("weight0", U, F32, takes_over="codes3g")
         weigh(weight0[:, FIRST], margin0_first[:])
-        weigh(weight0[:, SECOND], margin0_second[:])
+        weigh(weight0[:, SECOND], margin0_second)
         store(0, weight0[:], ALL)
-        weight1 = sbuf("weight1", U, F32, takes_over="codes3g")
+        weight1 = sbuf("weight1", U, F32, takes_over="scales3g")
         weigh(weight1[:], margin1)
         store(1, weight1[:], ALL)
-        weight2 = sbuf("weight2", U, F32, takes_over="scales3g")
+        weight2 = sbuf("weight2", U, F32)
         weigh(weight2[:], margin2[:])
         store(2, weight2[:], ALL)
         last = sbuf("last", U, F32)

@@ -28,7 +28,7 @@ ALL = slice(0, U)
 
 QUARTERS = tuple(slice(c, c + S // 4) for c in range(0, S, S // 4))
 HALVES = (slice(0, S // 2), slice(S // 2, S))
-PIECES = (QUARTERS, HALVES, HALVES, HALVES)
+PIECES = (QUARTERS, HALVES, HALVES, QUARTERS)
 FIRST_BANK = (0, 4, 6, 0)
 
 
@@ -181,36 +181,49 @@ def tile_picked_ydpo_dpo_p_kernel(tc, x_words, x_scales, hT, gT, offs, win, los,
         both_sides(1)
         dd1 = evacuate(1)
         rejected1 = fetch_rejected(1, dd1, (ALL,))
+
         cast_on_vector(2, H)
-        both_sides(2)
+        cast_on_vector(2, G)
+        quantize(2, H, takes_over="g_raw2")
+        multiply(2, H)
+        margin0_first = sbuf("margin0_first", U // 2, F32, takes_over="grouped2h")
+        gather_subtract(margin0_first[:], dd0, rejected0, FIRST)
+        quantize(2, G)
+        multiply(2, G)
         dd2 = evacuate(2)
+        rejected2_first = fetch_rejected(2, dd2, (FIRST,))
 
         cast_on_vector(3, H)
-        margin0_first = sbuf("margin0_first", U // 2, F32, takes_over="h_raw3")
-        gather_subtract(margin0_first[:], dd0, rejected0, FIRST)
+        margin0_second = sbuf("margin0_second", U // 2, F32, takes_over="h_raw3")
+        gather_subtract(margin0_second[:], dd0, rejected0, SECOND)
         both_sides(3)
-        held = sbuf("held", 2 * U + U // 2, F32, takes_over="grouped3g")
-        margin1, rejected2, margin0_second = held[:, :U], held[:, U : 2 * U], held[:, 2 * U :]
-        gather_subtract(margin0_second, dd0, rejected0, SECOND)
-        gather_subtract(margin1, dd1, rejected1, ALL)
-        for pairs in (FIRST, SECOND):
-            nc.vector.tensor_copy(rejected2[:, pairs], dd2[:].indirect(entries(los_sb, pairs)))
-        margin2 = sbuf("margin2", U, F32)
-        for pairs in (FIRST, SECOND):
-            gather_subtract(margin2[:, pairs], dd2, rejected2, pairs)
-        dd3 = evacuate(3)
+        margin1 = sbuf("margin1", U, F32, takes_over="grouped3g")
+        gather_subtract(margin1[:], dd1, rejected1, ALL)
+        dd3 = sbuf("dd3", S, F32)
+        for n, (bank, cols) in enumerate(zip(banks[3], PIECES[3])):
+            if n % 2 == 0:
+                nc.scalar.copy(dd3[:, cols], bank[:, : S // 4])
+            else:
+                nc.vector.tensor_copy(dd3[:, cols], bank[:, : S // 4])
+        held = sbuf("held", 2 * U, F32, takes_over="codes3g")
+        rejected2_second, weight1 = held[:, :U], held[:, U:]
+        nc.scalar.activation(rejected2_second[:, SECOND], dd2[:].indirect(entries(los_sb, SECOND)), ACT.Copy)
         rejected3 = fetch_rejected(3, dd3, (FIRST, SECOND))
+        margin2 = sbuf("margin2", U, F32, takes_over="scales3g")
+        gather_subtract(margin2[:, FIRST], dd2, rejected2_first, FIRST)
+        preferred3 = sbuf("preferred3", U // 2, F32)
+        nc.vector.tensor_copy(preferred3[:], dd3[:].indirect(entries(win_sb, SECOND)))
+        gather_subtract(margin2[:, SECOND], dd2, rejected2_second, SECOND)
         margin3 = sbuf("margin3", U, F32)
-        for pairs in (FIRST, SECOND):
-            gather_subtract(margin3[:, pairs], dd3, rejected3, pairs)
+        gather_subtract(margin3[:, FIRST], dd3, rejected3, FIRST)
+        nc.vector.tensor_tensor(margin3[:, SECOND], preferred3[:], rejected3[:, SECOND], ALU.subtract)
 
-        weight0 = sbuf("weight0", U, F32, takes_over="codes3g")
+        weight0 = sbuf("weight0", U, F32, takes_over="codes2g")
         weigh(weight0[:, FIRST], margin0_first[:])
-        weigh(weight0[:, SECOND], margin0_second)
+        weigh(weight0[:, SECOND], margin0_second[:])
         store(0, weight0[:], ALL)
-        weight1 = sbuf("weight1", U, F32, takes_over="scales3g")
-        weigh(weight1[:], margin1)
-        store(1, weight1[:], ALL)
+        weigh(weight1, margin1[:])
+        store(1, weight1, ALL)
         weight2 = sbuf("weight2", U, F32)
         weigh(weight2[:], margin2[:])
         store(2, weight2[:], ALL)

@@ -23,13 +23,10 @@ H, G = 0, 1
 SIGNS = (1.0, -1.0)
 SCALE_ROWS = K // 32
 QUADRANT = 32
-FIRST, SECOND = slice(0, U // 2), slice(U // 2, U)
-ALL = slice(0, U)
-
+FIRST, SECOND, ALL = slice(0, U // 2), slice(U // 2, U), slice(0, U)
 QUARTERS = tuple(slice(c, c + S // 4) for c in range(0, S, S // 4))
 HALVES = (slice(0, S // 2), slice(S // 2, S))
-PIECES = (QUARTERS, HALVES, HALVES, QUARTERS)
-FIRST_BANK = (0, 4, 6, 0)
+LEAD = P // 4
 
 
 def entries(list_tile, part):
@@ -50,38 +47,28 @@ def tile_picked_ydpo_dpo_p_kernel(tc, x_words, x_scales, hT, gT, offs, win, los,
         los_sb = keep.tile([P, U // 16], U16, name="los_sb")
         table_words = sbuf("table_words", T, I32)
         table_scales = sbuf("table_scales", T, U8)
-        raw = [
-            [keep.tile([P, PACK, P], F32, name="%s_raw%d" % (n, i), tag="%s_raw%d" % (n, i), align_bytes=64) for i in range(TILES)]
-            for n in "hg"
-        ]
+        raw = {(i, side): sbuf("raw%d%s" % (i, "hg"[side]), PACK * P, F32) for i in range(TILES) for side in (H, G)}
         rows = [a.rearrange("(p j) t -> p j t", j=PACK) for a in (hT, gT)]
 
-        def load(i, side):
-            nc.sync.dma_start(out=raw[side][i][:], in_=rows[side][:, :, P * i : P * (i + 1)])
+        def load(i, side, queue=nc.sync):
+            queue.dma_start(out=raw[i, side][:].rearrange("p (j t) -> p j t", j=PACK), in_=rows[side][:, :, P * i : P * (i + 1)])
 
-        nc.vector.memset(table_scales[:].bitcast(I32), 0)
+        def load_scales():
+            per_quadrant = SCALE_ROWS * QUADRANT // P
+            for r in range(per_quadrant):
+                nc.sync.dma_start(
+                    out=table_scales[r:P:QUADRANT, :].bitcast(I32),
+                    in_=x_scales[0, r:SCALE_ROWS:per_quadrant, :].bitcast(I32),
+                )
 
-        nc.sync.dma_start(offs_sb[:], offs)
-        load(0, H)
-        per_quadrant = SCALE_ROWS * QUADRANT // P
-        for r in range(per_quadrant):
-            nc.sync.dma_start(
-                out=table_scales[r:P:QUADRANT, :].bitcast(I32),
-                in_=x_scales[0, r:SCALE_ROWS:per_quadrant, :].bitcast(I32),
-            )
-        load(0, G)
-        nc.sync.dma_start(out=table_words[:], in_=x_words[0].rearrange("p n r -> p (n r)").bitcast(I32))
-        for i in range(1, TILES):
-            load(i, H)
-            load(i, G)
-            if i == 1:
-                nc.sync.dma_start(los_sb[:], los)
-                nc.sync.dma_start(win_sb[:], win)
+        def load_words(queue=nc.sync):
+            queue.dma_start(out=table_words[:], in_=x_words[0].rearrange("p n r -> p (n r)").bitcast(I32))
 
-        warm_in = keep.tile([P, 1], F32, name="warm_in")
-        warm_out = keep.tile([P, 1], F32, name="warm_out")
-        nc.gpsimd.memset(warm_in[:], 0.0)
-        nc.scalar.activation(warm_out[:], warm_in[:], ACT.Sigmoid)
+        def warm_up():
+            warm_in = keep.tile([P, 1], F32, name="warm_in")
+            warm_out = keep.tile([P, 1], F32, name="warm_out")
+            nc.gpsimd.memset(warm_in[:], 0.0)
+            nc.scalar.activation(warm_out[:], warm_in[:], ACT.Sigmoid)
 
         x_scale = sbuf("x_scale", S, U8)
         x_code = sbuf("x_code", S, U32)
@@ -94,37 +81,54 @@ def tile_picked_ydpo_dpo_p_kernel(tc, x_words, x_scales, hT, gT, offs, win, los,
         for i in range(1, TILES):
             for side in (H, G):
                 grouped[i, side] = sbuf("grouped%d%s" % (i, "hg"[side]), P * PACK, BF16)[:]
-        banks = [
-            [
-                psum.tile([P, S], F32, name="acc%d_%d" % (i, n), tag="bank%d" % (FIRST_BANK[i] + n))
-                for n in range(len(PIECES[i]))
-            ]
-            for i in range(TILES)
-        ]
 
-        def by_lines(i, side):
+        def bank(n, name):
+            return psum.tile([P, S], F32, name=name, tag="bank%d" % n)
+
+        def by_lines(i, side, cols):
+            part = slice(cols.start // LINE, cols.stop // LINE)
             dst = grouped[i, side].rearrange("p (c l j) -> p c j l", l=LINE, j=PACK)
-            return dst, raw[side][i][:].rearrange("p j (c l) -> p c j l", l=LINE)
+            src = raw[i, side][:].rearrange("p (j c l) -> p c j l", l=LINE, j=PACK)
+            return dst[:, part], src[:, part]
 
-        def cast_on_scalar(i, side):
-            dst, src = by_lines(i, side)
+        def cast_s(i, side, cols=slice(0, P)):
+            dst, src = by_lines(i, side, cols)
             if side == H:
                 nc.scalar.copy(dst, src)
             else:
                 nc.scalar.activation(dst, src, ACT.Copy, scale=SIGNS[side])
 
-        def cast_on_vector(i, side):
-            dst, src = by_lines(i, side)
+        def cast_v(i, side, cols=slice(0, P)):
+            dst, src = by_lines(i, side, cols)
             nc.vector.tensor_scalar(dst, src, SIGNS[side], None, ALU.mult)
 
-        def quantize(i, side, takes_over=None):
+        def cast_g(i, side, cols=slice(0, P)):
+            dst, src = by_lines(i, side, cols)
+            nc.gpsimd.tensor_scalar(dst, src, SIGNS[side], 0.0, ALU.mult, ALU.add)
+
+        sign = {}
+
+        def make_sign(i, side):
+            sign[i, side] = sbuf("sign%d%s" % (i, "hg"[side]), 1, F32)
+            nc.gpsimd.memset(sign[i, side][:], SIGNS[side])
+
+        def cast_v2(i, side, start=0):
+            dst, src = by_lines(i, side, slice(start, start + LEAD))
+            nc.vector.tensor_scalar(dst, src, sign[i, side][:], None, ALU.mult)
+            cast_v(i, side, slice(start + LEAD, P))
+
+        def row(i, side, j, n=1):
+            return raw[i, side][:, P * j : P * (j + n)]
+
+        def quantize(i, side, plane_in=None, takes_over=None):
             codes[i, side] = sbuf("codes%d%s" % (i, "hg"[side]), P, U32, takes_over)[:]
-            scales[i, side] = sbuf("scales%d%s" % (i, "hg"[side]), P, U8)[:]
+            behind = None if plane_in is None else "sign%d%s" % (plane_in[0], "hg"[plane_in[1]])
+            scales[i, side] = sbuf("scales%d%s" % (i, "hg"[side]), P, U8, behind)[:]
             nc.vector.quantize_mx(out=codes[i, side].bitcast(FP8X4), scales=scales[i, side], in_=grouped[i, side])
 
-        def product(i, side, bank, cols):
+        def product(i, side, acc, cols):
             nc.tensor.matmul_mx(
-                out=bank[:, : cols.stop - cols.start],
+                out=acc[:, : cols.stop - cols.start],
                 lhsT=codes[i, side].bitcast(FP8X4),
                 lhsT_scale=scales[i, side],
                 rhs=x_code[:, cols].bitcast(FP8X4),
@@ -133,101 +137,128 @@ def tile_picked_ydpo_dpo_p_kernel(tc, x_words, x_scales, hT, gT, offs, win, los,
                 stop=(side == G),
             )
 
-        def multiply(i, side):
-            for bank, cols in zip(banks[i], PIECES[i]):
-                product(i, side, bank, cols)
+        def multiply(i, side, accs, pieces):
+            for acc, cols in zip(accs, pieces):
+                product(i, side, acc, cols)
 
-        def evacuate(i, takes_over=None):
-            dd = sbuf("dd%d" % i, S, F32, takes_over)
-            for bank, cols in zip(banks[i], PIECES[i]):
-                nc.scalar.copy(dd[:, cols], bank[:, : cols.stop - cols.start])
-            return dd
+        def evac_s(dd, acc, cols):
+            nc.scalar.copy(dd[:, cols], acc[:, : cols.stop - cols.start])
 
-        def fetch_rejected(i, dd, parts):
-            rejected = sbuf("rejected%d" % i, U, F32)
-            for pairs in parts:
-                nc.scalar.activation(rejected[:, pairs], dd[:].indirect(entries(los_sb, pairs)), ACT.Copy)
-            return rejected
+        def evac_v(dd, acc, cols):
+            nc.vector.tensor_copy(dd[:, cols], acc[:, : cols.stop - cols.start])
 
-        def gather_subtract(dst, dd, rejected, pairs):
-            nc.vector.tensor_tensor(dst, dd[:].indirect(entries(win_sb, pairs)), rejected[:, pairs], ALU.subtract)
+        def fetch_s(dst, dd, lst, pairs):
+            nc.scalar.activation(dst, dd[:].indirect(entries(lst, pairs)), ACT.Copy)
 
-        def weigh(weight, margin):
-            nc.scalar.activation(weight, margin, ACT.Sigmoid, scale=-0.5)
+        def fetch_v(dst, dd, lst, pairs):
+            nc.vector.tensor_copy(dst, dd[:].indirect(entries(lst, pairs)))
 
-        def store(i, weight, pairs):
-            nc.sync.dma_start(out=out[P * i : P * (i + 1), pairs], in_=weight)
+        def fetch_sub(dst, dd, lst, pairs, other):
+            nc.vector.tensor_tensor(dst, dd[:].indirect(entries(lst, pairs)), other, ALU.subtract)
+
+        def weigh(weight, margin, scale=-0.5):
+            nc.scalar.activation(weight, margin, ACT.Sigmoid, scale=scale)
+
+        def store(i, weight, pairs, queue=nc.sync):
+            queue.dma_start(out=out[P * i : P * (i + 1), pairs], in_=weight)
+
+        for key in ((1, G), (2, H), (2, G), (3, H), (3, G)):
+            make_sign(*key)
+
+        nc.vector.memset(table_scales[:].bitcast(I32), 0)
+        nc.sync.dma_start(offs_sb[:], offs)
+        load(0, H)
+        load_scales()
+        load(0, G)
+        load_words()
+        load(1, H)
+        load(1, G)
+        nc.sync.dma_start(los_sb[:], los)
+        nc.sync.dma_start(win_sb[:], win)
+        for i in (2, 3):
+            load(i, H)
+            load(i, G)
+        warm_up()
 
         nc.vector.tensor_copy(x_scale[:], table_scales[:].indirect(offs_sb[:]))
-        cast_on_scalar(0, H)
-        cast_on_scalar(0, G)
+        cast_s(0, H)
+        cast_s(0, G)
         nc.vector.quantize_mx(out=codes0[:].bitcast(FP8X4), scales=scales0[:], in_=grouped0[:])
-        for cols in PIECES[0]:
+        for cols in QUARTERS:
             nc.vector.tensor_copy(x_code[:, cols], table_words[:].bitcast(U32).indirect(entries(offs_sb, cols)))
-        for bank, cols in zip(banks[0], PIECES[0]):
+        acc0 = [bank(n, "acc0_%d" % n) for n in range(4)]
+        for acc, cols in zip(acc0, QUARTERS):
             for side in (H, G):
-                product(0, side, bank, cols)
-        cast_on_scalar(1, H)
-        dd0 = evacuate(0, takes_over="h_raw1")
+                product(0, side, acc, cols)
+        cast_s(1, H)
+        dd0 = sbuf("dd0", S, F32, takes_over="raw1h")
+        for acc, cols in zip(acc0, QUARTERS):
+            evac_s(dd0, acc, cols)
 
-        def both_sides(i):
-            cast_on_vector(i, G)
-            quantize(i, H, takes_over="g_raw%d" % i)
-            multiply(i, H)
-            quantize(i, G)
-            multiply(i, G)
-
-        rejected0 = fetch_rejected(0, dd0, (FIRST, SECOND))
-        both_sides(1)
-        dd1 = evacuate(1)
-        rejected1 = fetch_rejected(1, dd1, (ALL,))
-
-        cast_on_vector(2, H)
-        cast_on_vector(2, G)
-        quantize(2, H, takes_over="g_raw2")
-        multiply(2, H)
-        margin0_first = sbuf("margin0_first", U // 2, F32, takes_over="grouped2h")
-        gather_subtract(margin0_first[:], dd0, rejected0, FIRST)
-        quantize(2, G)
-        multiply(2, G)
-        dd2 = evacuate(2)
-        rejected2_first = fetch_rejected(2, dd2, (FIRST,))
-
-        cast_on_vector(3, H)
-        margin0_second = sbuf("margin0_second", U // 2, F32, takes_over="h_raw3")
-        gather_subtract(margin0_second[:], dd0, rejected0, SECOND)
-        both_sides(3)
-        margin1 = sbuf("margin1", U, F32, takes_over="grouped3g")
-        gather_subtract(margin1[:], dd1, rejected1, ALL)
+        acc1 = [bank(4 + n, "acc1_%d" % n) for n in range(2)]
+        acc2 = [bank(6 + n, "acc2_%d" % n) for n in range(2)]
+        acc3 = [bank(n, "acc3_%d" % n) for n in range(2)]
+        HALF = U // 2
+        rej0a = sbuf("rej0a", HALF, F32)
+        fetch_s(rej0a[:], dd0, los_sb, FIRST)
+        cast_v2(1, G)
+        quantize(1, H, plane_in=(1, G))
+        multiply(1, H, acc1, HALVES)
+        cast_v2(2, H)
+        quantize(1, G, plane_in=(2, H))
+        multiply(1, G, acc1, HALVES)
+        dd1 = sbuf("dd1", S, F32)
+        for acc, cols in zip(acc1, HALVES):
+            evac_s(dd1, acc, cols)
+        rej0b = sbuf("rej0b", HALF, F32, takes_over="codes1g")
+        fetch_s(rej0b[:], dd0, los_sb, SECOND)
+        rej1a = sbuf("rej1a", HALF, F32)
+        fetch_s(rej1a[:], dd1, los_sb, FIRST)
+        cast_v2(2, G)
+        quantize(2, H, plane_in=(2, G))
+        multiply(2, H, acc2, HALVES)
+        cast_v2(3, H)
+        quantize(2, G, plane_in=(3, H))
+        multiply(2, G, acc2, HALVES)
+        dd2 = sbuf("dd2", S, F32)
+        for acc, cols in zip(acc2, HALVES):
+            evac_s(dd2, acc, cols)
+        rej1b = sbuf("rej1b", HALF, F32, takes_over="codes2g")
+        fetch_s(rej1b[:], dd1, los_sb, SECOND)
+        rej2 = sbuf("rej2", U, F32)
+        fetch_s(rej2[:], dd2, los_sb, ALL)
+        cast_v2(3, G)
+        quantize(3, H, plane_in=(3, G))
+        multiply(3, H, acc3, HALVES)
+        m0a, m0b = row(3, G, 1), row(3, G, 2)
+        fetch_sub(m0a, dd0, win_sb, FIRST, rej0a[:])
+        quantize(3, G)
+        multiply(3, G, acc3, HALVES)
+        fetch_sub(m0b, dd0, win_sb, SECOND, rej0b[:])
+        m1 = sbuf("m1", U, F32, takes_over="grouped3h")
+        fetch_sub(m1[:, FIRST], dd1, win_sb, FIRST, rej1a[:])
         dd3 = sbuf("dd3", S, F32)
-        for n, (bank, cols) in enumerate(zip(banks[3], PIECES[3])):
-            if n % 2 == 0:
-                nc.scalar.copy(dd3[:, cols], bank[:, : S // 4])
-            else:
-                nc.vector.tensor_copy(dd3[:, cols], bank[:, : S // 4])
-        held = sbuf("held", 2 * U, F32, takes_over="codes3g")
-        rejected2_second, weight1 = held[:, :U], held[:, U:]
-        nc.scalar.activation(rejected2_second[:, SECOND], dd2[:].indirect(entries(los_sb, SECOND)), ACT.Copy)
-        rejected3 = fetch_rejected(3, dd3, (FIRST, SECOND))
-        margin2 = sbuf("margin2", U, F32, takes_over="scales3g")
-        gather_subtract(margin2[:, FIRST], dd2, rejected2_first, FIRST)
-        preferred3 = sbuf("preferred3", U // 2, F32)
-        nc.vector.tensor_copy(preferred3[:], dd3[:].indirect(entries(win_sb, SECOND)))
-        gather_subtract(margin2[:, SECOND], dd2, rejected2_second, SECOND)
-        margin3 = sbuf("margin3", U, F32)
-        gather_subtract(margin3[:, FIRST], dd3, rejected3, FIRST)
-        nc.vector.tensor_tensor(margin3[:, SECOND], preferred3[:], rejected3[:, SECOND], ALU.subtract)
-
-        weight0 = sbuf("weight0", U, F32, takes_over="codes2g")
-        weigh(weight0[:, FIRST], margin0_first[:])
-        weigh(weight0[:, SECOND], margin0_second[:])
-        store(0, weight0[:], ALL)
-        weigh(weight1, margin1[:])
-        store(1, weight1, ALL)
-        weight2 = sbuf("weight2", U, F32)
-        weigh(weight2[:], margin2[:])
-        store(2, weight2[:], ALL)
-        last = sbuf("last", U, F32)
+        evac_v(dd3, acc3[0], HALVES[0])
+        evac_v(dd3, acc3[1], HALVES[1])
+        m1b = sbuf("m1b", HALF, F32, takes_over="codes3g")
+        fetch_sub(m1b[:], dd1, win_sb, SECOND, rej1b[:])
+        w = [sbuf("w%d" % i, U, F32) for i in range(1, TILES)]
+        w0 = sbuf("w0", U, F32, takes_over="scales3g")
+        weigh(w0[:], row(3, G, 1, 2))
+        store(0, w0[:], ALL)
+        rej3 = sbuf("rej3", U, F32)
+        fetch_s(rej3[:, FIRST], dd3, los_sb, FIRST)
+        fetch_s(rej3[:, SECOND], dd3, los_sb, SECOND)
+        m2 = sbuf("m2", U, F32, takes_over="codes1g")
+        fetch_sub(m2[:], dd2, win_sb, ALL, rej2[:])
+        weigh(w[0][:, FIRST], m1[:, FIRST])
+        weigh(w[0][:, SECOND], m1b[:])
+        store(1, w[0][:], ALL)
+        m3 = sbuf("m3", U, F32)
+        fetch_sub(m3[:, FIRST], dd3, win_sb, FIRST, rej3[:, FIRST])
+        fetch_sub(m3[:, SECOND], dd3, win_sb, SECOND, rej3[:, SECOND])
+        weigh(w[1][:], m2[:])
+        store(2, w[1][:], ALL)
         for pairs in (FIRST, SECOND):
-            weigh(last[:, pairs], margin3[:, pairs])
-            store(3, last[:, pairs], pairs)
+            weigh(w[2][:, pairs], m3[:, pairs])
+            store(3, w[2][:, pairs], pairs)

@@ -26,7 +26,7 @@ QUADRANT = 32
 FIRST, SECOND, ALL = slice(0, U // 2), slice(U // 2, U), slice(0, U)
 QUARTERS = tuple(slice(c, c + S // 4) for c in range(0, S, S // 4))
 HALVES = (slice(0, S // 2), slice(S // 2, S))
-LEAD = P // 4
+LEAD = 8
 
 
 def entries(list_tile, part):
@@ -103,14 +103,15 @@ def tile_picked_ydpo_dpo_p_kernel(tc, x_words, x_scales, hT, gT, offs, win, los,
             nc.vector.tensor_scalar(dst, src, SIGNS[side], None, ALU.mult)
 
         def cast_g(i, side, cols=slice(0, P)):
-            dst, src = by_lines(i, side, cols)
+            dst = grouped[i, side].rearrange("p (t j) -> p t j", j=PACK)[:, cols]
+            src = raw[i, side][:].rearrange("p (j t) -> p t j", j=PACK)[:, cols]
             nc.gpsimd.tensor_scalar(dst, src, SIGNS[side], 0.0, ALU.mult, ALU.add)
 
         sign = {}
 
         def make_sign(i, side):
             sign[i, side] = sbuf("sign%d%s" % (i, "hg"[side]), 1, F32)
-            nc.gpsimd.memset(sign[i, side][:], SIGNS[side])
+            nc.vector.memset(sign[i, side][:], SIGNS[side])
 
         def cast_v2(i, side, start=0):
             dst, src = by_lines(i, side, slice(start, start + LEAD))
@@ -162,10 +163,9 @@ def tile_picked_ydpo_dpo_p_kernel(tc, x_words, x_scales, hT, gT, offs, win, los,
         def store(i, weight, pairs, queue=nc.sync):
             queue.dma_start(out=out[P * i : P * (i + 1), pairs], in_=weight)
 
+        nc.vector.memset(table_scales[:].bitcast(I32), 0)
         for key in ((1, G), (2, H), (2, G), (3, H), (3, G)):
             make_sign(*key)
-
-        nc.vector.memset(table_scales[:].bitcast(I32), 0)
         nc.sync.dma_start(offs_sb[:], offs)
         load(0, H)
         load_scales()

@@ -67,7 +67,7 @@ def tile_picked_ydpo_dpo_p_kernel(tc, x_words, x_scales, hT, gT, offs, win, los,
         def warm_up():
             warm_in = keep.tile([P, 1], F32, name="warm_in")
             warm_out = keep.tile([P, 1], F32, name="warm_out")
-            nc.gpsimd.memset(warm_in[:], 0.0)
+            nc.vector.memset(warm_in[:], 0.0)
             nc.scalar.activation(warm_out[:], warm_in[:], ACT.Sigmoid)
 
         x_scale = sbuf("x_scale", S, U8)
@@ -164,8 +164,8 @@ def tile_picked_ydpo_dpo_p_kernel(tc, x_words, x_scales, hT, gT, offs, win, los,
             queue.dma_start(out=out[P * i : P * (i + 1), pairs], in_=weight)
 
         nc.vector.memset(table_scales[:].bitcast(I32), 0)
-        for key in ((1, G), (2, H), (2, G), (3, H), (3, G)):
-            make_sign(*key)
+        for i in range(1, TILES):
+            make_sign(i, G)
         nc.sync.dma_start(offs_sb[:], offs)
         load(0, H)
         load_scales()
@@ -174,10 +174,10 @@ def tile_picked_ydpo_dpo_p_kernel(tc, x_words, x_scales, hT, gT, offs, win, los,
         load(1, H)
         load(1, G)
         nc.sync.dma_start(los_sb[:], los)
-        nc.sync.dma_start(win_sb[:], win)
         for i in (2, 3):
             load(i, H)
             load(i, G)
+        nc.sync.dma_start(win_sb[:], win)
         warm_up()
 
         nc.vector.tensor_copy(x_scale[:], table_scales[:].indirect(offs_sb[:]))
@@ -199,26 +199,23 @@ def tile_picked_ydpo_dpo_p_kernel(tc, x_words, x_scales, hT, gT, offs, win, los,
         acc2 = [bank(6 + n, "acc2_%d" % n) for n in range(2)]
         acc3 = [bank(n, "acc3_%d" % n) for n in range(2)]
         HALF = U // 2
-        rej0a = sbuf("rej0a", HALF, F32)
-        fetch_s(rej0a[:], dd0, los_sb, FIRST)
+        rej0 = sbuf("rej0", U, F32)
+        fetch_s(rej0[:], dd0, los_sb, ALL)
         cast_v2(1, G)
         quantize(1, H, plane_in=(1, G))
         multiply(1, H, acc1, HALVES)
-        cast_v2(2, H)
-        quantize(1, G, plane_in=(2, H))
+        quantize(1, G)
         multiply(1, G, acc1, HALVES)
         dd1 = sbuf("dd1", S, F32)
         for acc, cols in zip(acc1, HALVES):
             evac_s(dd1, acc, cols)
-        rej0b = sbuf("rej0b", HALF, F32, takes_over="codes1g")
-        fetch_s(rej0b[:], dd0, los_sb, SECOND)
         rej1a = sbuf("rej1a", HALF, F32)
         fetch_s(rej1a[:], dd1, los_sb, FIRST)
+        cast_v(2, H)
         cast_v2(2, G)
         quantize(2, H, plane_in=(2, G))
         multiply(2, H, acc2, HALVES)
-        cast_v2(3, H)
-        quantize(2, G, plane_in=(3, H))
+        quantize(2, G)
         multiply(2, G, acc2, HALVES)
         dd2 = sbuf("dd2", S, F32)
         for acc, cols in zip(acc2, HALVES):
@@ -227,14 +224,13 @@ def tile_picked_ydpo_dpo_p_kernel(tc, x_words, x_scales, hT, gT, offs, win, los,
         fetch_s(rej1b[:], dd1, los_sb, SECOND)
         rej2 = sbuf("rej2", U, F32)
         fetch_s(rej2[:], dd2, los_sb, ALL)
+        cast_v(3, H)
         cast_v2(3, G)
         quantize(3, H, plane_in=(3, G))
         multiply(3, H, acc3, HALVES)
-        m0a, m0b = row(3, G, 1), row(3, G, 2)
-        fetch_sub(m0a, dd0, win_sb, FIRST, rej0a[:])
         quantize(3, G)
         multiply(3, G, acc3, HALVES)
-        fetch_sub(m0b, dd0, win_sb, SECOND, rej0b[:])
+        fetch_sub(row(3, G, 1, 2), dd0, win_sb, ALL, rej0[:])
         m1 = sbuf("m1", U, F32, takes_over="grouped3h")
         fetch_sub(m1[:, FIRST], dd1, win_sb, FIRST, rej1a[:])
         dd3 = sbuf("dd3", S, F32)
@@ -243,13 +239,13 @@ def tile_picked_ydpo_dpo_p_kernel(tc, x_words, x_scales, hT, gT, offs, win, los,
         m1b = sbuf("m1b", HALF, F32, takes_over="codes3g")
         fetch_sub(m1b[:], dd1, win_sb, SECOND, rej1b[:])
         w = [sbuf("w%d" % i, U, F32) for i in range(1, TILES)]
-        w0 = sbuf("w0", U, F32, takes_over="scales3g")
-        weigh(w0[:], row(3, G, 1, 2))
-        store(0, w0[:], ALL)
         rej3 = sbuf("rej3", U, F32)
         fetch_s(rej3[:, FIRST], dd3, los_sb, FIRST)
         fetch_s(rej3[:, SECOND], dd3, los_sb, SECOND)
-        m2 = sbuf("m2", U, F32, takes_over="codes1g")
+        w0 = sbuf("w0", U, F32, takes_over="codes2g")
+        weigh(w0[:], row(3, G, 1, 2))
+        store(0, w0[:], ALL)
+        m2 = sbuf("m2", U, F32, takes_over="scales3h")
         fetch_sub(m2[:], dd2, win_sb, ALL, rej2[:])
         weigh(w[0][:, FIRST], m1[:, FIRST])
         weigh(w[0][:, SECOND], m1b[:])

@@ -164,7 +164,7 @@ def tile_picked_ydpo_dpo_p_kernel(tc, x_words, x_scales, hT, gT, offs, win, los,
             queue.dma_start(out=out[P * i : P * (i + 1), pairs], in_=weight)
 
         nc.vector.memset(table_scales[:].bitcast(I32), 0)
-        for i in range(1, TILES):
+        for i in range(2, TILES):
             make_sign(i, G)
         nc.sync.dma_start(offs_sb[:], offs)
         load(0, H)
@@ -174,10 +174,11 @@ def tile_picked_ydpo_dpo_p_kernel(tc, x_words, x_scales, hT, gT, offs, win, los,
         load(1, H)
         load(1, G)
         nc.sync.dma_start(los_sb[:], los)
-        for i in (2, 3):
-            load(i, H)
-            load(i, G)
+        load(2, H)
+        load(2, G)
+        load(3, H)
         nc.sync.dma_start(win_sb[:], win)
+        load(3, G)
         warm_up()
 
         nc.vector.tensor_copy(x_scale[:], table_scales[:].indirect(offs_sb[:]))
@@ -190,8 +191,9 @@ def tile_picked_ydpo_dpo_p_kernel(tc, x_words, x_scales, hT, gT, offs, win, los,
         for acc, cols in zip(acc0, QUARTERS):
             for side in (H, G):
                 product(0, side, acc, cols)
-        cast_s(1, H)
-        dd0 = sbuf("dd0", S, F32, takes_over="raw1h")
+        cast_g(1, H)
+        cast_s(1, G)
+        dd0 = sbuf("dd0", S, F32, takes_over="raw1g")
         for acc, cols in zip(acc0, QUARTERS):
             evac_s(dd0, acc, cols)
 
@@ -200,13 +202,13 @@ def tile_picked_ydpo_dpo_p_kernel(tc, x_words, x_scales, hT, gT, offs, win, los,
         acc3 = [bank(n, "acc3_%d" % n) for n in range(2)]
         HALF = U // 2
         rej0 = sbuf("rej0", U, F32)
-        fetch_s(rej0[:], dd0, los_sb, ALL)
-        cast_v2(1, G)
-        quantize(1, H, plane_in=(1, G))
+        for pairs in (FIRST, SECOND):
+            fetch_s(rej0[:, pairs], dd0, los_sb, pairs)
+        quantize(1, H)
         multiply(1, H, acc1, HALVES)
         quantize(1, G)
         multiply(1, G, acc1, HALVES)
-        dd1 = sbuf("dd1", S, F32)
+        dd1 = sbuf("dd1", S, F32, takes_over="raw2g")
         for acc, cols in zip(acc1, HALVES):
             evac_s(dd1, acc, cols)
         rej1a = sbuf("rej1a", HALF, F32)
@@ -225,12 +227,15 @@ def tile_picked_ydpo_dpo_p_kernel(tc, x_words, x_scales, hT, gT, offs, win, los,
         rej2 = sbuf("rej2", U, F32)
         fetch_s(rej2[:], dd2, los_sb, ALL)
         cast_v(3, H)
+        m0a = sbuf("m0a", HALF, F32)
+        fetch_sub(m0a[:], dd0, win_sb, FIRST, rej0[:, FIRST])
         cast_v2(3, G)
         quantize(3, H, plane_in=(3, G))
         multiply(3, H, acc3, HALVES)
+        m0b = row(3, G, 1)
         quantize(3, G)
         multiply(3, G, acc3, HALVES)
-        fetch_sub(row(3, G, 1, 2), dd0, win_sb, ALL, rej0[:])
+        fetch_sub(m0b, dd0, win_sb, SECOND, rej0[:, SECOND])
         m1 = sbuf("m1", U, F32, takes_over="grouped3h")
         fetch_sub(m1[:, FIRST], dd1, win_sb, FIRST, rej1a[:])
         dd3 = sbuf("dd3", S, F32)
@@ -243,9 +248,10 @@ def tile_picked_ydpo_dpo_p_kernel(tc, x_words, x_scales, hT, gT, offs, win, los,
         fetch_s(rej3[:, FIRST], dd3, los_sb, FIRST)
         fetch_s(rej3[:, SECOND], dd3, los_sb, SECOND)
         w0 = sbuf("w0", U, F32, takes_over="codes2g")
-        weigh(w0[:], row(3, G, 1, 2))
+        weigh(w0[:, FIRST], m0a[:])
+        weigh(w0[:, SECOND], m0b)
         store(0, w0[:], ALL)
-        m2 = sbuf("m2", U, F32, takes_over="scales3h")
+        m2 = sbuf("m2", U, F32, takes_over="scales3g")
         fetch_sub(m2[:], dd2, win_sb, ALL, rej2[:])
         weigh(w[0][:, FIRST], m1[:, FIRST])
         weigh(w[0][:, SECOND], m1b[:])

@@ -78,9 +78,21 @@ def tile_picked_ydpo_dpo_p_kernel(tc, x_words, x_scales, hT, gT, offs, win, los,
         grouped = {(0, side): grouped0[:, P * PACK * side : P * PACK * (side + 1)] for side in (H, G)}
         codes = {(0, side): codes0[:, P * side : P * (side + 1)] for side in (H, G)}
         scales = {(0, side): scales0[:, P * side : P * (side + 1)] for side in (H, G)}
-        for i in range(1, TILES):
+        for side in (H, G):
+            grouped[1, side] = sbuf("grouped1%s" % "hg"[side], P * PACK, BF16)[:]
+        both = {}
+        for i in (2, 3):
+            both[i] = sbuf("grouped%d" % i, 2 * P * PACK, BF16)
             for side in (H, G):
-                grouped[i, side] = sbuf("grouped%d%s" % (i, "hg"[side]), P * PACK, BF16)[:]
+                grouped[i, side] = both[i][:, P * PACK * side : P * PACK * (side + 1)]
+
+        def quantize_both(i):
+            code = sbuf("codes%d" % i, 2 * P, U32)
+            plane = sbuf("scales%d" % i, 2 * P, U8)
+            for side in (H, G):
+                codes[i, side] = code[:, P * side : P * (side + 1)]
+                scales[i, side] = plane[:, P * side : P * (side + 1)]
+            nc.vector.quantize_mx(out=code[:].bitcast(FP8X4), scales=plane[:], in_=both[i][:])
 
         def bank(n, name):
             return psum.tile([P, S], F32, name=name, tag="bank%d" % n)
@@ -164,8 +176,7 @@ def tile_picked_ydpo_dpo_p_kernel(tc, x_words, x_scales, hT, gT, offs, win, los,
             queue.dma_start(out=out[P * i : P * (i + 1), pairs], in_=weight)
 
         nc.vector.memset(table_scales[:].bitcast(I32), 0)
-        for i in range(2, TILES):
-            make_sign(i, G)
+        warm_up()
         nc.sync.dma_start(offs_sb[:], offs)
         load(0, H)
         load_scales()
@@ -174,12 +185,10 @@ def tile_picked_ydpo_dpo_p_kernel(tc, x_words, x_scales, hT, gT, offs, win, los,
         load(1, H)
         load(1, G)
         nc.sync.dma_start(los_sb[:], los)
-        load(2, H)
-        load(2, G)
-        load(3, H)
+        for i in (2, 3):
+            load(i, H)
+            load(i, G)
         nc.sync.dma_start(win_sb[:], win)
-        load(3, G)
-        warm_up()
 
         nc.vector.tensor_copy(x_scale[:], table_scales[:].indirect(offs_sb[:]))
         cast_s(0, H)
@@ -200,67 +209,52 @@ def tile_picked_ydpo_dpo_p_kernel(tc, x_words, x_scales, hT, gT, offs, win, los,
         acc1 = [bank(4 + n, "acc1_%d" % n) for n in range(2)]
         acc2 = [bank(6 + n, "acc2_%d" % n) for n in range(2)]
         acc3 = [bank(n, "acc3_%d" % n) for n in range(2)]
-        HALF = U // 2
+        w = [sbuf("w%d" % i, U, F32) for i in range(TILES)]
         rej0 = sbuf("rej0", U, F32)
-        for pairs in (FIRST, SECOND):
-            fetch_s(rej0[:, pairs], dd0, los_sb, pairs)
+        fetch_s(rej0[:], dd0, los_sb, ALL)
         quantize(1, H)
         multiply(1, H, acc1, HALVES)
+        cast_v(2, H)
         quantize(1, G)
         multiply(1, G, acc1, HALVES)
+        cast_v(2, G)
         dd1 = sbuf("dd1", S, F32, takes_over="raw2g")
         for acc, cols in zip(acc1, HALVES):
             evac_s(dd1, acc, cols)
-        rej1a = sbuf("rej1a", HALF, F32)
-        fetch_s(rej1a[:], dd1, los_sb, FIRST)
-        cast_v(2, H)
-        cast_v2(2, G)
-        quantize(2, H, plane_in=(2, G))
-        multiply(2, H, acc2, HALVES)
-        quantize(2, G)
-        multiply(2, G, acc2, HALVES)
+        quantize_both(2)
+        for side in (H, G):
+            multiply(2, side, acc2, HALVES)
+        for side in (H, G):
+            cast_v(3, side)
+            quantize(3, side)
+            multiply(3, side, acc3, HALVES)
         dd2 = sbuf("dd2", S, F32)
         for acc, cols in zip(acc2, HALVES):
             evac_s(dd2, acc, cols)
-        rej1b = sbuf("rej1b", HALF, F32, takes_over="codes2g")
-        fetch_s(rej1b[:], dd1, los_sb, SECOND)
+        rej1 = sbuf("rej1", U, F32, takes_over="scales2")[:]
+        m0 = sbuf("m0", U, F32, takes_over="raw3g")[:]
+        fetch_s(rej1, dd1, los_sb, ALL)
+        fetch_sub(m0, dd0, win_sb, ALL, rej0[:])
         rej2 = sbuf("rej2", U, F32)
         fetch_s(rej2[:], dd2, los_sb, ALL)
-        cast_v(3, H)
-        m0a = sbuf("m0a", HALF, F32)
-        fetch_sub(m0a[:], dd0, win_sb, FIRST, rej0[:, FIRST])
-        cast_v2(3, G)
-        quantize(3, H, plane_in=(3, G))
-        multiply(3, H, acc3, HALVES)
-        m0b = row(3, G, 1)
-        quantize(3, G)
-        multiply(3, G, acc3, HALVES)
-        fetch_sub(m0b, dd0, win_sb, SECOND, rej0[:, SECOND])
-        m1 = sbuf("m1", U, F32, takes_over="grouped3h")
-        fetch_sub(m1[:, FIRST], dd1, win_sb, FIRST, rej1a[:])
+        weigh(w[0][:], m0)
+        store(0, w[0][:], ALL)
         dd3 = sbuf("dd3", S, F32)
-        evac_v(dd3, acc3[0], HALVES[0])
-        evac_v(dd3, acc3[1], HALVES[1])
-        m1b = sbuf("m1b", HALF, F32, takes_over="codes3g")
-        fetch_sub(m1b[:], dd1, win_sb, SECOND, rej1b[:])
-        w = [sbuf("w%d" % i, U, F32) for i in range(1, TILES)]
+        for acc, cols in zip(acc3, HALVES):
+            evac_v(dd3, acc, cols)
+        m12 = sbuf("m12", 2 * U, F32, takes_over="scales3g")
+        m1, m2 = m12[:, :U], m12[:, U:]
+        fetch_sub(m1, dd1, win_sb, ALL, rej1)
+        fetch_sub(m2, dd2, win_sb, ALL, rej2[:])
         rej3 = sbuf("rej3", U, F32)
-        fetch_s(rej3[:, FIRST], dd3, los_sb, FIRST)
-        fetch_s(rej3[:, SECOND], dd3, los_sb, SECOND)
-        w0 = sbuf("w0", U, F32, takes_over="codes2g")
-        weigh(w0[:, FIRST], m0a[:])
-        weigh(w0[:, SECOND], m0b)
-        store(0, w0[:], ALL)
-        m2 = sbuf("m2", U, F32, takes_over="scales3g")
-        fetch_sub(m2[:], dd2, win_sb, ALL, rej2[:])
-        weigh(w[0][:, FIRST], m1[:, FIRST])
-        weigh(w[0][:, SECOND], m1b[:])
-        store(1, w[0][:], ALL)
-        m3 = sbuf("m3", U, F32)
-        fetch_sub(m3[:, FIRST], dd3, win_sb, FIRST, rej3[:, FIRST])
-        fetch_sub(m3[:, SECOND], dd3, win_sb, SECOND, rej3[:, SECOND])
-        weigh(w[1][:], m2[:])
-        store(2, w[1][:], ALL)
         for pairs in (FIRST, SECOND):
-            weigh(w[2][:, pairs], m3[:, pairs])
-            store(3, w[2][:, pairs], pairs)
+            fetch_s(rej3[:, pairs], dd3, los_sb, pairs)
+        m3 = sbuf("m3", U, F32)
+        for pairs in (FIRST, SECOND):
+            fetch_sub(m3[:, pairs], dd3, win_sb, pairs, rej3[:, pairs])
+        for i, m in ((1, m1), (2, m2)):
+            weigh(w[i][:], m)
+            store(i, w[i][:], ALL)
+        for pairs in (FIRST, SECOND):
+            weigh(w[3][:, pairs], m3[:, pairs])
+            store(3, w[3][:, pairs], pairs)

@@ -97,10 +97,10 @@ def tile_picked_ydpo_dpo_p_kernel(tc, x_words, x_scales, hT, gT, offs, win, los,
         def bank(n, name):
             return psum.tile([P, S], F32, name=name, tag="bank%d" % n)
 
-        def by_lines(i, side, cols):
-            part = slice(cols.start // LINE, cols.stop // LINE)
-            dst = grouped[i, side].rearrange("p (c l j) -> p c j l", l=LINE, j=PACK)
-            src = raw[i, side][:].rearrange("p (j c l) -> p c j l", l=LINE, j=PACK)
+        def by_lines(i, side, cols, run=LINE):
+            part = slice(cols.start // run, cols.stop // run)
+            dst = grouped[i, side].rearrange("p (c l j) -> p c j l", l=run, j=PACK)
+            src = raw[i, side][:].rearrange("p (j c l) -> p c j l", l=run, j=PACK)
             return dst[:, part], src[:, part]
 
         def cast_s(i, side, cols=slice(0, P)):
@@ -111,7 +111,7 @@ def tile_picked_ydpo_dpo_p_kernel(tc, x_words, x_scales, hT, gT, offs, win, los,
                 nc.scalar.activation(dst, src, ACT.Copy, scale=SIGNS[side])
 
         def cast_v(i, side, cols=slice(0, P)):
-            dst, src = by_lines(i, side, cols)
+            dst, src = by_lines(i, side, cols, 2)
             nc.vector.tensor_scalar(dst, src, SIGNS[side], None, ALU.mult)
 
         def cast_g(i, side, cols=slice(0, P)):

@@ -17,7 +17,6 @@ ALU = mybir.AluOpType
 
 P = 128
 PACK = 4
-LINE = 4
 TILES = V // P
 H, G = 0, 1
 SIGNS = (1.0, -1.0)
@@ -26,7 +25,7 @@ QUADRANT = 32
 FIRST, SECOND, ALL = slice(0, U // 2), slice(U // 2, U), slice(0, U)
 QUARTERS = tuple(slice(c, c + S // 4) for c in range(0, S, S // 4))
 HALVES = (slice(0, S // 2), slice(S // 2, S))
-LEAD = 8
+WHOLE = (slice(0, S),)
 
 
 def entries(list_tile, part):
@@ -42,16 +41,22 @@ def tile_picked_ydpo_dpo_p_kernel(tc, x_words, x_scales, hT, gT, offs, win, los,
         def sbuf(name, columns, dtype, takes_over=None):
             return keep.tile([P, columns], dtype, name=name, tag=takes_over or name, align_bytes=64)
 
+        def label(kind, i, side):
+            return "%s%d%s" % (kind, i, "hg"[side])
+
         offs_sb = keep.tile([P, S // 16], U16, name="offs_sb")
         win_sb = keep.tile([P, U // 16], U16, name="win_sb")
         los_sb = keep.tile([P, U // 16], U16, name="los_sb")
         table_words = sbuf("table_words", T, I32)
         table_scales = sbuf("table_scales", T, U8)
-        raw = {(i, side): sbuf("raw%d%s" % (i, "hg"[side]), PACK * P, F32) for i in range(TILES) for side in (H, G)}
+        raw = {(i, side): sbuf(label("raw", i, side), PACK * P, F32) for i in range(TILES) for side in (H, G)}
         rows = [a.rearrange("(p j) t -> p j t", j=PACK) for a in (hT, gT)]
+        x_scale = {}
+        x_code = sbuf("x_code", S, U32)
+        grouped, both, codes, scales = {}, {}, {}, {}
 
-        def load(i, side, queue=nc.sync):
-            queue.dma_start(out=raw[i, side][:].rearrange("p (j t) -> p j t", j=PACK), in_=rows[side][:, :, P * i : P * (i + 1)])
+        def load(i, side):
+            nc.sync.dma_start(out=raw[i, side][:].rearrange("p (j t) -> p j t", j=PACK), in_=rows[side][:, :, P * i : P * (i + 1)])
 
         def load_scales():
             per_quadrant = SCALE_ROWS * QUADRANT // P
@@ -61,8 +66,8 @@ def tile_picked_ydpo_dpo_p_kernel(tc, x_words, x_scales, hT, gT, offs, win, los,
                     in_=x_scales[0, r:SCALE_ROWS:per_quadrant, :].bitcast(I32),
                 )
 
-        def load_words(queue=nc.sync):
-            queue.dma_start(out=table_words[:], in_=x_words[0].rearrange("p n r -> p (n r)").bitcast(I32))
+        def load_words():
+            nc.sync.dma_start(out=table_words[:], in_=x_words[0].rearrange("p n r -> p (n r)").bitcast(I32))
 
         def warm_up():
             warm_in = keep.tile([P, 1], F32, name="warm_in")
@@ -70,48 +75,30 @@ def tile_picked_ydpo_dpo_p_kernel(tc, x_words, x_scales, hT, gT, offs, win, los,
             nc.vector.memset(warm_in[:], 0.0)
             nc.scalar.activation(warm_out[:], warm_in[:], ACT.Sigmoid)
 
-        x_scale = sbuf("x_scale", S, U8)
-        x_code = sbuf("x_code", S, U32)
-        grouped0 = sbuf("grouped0", 2 * P * PACK, BF16)
-        codes0 = sbuf("codes0", 2 * P, U32)
-        scales0 = sbuf("scales0", 2 * P, U8)
-        grouped = {(0, side): grouped0[:, P * PACK * side : P * PACK * (side + 1)] for side in (H, G)}
-        codes = {(0, side): codes0[:, P * side : P * (side + 1)] for side in (H, G)}
-        scales = {(0, side): scales0[:, P * side : P * (side + 1)] for side in (H, G)}
-        for side in (H, G):
-            grouped[1, side] = sbuf("grouped1%s" % "hg"[side], P * PACK, BF16)[:]
-        both = {}
-        for i in (2, 3):
-            both[i] = sbuf("grouped%d" % i, 2 * P * PACK, BF16)
+        def stage_together(i, takes_over=None):
+            both[i] = sbuf("grouped%d" % i, 2 * P * PACK, BF16, takes_over)
             for side in (H, G):
                 grouped[i, side] = both[i][:, P * PACK * side : P * PACK * (side + 1)]
 
-        def quantize_both(i):
-            code = sbuf("codes%d" % i, 2 * P, U32)
-            plane = sbuf("scales%d" % i, 2 * P, U8)
+        def stage_apart(i):
             for side in (H, G):
-                codes[i, side] = code[:, P * side : P * (side + 1)]
-                scales[i, side] = plane[:, P * side : P * (side + 1)]
-            nc.vector.quantize_mx(out=code[:].bitcast(FP8X4), scales=plane[:], in_=both[i][:])
+                grouped[i, side] = sbuf(label("grouped", i, side), P * PACK, BF16)[:]
 
-        def bank(n, name):
-            return psum.tile([P, S], F32, name=name, tag="bank%d" % n)
-
-        def by_lines(i, side, cols, run=LINE):
+        def by_runs(i, side, run, cols):
             part = slice(cols.start // run, cols.stop // run)
             dst = grouped[i, side].rearrange("p (c l j) -> p c j l", l=run, j=PACK)
             src = raw[i, side][:].rearrange("p (j c l) -> p c j l", l=run, j=PACK)
             return dst[:, part], src[:, part]
 
         def cast_s(i, side, cols=slice(0, P)):
-            dst, src = by_lines(i, side, cols)
+            dst, src = by_runs(i, side, 4, cols)
             if side == H:
                 nc.scalar.copy(dst, src)
             else:
                 nc.scalar.activation(dst, src, ACT.Copy, scale=SIGNS[side])
 
         def cast_v(i, side, cols=slice(0, P)):
-            dst, src = by_lines(i, side, cols, 2)
+            dst, src = by_runs(i, side, 2, cols)
             nc.vector.tensor_scalar(dst, src, SIGNS[side], None, ALU.mult)
 
         def cast_g(i, side, cols=slice(0, P)):
@@ -119,25 +106,25 @@ def tile_picked_ydpo_dpo_p_kernel(tc, x_words, x_scales, hT, gT, offs, win, los,
             src = raw[i, side][:].rearrange("p (j t) -> p t j", j=PACK)[:, cols]
             nc.gpsimd.tensor_scalar(dst, src, SIGNS[side], 0.0, ALU.mult, ALU.add)
 
-        sign = {}
+        def quantize_both(i, takes_over=None):
+            code = sbuf("codes%d" % i, 2 * P, U32, takes_over)
+            plane = sbuf("scales%d" % i, 2 * P, U8)
+            for side in (H, G):
+                codes[i, side] = code[:, P * side : P * (side + 1)]
+                scales[i, side] = plane[:, P * side : P * (side + 1)]
+            nc.vector.quantize_mx(out=code[:].bitcast(FP8X4), scales=plane[:], in_=both[i][:])
 
-        def make_sign(i, side):
-            sign[i, side] = sbuf("sign%d%s" % (i, "hg"[side]), 1, F32)
-            nc.vector.memset(sign[i, side][:], SIGNS[side])
-
-        def cast_v2(i, side, start=0):
-            dst, src = by_lines(i, side, slice(start, start + LEAD))
-            nc.vector.tensor_scalar(dst, src, sign[i, side][:], None, ALU.mult)
-            cast_v(i, side, slice(start + LEAD, P))
-
-        def row(i, side, j, n=1):
-            return raw[i, side][:, P * j : P * (j + n)]
-
-        def quantize(i, side, plane_in=None, takes_over=None):
-            codes[i, side] = sbuf("codes%d%s" % (i, "hg"[side]), P, U32, takes_over)[:]
-            behind = None if plane_in is None else "sign%d%s" % (plane_in[0], "hg"[plane_in[1]])
-            scales[i, side] = sbuf("scales%d%s" % (i, "hg"[side]), P, U8, behind)[:]
+        def quantize(i, side, takes_over=None):
+            codes[i, side] = sbuf(label("codes", i, side), P, U32, takes_over)[:]
+            scales[i, side] = sbuf(label("scales", i, side), P, U8)[:]
             nc.vector.quantize_mx(out=codes[i, side].bitcast(FP8X4), scales=scales[i, side], in_=grouped[i, side])
+
+        def banks(first, i, pieces):
+            return [psum.tile([P, S], F32, name="acc%d_%d" % (i, n), tag="bank%d" % (first + n)) for n in range(len(pieces))]
+
+        def picked_scales(cols):
+            start = max(c for c in x_scale if c <= cols.start)
+            return x_scale[start][:, cols.start - start : cols.stop - start]
 
         def product(i, side, acc, cols):
             nc.tensor.matmul_mx(
@@ -145,7 +132,7 @@ def tile_picked_ydpo_dpo_p_kernel(tc, x_words, x_scales, hT, gT, offs, win, los,
                 lhsT=codes[i, side].bitcast(FP8X4),
                 lhsT_scale=scales[i, side],
                 rhs=x_code[:, cols].bitcast(FP8X4),
-                rhs_scale=x_scale[:, cols],
+                rhs_scale=picked_scales(cols),
                 start=(side == H),
                 stop=(side == G),
             )
@@ -154,6 +141,12 @@ def tile_picked_ydpo_dpo_p_kernel(tc, x_words, x_scales, hT, gT, offs, win, los,
             for acc, cols in zip(accs, pieces):
                 product(i, side, acc, cols)
 
+        def gather_words(cols):
+            nc.vector.tensor_copy(x_code[:, cols], table_words[:].bitcast(U32).indirect(entries(offs_sb, cols)))
+
+        def gather_scales(cols):
+            nc.vector.tensor_copy(picked_scales(cols), table_scales[:].indirect(entries(offs_sb, cols)))
+
         def evac_s(dd, acc, cols):
             nc.scalar.copy(dd[:, cols], acc[:, : cols.stop - cols.start])
 
@@ -161,20 +154,35 @@ def tile_picked_ydpo_dpo_p_kernel(tc, x_words, x_scales, hT, gT, offs, win, los,
             nc.vector.tensor_copy(dd[:, cols], acc[:, : cols.stop - cols.start])
 
         def fetch_s(dst, dd, lst, pairs):
-            nc.scalar.activation(dst, dd[:].indirect(entries(lst, pairs)), ACT.Copy)
+            nc.scalar.activation(dst[:, pairs], dd[:].indirect(entries(lst, pairs)), ACT.Copy)
 
         def fetch_v(dst, dd, lst, pairs):
-            nc.vector.tensor_copy(dst, dd[:].indirect(entries(lst, pairs)))
+            nc.vector.tensor_copy(dst[:, pairs], dd[:].indirect(entries(lst, pairs)))
 
         def fetch_sub(dst, dd, lst, pairs, other):
-            nc.vector.tensor_tensor(dst, dd[:].indirect(entries(lst, pairs)), other, ALU.subtract)
+            nc.vector.tensor_tensor(dst[:, pairs], dd[:].indirect(entries(lst, pairs)), other[:, pairs], ALU.subtract)
 
-        def weigh(weight, margin, scale=-0.5):
-            nc.scalar.activation(weight, margin, ACT.Sigmoid, scale=scale)
+        def sub(engine, dst, a, b, pairs):
+            engine.tensor_tensor(dst[:, pairs], a[:, pairs], b[:, pairs], ALU.subtract)
 
-        def store(i, weight, pairs, queue=nc.sync):
-            queue.dma_start(out=out[P * i : P * (i + 1), pairs], in_=weight)
+        def weigh(weight, margin, pairs, scale=-0.5):
+            nc.scalar.activation(weight[:, pairs], margin[:, pairs], ACT.Sigmoid, scale=scale)
 
+        def store(i, weight, pairs):
+            nc.sync.dma_start(out=out[P * i : P * (i + 1), pairs], in_=weight[:, pairs])
+
+        def finish(i, margin, pairs, scale=-0.5):
+            if i not in w:
+                w[i] = sbuf("w%d" % i, U, F32)
+            weigh(w[i], margin, pairs, scale)
+            store(i, w[i], pairs)
+
+        w = {}
+
+        stage_together(0)
+        stage_apart(1)
+        stage_together(2)
+        stage_together(3)
         nc.vector.memset(table_scales[:].bitcast(I32), 0)
         warm_up()
         nc.sync.dma_start(offs_sb[:], offs)
@@ -185,33 +193,35 @@ def tile_picked_ydpo_dpo_p_kernel(tc, x_words, x_scales, hT, gT, offs, win, los,
         load(1, H)
         load(1, G)
         nc.sync.dma_start(los_sb[:], los)
-        for i in (2, 3):
-            load(i, H)
-            load(i, G)
+        load(2, H)
+        load(2, G)
+        load(3, H)
+        load(3, G)
         nc.sync.dma_start(win_sb[:], win)
-
-        nc.vector.tensor_copy(x_scale[:], table_scales[:].indirect(offs_sb[:]))
+        x_scale[0] = sbuf("x_scale", S, U8)
+        gather_scales(WHOLE[0])
         cast_s(0, H)
         cast_s(0, G)
-        nc.vector.quantize_mx(out=codes0[:].bitcast(FP8X4), scales=scales0[:], in_=grouped0[:])
+        quantize_both(0)
         for cols in QUARTERS:
-            nc.vector.tensor_copy(x_code[:, cols], table_words[:].bitcast(U32).indirect(entries(offs_sb, cols)))
-        acc0 = [bank(n, "acc0_%d" % n) for n in range(4)]
-        for acc, cols in zip(acc0, QUARTERS):
+            gather_words(cols)
+        acc0 = banks(0, 0, QUARTERS[1:])
+        places0 = [acc0[0][:, : S // 4], acc0[0][:, S // 4 : S // 2], acc0[1], acc0[2]]
+        for acc, cols in zip(places0, QUARTERS):
             for side in (H, G):
                 product(0, side, acc, cols)
         cast_g(1, H)
         cast_s(1, G)
-        dd0 = sbuf("dd0", S, F32, takes_over="raw1g")
-        for acc, cols in zip(acc0, QUARTERS):
+        dd0 = sbuf("dd0", S, F32, takes_over="raw1h")
+        evac_s(dd0, acc0[0], HALVES[0])
+        for acc, cols in zip(acc0[1:], QUARTERS[2:]):
             evac_s(dd0, acc, cols)
+        acc1 = banks(4, 1, HALVES)
+        acc2 = banks(6, 2, HALVES)
+        acc3 = banks(0, 3, HALVES)
 
-        acc1 = [bank(4 + n, "acc1_%d" % n) for n in range(2)]
-        acc2 = [bank(6 + n, "acc2_%d" % n) for n in range(2)]
-        acc3 = [bank(n, "acc3_%d" % n) for n in range(2)]
-        w = [sbuf("w%d" % i, U, F32) for i in range(TILES)]
         rej0 = sbuf("rej0", U, F32)
-        fetch_s(rej0[:], dd0, los_sb, ALL)
+        fetch_s(rej0, dd0, los_sb, ALL)
         quantize(1, H)
         multiply(1, H, acc1, HALVES)
         cast_v(2, H)
@@ -222,8 +232,9 @@ def tile_picked_ydpo_dpo_p_kernel(tc, x_words, x_scales, hT, gT, offs, win, los,
         for acc, cols in zip(acc1, HALVES):
             evac_s(dd1, acc, cols)
         quantize_both(2)
-        for side in (H, G):
-            multiply(2, side, acc2, HALVES)
+        for acc, cols in zip(acc2, HALVES):
+            for side in (H, G):
+                product(2, side, acc, cols)
         for side in (H, G):
             cast_v(3, side)
             quantize(3, side)
@@ -231,30 +242,27 @@ def tile_picked_ydpo_dpo_p_kernel(tc, x_words, x_scales, hT, gT, offs, win, los,
         dd2 = sbuf("dd2", S, F32)
         for acc, cols in zip(acc2, HALVES):
             evac_s(dd2, acc, cols)
-        rej1 = sbuf("rej1", U, F32, takes_over="scales2")[:]
-        m0 = sbuf("m0", U, F32, takes_over="raw3g")[:]
+        rej1 = sbuf("rej1", U, F32, takes_over="scales2")
+        m0 = sbuf("m0", U, F32, takes_over="raw3g")
         fetch_s(rej1, dd1, los_sb, ALL)
-        fetch_sub(m0, dd0, win_sb, ALL, rej0[:])
+        fetch_sub(m0, dd0, win_sb, ALL, rej0)
         rej2 = sbuf("rej2", U, F32)
-        fetch_s(rej2[:], dd2, los_sb, ALL)
-        weigh(w[0][:], m0)
-        store(0, w[0][:], ALL)
         dd3 = sbuf("dd3", S, F32)
-        for acc, cols in zip(acc3, HALVES):
-            evac_v(dd3, acc, cols)
+        evac_s(dd3, acc3[0], HALVES[0])
+        fetch_s(rej2, dd2, los_sb, ALL)
+        finish(0, m0, ALL)
+        evac_v(dd3, acc3[1], HALVES[1])
         m12 = sbuf("m12", 2 * U, F32, takes_over="scales3g")
         m1, m2 = m12[:, :U], m12[:, U:]
         fetch_sub(m1, dd1, win_sb, ALL, rej1)
-        fetch_sub(m2, dd2, win_sb, ALL, rej2[:])
+        fetch_sub(m2, dd2, win_sb, ALL, rej2)
         rej3 = sbuf("rej3", U, F32)
         for pairs in (FIRST, SECOND):
-            fetch_s(rej3[:, pairs], dd3, los_sb, pairs)
+            fetch_s(rej3, dd3, los_sb, pairs)
         m3 = sbuf("m3", U, F32)
         for pairs in (FIRST, SECOND):
-            fetch_sub(m3[:, pairs], dd3, win_sb, pairs, rej3[:, pairs])
-        for i, m in ((1, m1), (2, m2)):
-            weigh(w[i][:], m)
-            store(i, w[i][:], ALL)
+            fetch_sub(m3, dd3, win_sb, pairs, rej3)
+        finish(1, m1, ALL)
+        finish(2, m2, ALL)
         for pairs in (FIRST, SECOND):
-            weigh(w[3][:, pairs], m3[:, pairs])
-            store(3, w[3][:, pairs], pairs)
+            finish(3, m3, pairs)

@@ -49,14 +49,19 @@ def tile_picked_ydpo_dpo_p_kernel(tc, x_words, x_scales, hT, gT, offs, win, los,
         los_sb = keep.tile([P, U // 16], U16, name="los_sb")
         table_words = sbuf("table_words", T, I32)
         table_scales = sbuf("table_scales", T, U8)
-        raw = {(i, side): sbuf(label("raw", i, side), PACK * P, F32) for i in range(TILES) for side in (H, G)}
+        raw = {}
         rows = [a.rearrange("(p j) t -> p j t", j=PACK) for a in (hT, gT)]
         x_scale = {}
         x_code = sbuf("x_code", S, U32)
         grouped, both, codes, scales = {}, {}, {}, {}
 
-        def load(i, side):
-            nc.sync.dma_start(out=raw[i, side][:].rearrange("p (j t) -> p j t", j=PACK), in_=rows[side][:, :, P * i : P * (i + 1)])
+        def load(side, start, stop):
+            raw[side, start] = sbuf("raw%s%d" % ("hg"[side], start), PACK * (stop - start), F32)
+            nc.sync.dma_start(out=raw[side, start][:].rearrange("p (j t) -> p j t", j=PACK), in_=rows[side][:, :, start:stop])
+
+        def loaded(i, side, cols):
+            start = max(s for d, s in raw if d == side and s <= P * i + cols.start)
+            return raw[side, start][:], slice(P * i + cols.start - start, P * i + cols.stop - start)
 
         def load_scales():
             per_quadrant = SCALE_ROWS * QUADRANT // P
@@ -85,10 +90,10 @@ def tile_picked_ydpo_dpo_p_kernel(tc, x_words, x_scales, hT, gT, offs, win, los,
                 grouped[i, side] = sbuf(label("grouped", i, side), P * PACK, BF16)[:]
 
         def by_runs(i, side, run, cols):
-            part = slice(cols.start // run, cols.stop // run)
+            source, place = loaded(i, side, cols)
             dst = grouped[i, side].rearrange("p (c l j) -> p c j l", l=run, j=PACK)
-            src = raw[i, side][:].rearrange("p (j c l) -> p c j l", l=run, j=PACK)
-            return dst[:, part], src[:, part]
+            src = source.rearrange("p (j c l) -> p c j l", l=run, j=PACK)
+            return dst[:, cols.start // run : cols.stop // run], src[:, place.start // run : place.stop // run]
 
         def cast_s(i, side, cols=slice(0, P)):
             dst, src = by_runs(i, side, 4, cols)
@@ -103,7 +108,8 @@ def tile_picked_ydpo_dpo_p_kernel(tc, x_words, x_scales, hT, gT, offs, win, los,
 
         def cast_g(i, side, cols=slice(0, P)):
             dst = grouped[i, side].rearrange("p (t j) -> p t j", j=PACK)[:, cols]
-            src = raw[i, side][:].rearrange("p (j t) -> p t j", j=PACK)[:, cols]
+            source, place = loaded(i, side, cols)
+            src = source.rearrange("p (j t) -> p t j", j=PACK)[:, place]
             nc.gpsimd.tensor_scalar(dst, src, SIGNS[side], 0.0, ALU.mult, ALU.add)
 
         def quantize_both(i, takes_over=None):
@@ -112,7 +118,7 @@ def tile_picked_ydpo_dpo_p_kernel(tc, x_words, x_scales, hT, gT, offs, win, los,
             for side in (H, G):
                 codes[i, side] = code[:, P * side : P * (side + 1)]
                 scales[i, side] = plane[:, P * side : P * (side + 1)]
-            nc.vector.quantize_mx(out=code[:].bitcast(FP8X4), scales=plane[:], in_=both[i][:])
+            nc.vector.quantize_mx(out=code[:].bitcast(FP8X4), scales=plane[:], in_=both[i][:, :])
 
         def quantize(i, side, takes_over=None):
             codes[i, side] = sbuf(label("codes", i, side), P, U32, takes_over)[:]
@@ -126,20 +132,20 @@ def tile_picked_ydpo_dpo_p_kernel(tc, x_words, x_scales, hT, gT, offs, win, los,
             start = max(c for c in x_scale if c <= cols.start)
             return x_scale[start][:, cols.start - start : cols.stop - start]
 
-        def product(i, side, acc, cols):
+        def product(i, side, acc, cols, first=H):
             nc.tensor.matmul_mx(
                 out=acc[:, : cols.stop - cols.start],
                 lhsT=codes[i, side].bitcast(FP8X4),
                 lhsT_scale=scales[i, side],
                 rhs=x_code[:, cols].bitcast(FP8X4),
                 rhs_scale=picked_scales(cols),
-                start=(side == H),
-                stop=(side == G),
+                start=(side == first),
+                stop=(side != first),
             )
 
-        def multiply(i, side, accs, pieces):
+        def multiply(i, side, accs, pieces, first=H):
             for acc, cols in zip(accs, pieces):
-                product(i, side, acc, cols)
+                product(i, side, acc, cols, first)
 
         def gather_words(cols):
             nc.vector.tensor_copy(x_code[:, cols], table_words[:].bitcast(U32).indirect(entries(offs_sb, cols)))
@@ -185,24 +191,26 @@ def tile_picked_ydpo_dpo_p_kernel(tc, x_words, x_scales, hT, gT, offs, win, los,
         stage_together(3)
         nc.vector.memset(table_scales[:].bitcast(I32), 0)
         warm_up()
+        sign_h = sbuf("sign_h", 1, F32)
+        nc.vector.memset(sign_h[:], SIGNS[H])
         nc.sync.dma_start(offs_sb[:], offs)
-        load(0, H)
+        load(H, 0, 192)
         load_scales()
-        load(0, G)
+        load(G, 0, 128)
         load_words()
-        load(1, H)
-        load(1, G)
+        load(G, 128, 256)
+        load(H, 192, 384)
         nc.sync.dma_start(los_sb[:], los)
-        load(2, H)
-        load(2, G)
-        load(3, H)
-        load(3, G)
+        load(G, 256, 384)
+        load(H, 384, 512)
+        load(G, 384, 512)
         nc.sync.dma_start(win_sb[:], win)
         x_scale[0] = sbuf("x_scale", S, U8)
         gather_scales(WHOLE[0])
         cast_s(0, H)
         cast_s(0, G)
         quantize_both(0)
+        cast_s(1, H, slice(0, 64))
         for cols in QUARTERS:
             gather_words(cols)
         acc0 = banks(0, 0, QUARTERS[1:])
@@ -210,25 +218,25 @@ def tile_picked_ydpo_dpo_p_kernel(tc, x_words, x_scales, hT, gT, offs, win, los,
         for acc, cols in zip(places0, QUARTERS):
             for side in (H, G):
                 product(0, side, acc, cols)
-        cast_g(1, H)
-        cast_s(1, G)
-        dd0 = sbuf("dd0", S, F32, takes_over="raw1h")
+        cast_g(1, G)
+        dst, src = by_runs(1, H, 4, slice(64, P))
+        nc.scalar.activation(dst, src, ACT.Copy, scale=sign_h[:])
+        dd0 = sbuf("dd0", S, F32, takes_over="sign_h")
         evac_s(dd0, acc0[0], HALVES[0])
         for acc, cols in zip(acc0[1:], QUARTERS[2:]):
             evac_s(dd0, acc, cols)
         acc1 = banks(4, 1, HALVES)
         acc2 = banks(6, 2, HALVES)
         acc3 = banks(0, 3, HALVES)
-
         rej0 = sbuf("rej0", U, F32)
         fetch_s(rej0, dd0, los_sb, ALL)
-        quantize(1, H)
-        multiply(1, H, acc1, HALVES)
         cast_v(2, H)
         quantize(1, G)
-        multiply(1, G, acc1, HALVES)
+        multiply(1, G, acc1, HALVES, first=G)
         cast_v(2, G)
-        dd1 = sbuf("dd1", S, F32, takes_over="raw2g")
+        quantize(1, H)
+        multiply(1, H, acc1, HALVES, first=G)
+        dd1 = sbuf("dd1", S, F32, takes_over="rawg256")
         for acc, cols in zip(acc1, HALVES):
             evac_s(dd1, acc, cols)
         quantize_both(2)
@@ -239,19 +247,20 @@ def tile_picked_ydpo_dpo_p_kernel(tc, x_words, x_scales, hT, gT, offs, win, los,
             cast_v(3, side)
             quantize(3, side)
             multiply(3, side, acc3, HALVES)
+
         dd2 = sbuf("dd2", S, F32)
         for acc, cols in zip(acc2, HALVES):
             evac_s(dd2, acc, cols)
         rej1 = sbuf("rej1", U, F32, takes_over="scales2")
-        m0 = sbuf("m0", U, F32, takes_over="raw3g")
+        m0 = sbuf("m0", U, F32, takes_over="rawg384")
         fetch_s(rej1, dd1, los_sb, ALL)
         fetch_sub(m0, dd0, win_sb, ALL, rej0)
         rej2 = sbuf("rej2", U, F32)
-        dd3 = sbuf("dd3", S, F32)
-        evac_s(dd3, acc3[0], HALVES[0])
         fetch_s(rej2, dd2, los_sb, ALL)
         finish(0, m0, ALL)
-        evac_v(dd3, acc3[1], HALVES[1])
+        dd3 = sbuf("dd3", S, F32)
+        for acc, cols in zip(acc3, HALVES):
+            evac_v(dd3, acc, cols)
         m12 = sbuf("m12", 2 * U, F32, takes_over="scales3g")
         m1, m2 = m12[:, :U], m12[:, U:]
         fetch_sub(m1, dd1, win_sb, ALL, rej1)

@@ -198,8 +198,8 @@ def tile_picked_ydpo_dpo_p_kernel(tc, x_words, x_scales, hT, gT, offs, win, los,
         load_scales()
         load(G, 0, 128)
         load_words()
-        load(G, 128, 256)
         load(H, 192, 384)
+        load(G, 128, 256)
         nc.sync.dma_start(los_sb[:], los)
         load(G, 256, 384)
         load(H, 384, 512)
@@ -218,10 +218,10 @@ def tile_picked_ydpo_dpo_p_kernel(tc, x_words, x_scales, hT, gT, offs, win, los,
         for acc, cols in zip(places0, QUARTERS):
             for side in (H, G):
                 product(0, side, acc, cols)
-        cast_g(1, G)
-        dst, src = by_runs(1, H, 4, slice(64, P))
+        cast_g(1, H, slice(64, P))
+        dst, src = by_runs(2, H, 4, slice(0, P))
         nc.scalar.activation(dst, src, ACT.Copy, scale=sign_h[:])
-        dd0 = sbuf("dd0", S, F32, takes_over="sign_h")
+        dd0 = sbuf("dd0", S, F32, takes_over="rawh192")
         evac_s(dd0, acc0[0], HALVES[0])
         for acc, cols in zip(acc0[1:], QUARTERS[2:]):
             evac_s(dd0, acc, cols)
@@ -230,12 +230,12 @@ def tile_picked_ydpo_dpo_p_kernel(tc, x_words, x_scales, hT, gT, offs, win, los,
         acc3 = banks(0, 3, HALVES)
         rej0 = sbuf("rej0", U, F32)
         fetch_s(rej0, dd0, los_sb, ALL)
-        cast_v(2, H)
+        cast_v(1, G)
+        quantize(1, H, takes_over="sign_h")
+        multiply(1, H, acc1, HALVES)
         quantize(1, G)
-        multiply(1, G, acc1, HALVES, first=G)
+        multiply(1, G, acc1, HALVES)
         cast_v(2, G)
-        quantize(1, H)
-        multiply(1, H, acc1, HALVES, first=G)
         dd1 = sbuf("dd1", S, F32, takes_over="rawg256")
         for acc, cols in zip(acc1, HALVES):
             evac_s(dd1, acc, cols)

@@ -186,7 +186,7 @@ def tile_picked_ydpo_dpo_p_kernel(tc, x_words, x_scales, hT, gT, offs, win, los,
         w = {}
 
         stage_together(0)
-        stage_apart(1)
+        grouped[1, G] = sbuf("grouped1g", P * PACK, BF16)[:]
         stage_together(2)
         stage_together(3)
         nc.vector.memset(table_scales[:].bitcast(I32), 0)
@@ -210,6 +210,7 @@ def tile_picked_ydpo_dpo_p_kernel(tc, x_words, x_scales, hT, gT, offs, win, los,
         cast_s(0, H)
         cast_s(0, G)
         quantize_both(0)
+        grouped[1, H] = sbuf("grouped1h", P * PACK, BF16, takes_over="rawg0")[:]
         cast_s(1, H, slice(0, 64))
         for cols in QUARTERS:
             gather_words(cols)

@@ -193,8 +193,8 @@ def tile_picked_ydpo_dpo_p_kernel(tc, x_words, x_scales, hT, gT, offs, win, los,
         warm_up()
         sign_h = sbuf("sign_h", 1, F32)
         nc.vector.memset(sign_h[:], SIGNS[H])
-        nc.sync.dma_start(offs_sb[:], offs)
         load(H, 0, 192)
+        nc.sync.dma_start(offs_sb[:], offs)
         load_scales()
         load(G, 0, 128)
         load_words()

@@ -186,7 +186,7 @@ def tile_picked_ydpo_dpo_p_kernel(tc, x_words, x_scales, hT, gT, offs, win, los,
         w = {}
 
         stage_together(0)
-        grouped[1, G] = sbuf("grouped1g", P * PACK, BF16)[:]
+        stage_apart(1)
         stage_together(2)
         stage_together(3)
         nc.vector.memset(table_scales[:].bitcast(I32), 0)
@@ -210,7 +210,6 @@ def tile_picked_ydpo_dpo_p_kernel(tc, x_words, x_scales, hT, gT, offs, win, los,
         cast_s(0, H)
         cast_s(0, G)
         quantize_both(0)
-        grouped[1, H] = sbuf("grouped1h", P * PACK, BF16, takes_over="rawg0")[:]
         cast_s(1, H, slice(0, 64))
         for cols in QUARTERS:
             gather_words(cols)

@@ -17,7 +17,6 @@ ALU = mybir.AluOpType
 
 P = 128
 PACK = 4
-TILES = V // P
 H, G = 0, 1
 SIGNS = (1.0, -1.0)
 SCALE_ROWS = K // 32
@@ -25,7 +24,10 @@ QUADRANT = 32
 FIRST, SECOND, ALL = slice(0, U // 2), slice(U // 2, U), slice(0, U)
 QUARTERS = tuple(slice(c, c + S // 4) for c in range(0, S, S // 4))
 HALVES = (slice(0, S // 2), slice(S // 2, S))
-WHOLE = (slice(0, S),)
+WHOLE = slice(0, S)
+COLS = slice(0, P)
+LINE = 256
+LEAD_X_SCALE, LEAD_CODES, LEAD_SCALES = 64, 32, 192
 
 
 def entries(list_tile, part):
@@ -39,7 +41,10 @@ def tile_picked_ydpo_dpo_p_kernel(tc, x_words, x_scales, hT, gT, offs, win, los,
         psum = ctx.enter_context(tc.psum_pool(name="psum", bufs=1))
 
         def sbuf(name, columns, dtype, takes_over=None):
-            return keep.tile([P, columns], dtype, name=name, tag=takes_over or name, align_bytes=64)
+            return keep.tile([P, columns], dtype, name=name, tag=takes_over or name, align_bytes=LINE)
+
+        def shifted(name, columns, dtype, lead, takes_over=None):
+            return sbuf(name, lead + columns, dtype, takes_over)[:, lead:]
 
         def label(kind, i, side):
             return "%s%d%s" % (kind, i, "hg"[side])
@@ -51,28 +56,28 @@ def tile_picked_ydpo_dpo_p_kernel(tc, x_words, x_scales, hT, gT, offs, win, los,
         table_scales = sbuf("table_scales", T, U8)
         raw = {}
         rows = [a.rearrange("(p j) t -> p j t", j=PACK) for a in (hT, gT)]
-        x_scale = {}
-        x_code = sbuf("x_code", S, U32)
-        grouped, both, codes, scales = {}, {}, {}, {}
+        x_scale, x_code = {}, {}
+        grouped, both, codes, scales, w = {}, {}, {}, {}, {}
 
-        def load(side, start, stop):
-            raw[side, start] = sbuf("raw%s%d" % ("hg"[side], start), PACK * (stop - start), F32)
-            nc.sync.dma_start(out=raw[side, start][:].rearrange("p (j t) -> p j t", j=PACK), in_=rows[side][:, :, start:stop])
+        def load(side, start, stop, queue=nc.sync, takes_over=None, pitch=None):
+            room = sbuf("raw%s%d" % ("hg"[side], start), PACK * (pitch or stop - start), F32, takes_over)
+            raw[side, start] = room[:].rearrange("p (j t) -> p j t", j=PACK)[:, :, : stop - start]
+            queue.dma_start(out=raw[side, start], in_=rows[side][:, :, start:stop])
 
         def loaded(i, side, cols):
             start = max(s for d, s in raw if d == side and s <= P * i + cols.start)
-            return raw[side, start][:], slice(P * i + cols.start - start, P * i + cols.stop - start)
+            return raw[side, start], slice(P * i + cols.start - start, P * i + cols.stop - start)
 
-        def load_scales():
+        def load_scales(queue=nc.sync):
             per_quadrant = SCALE_ROWS * QUADRANT // P
             for r in range(per_quadrant):
-                nc.sync.dma_start(
+                queue.dma_start(
                     out=table_scales[r:P:QUADRANT, :].bitcast(I32),
                     in_=x_scales[0, r:SCALE_ROWS:per_quadrant, :].bitcast(I32),
                 )
 
-        def load_words():
-            nc.sync.dma_start(out=table_words[:], in_=x_words[0].rearrange("p n r -> p (n r)").bitcast(I32))
+        def load_words(queue=nc.sync):
+            queue.dma_start(out=table_words[:], in_=x_words[0].rearrange("p n r -> p (n r)").bitcast(I32))
 
         def warm_up():
             warm_in = keep.tile([P, 1], F32, name="warm_in")
@@ -85,73 +90,86 @@ def tile_picked_ydpo_dpo_p_kernel(tc, x_words, x_scales, hT, gT, offs, win, los,
             for side in (H, G):
                 grouped[i, side] = both[i][:, P * PACK * side : P * PACK * (side + 1)]
 
-        def stage_apart(i):
-            for side in (H, G):
-                grouped[i, side] = sbuf(label("grouped", i, side), P * PACK, BF16)[:]
+        def stage(i, side, takes_over=None):
+            grouped[i, side] = sbuf(label("grouped", i, side), P * PACK, BF16, takes_over)[:]
 
         def by_runs(i, side, run, cols):
             source, place = loaded(i, side, cols)
             dst = grouped[i, side].rearrange("p (c l j) -> p c j l", l=run, j=PACK)
-            src = source.rearrange("p (j c l) -> p c j l", l=run, j=PACK)
+            src = source.rearrange("p j (c l) -> p c j l", l=run)
             return dst[:, cols.start // run : cols.stop // run], src[:, place.start // run : place.stop // run]
 
-        def cast_s(i, side, cols=slice(0, P)):
+        def cast_s(i, side, cols=COLS, sign=None):
             dst, src = by_runs(i, side, 4, cols)
-            if side == H:
+            if sign is not None:
+                nc.scalar.activation(dst, src, ACT.Copy, scale=sign[:])
+            elif side == H:
                 nc.scalar.copy(dst, src)
             else:
                 nc.scalar.activation(dst, src, ACT.Copy, scale=SIGNS[side])
 
-        def cast_v(i, side, cols=slice(0, P)):
+        def cast_v(i, side, cols=COLS, sign=None):
             dst, src = by_runs(i, side, 2, cols)
-            nc.vector.tensor_scalar(dst, src, SIGNS[side], None, ALU.mult)
+            nc.vector.tensor_scalar(dst, src, SIGNS[side] if sign is None else sign[:], None, ALU.mult)
 
-        def cast_g(i, side, cols=slice(0, P)):
+        def cast_g(i, side, cols=COLS):
             dst = grouped[i, side].rearrange("p (t j) -> p t j", j=PACK)[:, cols]
             source, place = loaded(i, side, cols)
-            src = source.rearrange("p (j t) -> p t j", j=PACK)[:, place]
+            src = source.rearrange("p j t -> p t j")[:, place]
+            nc.gpsimd.tensor_scalar(dst, src, SIGNS[side], 0.0, ALU.mult, ALU.add)
+
+        def cast_across_g(row, first, side, start, stop):
+            origin = max(s for d, s in raw if d == side and s <= start)
+            dst = row.rearrange("p (t j) -> p t j", j=PACK)[:, start - first : stop - first]
+            src = raw[side, origin].rearrange("p j t -> p t j")[:, start - origin : stop - origin]
             nc.gpsimd.tensor_scalar(dst, src, SIGNS[side], 0.0, ALU.mult, ALU.add)
 
         def quantize_both(i, takes_over=None):
-            code = sbuf("codes%d" % i, 2 * P, U32, takes_over)
-            plane = sbuf("scales%d" % i, 2 * P, U8)
+            code = shifted("codes%d" % i, 2 * P, U32, LEAD_CODES, takes_over)
+            plane = shifted("scales%d" % i, 2 * P, U8, LEAD_SCALES)
             for side in (H, G):
                 codes[i, side] = code[:, P * side : P * (side + 1)]
                 scales[i, side] = plane[:, P * side : P * (side + 1)]
-            nc.vector.quantize_mx(out=code[:].bitcast(FP8X4), scales=plane[:], in_=both[i][:, :])
+            nc.vector.quantize_mx(out=code.bitcast(FP8X4), scales=plane, in_=both[i][:, :])
 
         def quantize(i, side, takes_over=None):
-            codes[i, side] = sbuf(label("codes", i, side), P, U32, takes_over)[:]
-            scales[i, side] = sbuf(label("scales", i, side), P, U8)[:]
+            codes[i, side] = shifted(label("codes", i, side), P, U32, LEAD_CODES, takes_over)
+            scales[i, side] = shifted(label("scales", i, side), P, U8, LEAD_SCALES)
             nc.vector.quantize_mx(out=codes[i, side].bitcast(FP8X4), scales=scales[i, side], in_=grouped[i, side])
 
-        def banks(first, i, pieces):
-            return [psum.tile([P, S], F32, name="acc%d_%d" % (i, n), tag="bank%d" % (first + n)) for n in range(len(pieces))]
+        def bank(number, name):
+            return psum.tile([P, S], F32, name=name, tag="bank%d" % number)
 
-        def picked_scales(cols):
-            start = max(c for c in x_scale if c <= cols.start)
-            return x_scale[start][:, cols.start - start : cols.stop - start]
+        def banks(first, i, count):
+            return [bank(first + n, "acc%d_%d" % (i, n)) for n in range(count)]
 
-        def product(i, side, acc, cols, first=H):
+        def picked(pieces, cols):
+            start = max(c for c in pieces if c <= cols.start)
+            return pieces[start][:, cols.start - start : cols.stop - start]
+
+        def product(i, side, acc, cols, start, stop):
             nc.tensor.matmul_mx(
                 out=acc[:, : cols.stop - cols.start],
                 lhsT=codes[i, side].bitcast(FP8X4),
                 lhsT_scale=scales[i, side],
-                rhs=x_code[:, cols].bitcast(FP8X4),
-                rhs_scale=picked_scales(cols),
-                start=(side == first),
-                stop=(side != first),
+                rhs=picked(x_code, cols).bitcast(FP8X4),
+                rhs_scale=picked(x_scale, cols),
+                start=start,
+                stop=stop,
             )
 
-        def multiply(i, side, accs, pieces, first=H):
-            for acc, cols in zip(accs, pieces):
-                product(i, side, acc, cols, first)
+        def multiply(i, side, accs, halves=HALVES):
+            for acc, half in zip(accs, halves):
+                cuts = [c for c in sorted(x_code) if half.start < c < half.stop]
+                edges = [half.start] + cuts + [half.stop]
+                for a, b in zip(edges, edges[1:]):
+                    product(i, side, acc[:, a - half.start :], slice(a, b), side == H and a == half.start, side == G and b == half.stop)
 
         def gather_words(cols):
-            nc.vector.tensor_copy(x_code[:, cols], table_words[:].bitcast(U32).indirect(entries(offs_sb, cols)))
+            nc.vector.tensor_copy(picked(x_code, cols), table_words[:].bitcast(U32).indirect(entries(offs_sb, cols)))
 
         def gather_scales(cols):
-            nc.vector.tensor_copy(picked_scales(cols), table_scales[:].indirect(entries(offs_sb, cols)))
+            nc.vector.tensor_copy(picked(x_scale, cols), table_scales[:].indirect(entries(offs_sb, cols)))
 
         def evac_s(dd, acc, cols):
             nc.scalar.copy(dd[:, cols], acc[:, : cols.stop - cols.start])
@@ -168,25 +186,19 @@ def tile_picked_ydpo_dpo_p_kernel(tc, x_words, x_scales, hT, gT, offs, win, los,
         def fetch_sub(dst, dd, lst, pairs, other):
             nc.vector.tensor_tensor(dst[:, pairs], dd[:].indirect(entries(lst, pairs)), other[:, pairs], ALU.subtract)
 
-        def sub(engine, dst, a, b, pairs):
-            engine.tensor_tensor(dst[:, pairs], a[:, pairs], b[:, pairs], ALU.subtract)
-
-        def weigh(weight, margin, pairs, scale=-0.5):
-            nc.scalar.activation(weight[:, pairs], margin[:, pairs], ACT.Sigmoid, scale=scale)
-
-        def store(i, weight, pairs):
-            nc.sync.dma_start(out=out[P * i : P * (i + 1), pairs], in_=weight[:, pairs])
-
         def finish(i, margin, pairs, scale=-0.5):
             if i not in w:
                 w[i] = sbuf("w%d" % i, U, F32)
-            weigh(w[i], margin, pairs, scale)
-            store(i, w[i], pairs)
+            nc.scalar.activation(w[i][:, pairs], margin[:, pairs], ACT.Sigmoid, scale=scale)
+            nc.sync.dma_start(out=out[P * i : P * (i + 1), pairs], in_=w[i][:, pairs])
 
-        w = {}
+        def clock(name, ap):
+            tick = keep.tile([P, 1], ap.dtype, name=name)
+            nc.gpsimd.tensor_copy(tick[:], ap)
 
         stage_together(0)
-        stage_apart(1)
+        stage(1, H)
+        stage(1, G)
         stage_together(2)
         stage_together(3)
         nc.vector.memset(table_scales[:].bitcast(I32), 0)
@@ -205,48 +217,48 @@ def tile_picked_ydpo_dpo_p_kernel(tc, x_words, x_scales, hT, gT, offs, win, los,
         load(H, 384, 512)
         load(G, 384, 512)
         nc.sync.dma_start(win_sb[:], win)
-        x_scale[0] = sbuf("x_scale", S, U8)
-        gather_scales(WHOLE[0])
+        x_scale[0] = shifted("x_scale", S, U8, LEAD_X_SCALE)
+        x_code[0] = sbuf("x_code", S, U32)
+        gather_scales(WHOLE)
         cast_s(0, H)
         cast_s(0, G)
         quantize_both(0)
         cast_s(1, H, slice(0, 64))
         for cols in QUARTERS:
             gather_words(cols)
-        acc0 = banks(0, 0, QUARTERS[1:])
+        acc0 = banks(0, 0, 3)
         places0 = [acc0[0][:, : S // 4], acc0[0][:, S // 4 : S // 2], acc0[1], acc0[2]]
         for acc, cols in zip(places0, QUARTERS):
             for side in (H, G):
-                product(0, side, acc, cols)
+                product(0, side, acc, cols, side == H, side == G)
         cast_g(1, H, slice(64, P))
-        dst, src = by_runs(2, H, 4, slice(0, P))
-        nc.scalar.activation(dst, src, ACT.Copy, scale=sign_h[:])
+        cast_s(2, H, sign=sign_h)
         dd0 = sbuf("dd0", S, F32, takes_over="rawh192")
         evac_s(dd0, acc0[0], HALVES[0])
         for acc, cols in zip(acc0[1:], QUARTERS[2:]):
             evac_s(dd0, acc, cols)
-        acc1 = banks(4, 1, HALVES)
-        acc2 = banks(6, 2, HALVES)
-        acc3 = banks(0, 3, HALVES)
+        acc1 = banks(4, 1, 2)
+        acc2 = banks(6, 2, 2)
+        acc3 = banks(0, 3, 2)
         rej0 = sbuf("rej0", U, F32)
         fetch_s(rej0, dd0, los_sb, ALL)
         cast_v(1, G)
         quantize(1, H, takes_over="sign_h")
-        multiply(1, H, acc1, HALVES)
+        multiply(1, H, acc1)
         quantize(1, G)
-        multiply(1, G, acc1, HALVES)
+        multiply(1, G, acc1)
         cast_v(2, G)
         dd1 = sbuf("dd1", S, F32, takes_over="rawg256")
         for acc, cols in zip(acc1, HALVES):
             evac_s(dd1, acc, cols)
         quantize_both(2)
-        for acc, cols in zip(acc2, HALVES):
+        for acc, half in zip(acc2, HALVES):
             for side in (H, G):
-                product(2, side, acc, cols)
+                multiply(2, side, [acc], [half])
         for side in (H, G):
             cast_v(3, side)
             quantize(3, side)
-            multiply(3, side, acc3, HALVES)
+            multiply(3, side, acc3)
 
         dd2 = sbuf("dd2", S, F32)
         for acc, cols in zip(acc2, HALVES):

@@ -49,9 +49,9 @@ def tile_picked_ydpo_dpo_p_kernel(tc, x_words, x_scales, hT, gT, offs, win, los,
         def label(kind, i, side):
             return "%s%d%s" % (kind, i, "hg"[side])
 
-        offs_sb = keep.tile([P, S // 16], U16, name="offs_sb")
-        win_sb = keep.tile([P, U // 16], U16, name="win_sb")
-        los_sb = keep.tile([P, U // 16], U16, name="los_sb")
+        offs_sb = keep.tile([P, S // 16], U16, name="offs_sb", align_bytes=LINE)
+        win_sb = keep.tile([P, U // 16], U16, name="win_sb", align_bytes=LINE)
+        los_sb = keep.tile([P, U // 16], U16, name="los_sb", align_bytes=LINE)
         table_words = sbuf("table_words", T, I32)
         table_scales = sbuf("table_scales", T, U8)
         raw = {}
@@ -197,21 +197,20 @@ def tile_picked_ydpo_dpo_p_kernel(tc, x_words, x_scales, hT, gT, offs, win, los,
             nc.gpsimd.tensor_copy(tick[:], ap)
 
         stage_together(0)
-        stage(1, H)
-        stage(1, G)
         stage_together(2)
-        stage_together(3)
+        stage(3, H)
+        stage(3, G)
         nc.vector.memset(table_scales[:].bitcast(I32), 0)
         warm_up()
-        sign_h = sbuf("sign_h", 1, F32)
-        nc.vector.memset(sign_h[:], SIGNS[H])
-        load(H, 0, 192)
+        sign_g = sbuf("sign_g", 1, F32)
+        nc.vector.memset(sign_g[:], SIGNS[G])
+        load(H, 0, 256)
         nc.sync.dma_start(offs_sb[:], offs)
         load_scales()
         load(G, 0, 128)
         load_words()
-        load(H, 192, 384)
         load(G, 128, 256)
+        load(H, 256, 384)
         nc.sync.dma_start(los_sb[:], los)
         load(G, 256, 384)
         load(H, 384, 512)
@@ -223,7 +222,8 @@ def tile_picked_ydpo_dpo_p_kernel(tc, x_words, x_scales, hT, gT, offs, win, los,
         cast_s(0, H)
         cast_s(0, G)
         quantize_both(0)
-        cast_s(1, H, slice(0, 64))
+        stage_together(1, takes_over="rawg0")
+        cast_s(1, H)
         for cols in QUARTERS:
             gather_words(cols)
         acc0 = banks(0, 0, 3)
@@ -231,9 +231,9 @@ def tile_picked_ydpo_dpo_p_kernel(tc, x_words, x_scales, hT, gT, offs, win, los,
         for acc, cols in zip(places0, QUARTERS):
             for side in (H, G):
                 product(0, side, acc, cols, side == H, side == G)
-        cast_g(1, H, slice(64, P))
-        cast_s(2, H, sign=sign_h)
-        dd0 = sbuf("dd0", S, F32, takes_over="rawh192")
+        cast_s(1, G)
+        cast_s(2, H)
+        dd0 = sbuf("dd0", S, F32, takes_over="rawg128")
         evac_s(dd0, acc0[0], HALVES[0])
         for acc, cols in zip(acc0[1:], QUARTERS[2:]):
             evac_s(dd0, acc, cols)
@@ -242,11 +242,10 @@ def tile_picked_ydpo_dpo_p_kernel(tc, x_words, x_scales, hT, gT, offs, win, los,
         acc3 = banks(0, 3, 2)
         rej0 = sbuf("rej0", U, F32)
         fetch_s(rej0, dd0, los_sb, ALL)
-        cast_v(1, G)
-        quantize(1, H, takes_over="sign_h")
-        multiply(1, H, acc1)
-        quantize(1, G)
-        multiply(1, G, acc1)
+        quantize_both(1)
+        for acc, half in zip(acc1, HALVES):
+            for side in (H, G):
+                multiply(1, side, [acc], [half])
         cast_v(2, G)
         dd1 = sbuf("dd1", S, F32, takes_over="rawg256")
         for acc, cols in zip(acc1, HALVES):
@@ -255,18 +254,22 @@ def tile_picked_ydpo_dpo_p_kernel(tc, x_words, x_scales, hT, gT, offs, win, los,
         for acc, half in zip(acc2, HALVES):
             for side in (H, G):
                 multiply(2, side, [acc], [half])
-        for side in (H, G):
-            cast_v(3, side)
-            quantize(3, side)
-            multiply(3, side, acc3)
+        cast_v(3, H)
+        cast_v(3, G, slice(0, 8), sign=sign_g)
+        cast_v(3, G, slice(8, P))
+        quantize(3, H, takes_over="sign_g")
+        multiply(3, H, acc3)
+        quantize(3, G)
+        multiply(3, G, acc3)
 
         dd2 = sbuf("dd2", S, F32)
         for acc, cols in zip(acc2, HALVES):
             evac_s(dd2, acc, cols)
         rej1 = sbuf("rej1", U, F32, takes_over="scales2")
         m0 = sbuf("m0", U, F32, takes_over="rawg384")
-        fetch_s(rej1, dd1, los_sb, ALL)
+        fetch_s(rej1, dd1, los_sb, slice(0, U - 128))
         fetch_sub(m0, dd0, win_sb, ALL, rej0)
+        fetch_v(rej1, dd1, los_sb, slice(U - 128, U))
         rej2 = sbuf("rej2", U, F32)
         fetch_s(rej2, dd2, los_sb, ALL)
         finish(0, m0, ALL)

from contextlib import ExitStack

import concourse.mybir as mybir

K, T, S, V, U = 512, 1024, 512, 512, 256
FLOPS = 2 * 2 * K * V * S

F32 = mybir.dt.float32
BF16 = mybir.dt.bfloat16
I32 = mybir.dt.int32
U32 = mybir.dt.uint32
U16 = mybir.dt.uint16
U8 = mybir.dt.uint8
FP8X4 = mybir.dt.float8_e4m3fn_x4
ACT = mybir.ActivationFunctionType
ALU = mybir.AluOpType

P = 128
PACK = 4
H, G = 0, 1
SIGNS = (1.0, -1.0)
SCALE_ROWS = K // 32
QUADRANT = 32
FIRST, SECOND, ALL = slice(0, U // 2), slice(U // 2, U), slice(0, U)
QUARTERS = tuple(slice(c, c + S // 4) for c in range(0, S, S // 4))
HALVES = (slice(0, S // 2), slice(S // 2, S))
WHOLE = slice(0, S)
COLS = slice(0, P)
LINE = 256
LEAD_X_SCALE, LEAD_CODES, LEAD_SCALES = 64, 32, 192


def entries(list_tile, part):
    return list_tile[:, part.start // 16 : part.stop // 16]


def tile_picked_ydpo_dpo_p_kernel(tc, x_words, x_scales, hT, gT, offs, win, los, out):
    nc = tc.nc
    with ExitStack() as ctx:
        keep = ctx.enter_context(tc.tile_pool(name="keep", bufs=1))
        psum = ctx.enter_context(tc.psum_pool(name="psum", bufs=1))

        def sbuf(name, columns, dtype, takes_over=None):
            return keep.tile([P, columns], dtype, name=name, tag=takes_over or name, align_bytes=LINE)

        def shifted(name, columns, dtype, lead, takes_over=None):
            return sbuf(name, lead + columns, dtype, takes_over)[:, lead:]

        def label(kind, i, side):
            return "%s%d%s" % (kind, i, "hg"[side])

        offs_sb = keep.tile([P, S // 16], U16, name="offs_sb", align_bytes=LINE)
        win_sb = keep.tile([P, U // 16], U16, name="win_sb", align_bytes=LINE)
        los_sb = keep.tile([P, U // 16], U16, name="los_sb", align_bytes=LINE)
        table_words = sbuf("table_words", T, I32)
        table_scales = sbuf("table_scales", T, U8)
        raw = {}
        rows = [a.rearrange("(p j) t -> p j t", j=PACK) for a in (hT, gT)]
        x_scale, x_code = {}, {}
        grouped, both, codes, scales, w = {}, {}, {}, {}, {}

        def load(side, start, stop, queue=nc.sync, takes_over=None, pitch=None):
            room = sbuf("raw%s%d" % ("hg"[side], start), PACK * (pitch or stop - start), F32, takes_over)
            raw[side, start] = room[:].rearrange("p (j t) -> p j t", j=PACK)[:, :, : stop - start]
            queue.dma_start(out=raw[side, start], in_=rows[side][:, :, start:stop])

        def loaded(i, side, cols):
            start = max(s for d, s in raw if d == side and s <= P * i + cols.start)
            return raw[side, start], slice(P * i + cols.start - start, P * i + cols.stop - start)

        def load_scales(queue=nc.sync):
            per_quadrant = SCALE_ROWS * QUADRANT // P
            for r in range(per_quadrant):
                queue.dma_start(
                    out=table_scales[r:P:QUADRANT, :].bitcast(I32),
                    in_=x_scales[0, r:SCALE_ROWS:per_quadrant, :].bitcast(I32),
                )

        def load_words(queue=nc.sync):
            queue.dma_start(out=table_words[:], in_=x_words[0].rearrange("p n r -> p (n r)").bitcast(I32))

        def warm_up():
            warm_in = keep.tile([P, 1], F32, name="warm_in")
            warm_out = keep.tile([P, 1], F32, name="warm_out")
            nc.vector.memset(warm_in[:], 0.0)
            nc.scalar.activation(warm_out[:], warm_in[:], ACT.Sigmoid)

        def stage_together(i, takes_over=None):
            both[i] = sbuf("grouped%d" % i, 2 * P * PACK, BF16, takes_over)
            for side in (H, G):
                grouped[i, side] = both[i][:, P * PACK * side : P * PACK * (side + 1)]

        def stage(i, side, takes_over=None):
            grouped[i, side] = sbuf(label("grouped", i, side), P * PACK, BF16, takes_over)[:]

        def by_runs(i, side, run, cols):
            source, place = loaded(i, side, cols)
            dst = grouped[i, side].rearrange("p (c l j) -> p c j l", l=run, j=PACK)
            src = source.rearrange("p j (c l) -> p c j l", l=run)
            return dst[:, cols.start // run : cols.stop // run], src[:, place.start // run : place.stop // run]

        def cast_s(i, side, cols=COLS, sign=None):
            dst, src = by_runs(i, side, 4, cols)
            if sign is not None:
                nc.scalar.activation(dst, src, ACT.Copy, scale=sign[:])
            elif side == H:
                nc.scalar.copy(dst, src)
            else:
                nc.scalar.activation(dst, src, ACT.Copy, scale=SIGNS[side])

        def cast_v(i, side, cols=COLS, sign=None):
            dst, src = by_runs(i, side, 2, cols)
            nc.vector.tensor_scalar(dst, src, SIGNS[side] if sign is None else sign[:], None, ALU.mult)

        def cast_g(i, side, cols=COLS):
            dst = grouped[i, side].rearrange("p (t j) -> p t j", j=PACK)[:, cols]
            source, place = loaded(i, side, cols)
            src = source.rearrange("p j t -> p t j")[:, place]
            nc.gpsimd.tensor_scalar(dst, src, SIGNS[side], 0.0, ALU.mult, ALU.add)

        def cast_across_g(row, first, side, start, stop):
            origin = max(s for d, s in raw if d == side and s <= start)
            dst = row.rearrange("p (t j) -> p t j", j=PACK)[:, start - first : stop - first]
            src = raw[side, origin].rearrange("p j t -> p t j")[:, start - origin : stop - origin]
            nc.gpsimd.tensor_scalar(dst, src, SIGNS[side], 0.0, ALU.mult, ALU.add)

        def quantize_both(i, takes_over=None):
            code = shifted("codes%d" % i, 2 * P, U32, LEAD_CODES, takes_over)
            plane = shifted("scales%d" % i, 2 * P, U8, LEAD_SCALES)
            for side in (H, G):
                codes[i, side] = code[:, P * side : P * (side + 1)]
                scales[i, side] = plane[:, P * side : P * (side + 1)]
            nc.vector.quantize_mx(out=code.bitcast(FP8X4), scales=plane, in_=both[i][:, :])

        def quantize(i, side, takes_over=None):
            codes[i, side] = shifted(label("codes", i, side), P, U32, LEAD_CODES, takes_over)
            scales[i, side] = shifted(label("scales", i, side), P, U8, LEAD_SCALES)
            nc.vector.quantize_mx(out=codes[i, side].bitcast(FP8X4), scales=scales[i, side], in_=grouped[i, side])

        def bank(number, name):
            return psum.tile([P, S], F32, name=name, tag="bank%d" % number)

        def banks(first, i, count):
            return [bank(first + n, "acc%d_%d" % (i, n)) for n in range(count)]

        def picked(pieces, cols):
            start = max(c for c in pieces if c <= cols.start)
            return pieces[start][:, cols.start - start : cols.stop - start]

        def product(i, side, acc, cols, start, stop):
            nc.tensor.matmul_mx(
                out=acc[:, : cols.stop - cols.start],
                lhsT=codes[i, side].bitcast(FP8X4),
                lhsT_scale=scales[i, side],
                rhs=picked(x_code, cols).bitcast(FP8X4),
                rhs_scale=picked(x_scale, cols),
                start=start,
                stop=stop,
            )

        def multiply(i, side, accs, halves=HALVES):
            for acc, half in zip(accs, halves):
                cuts = [c for c in sorted(x_code) if half.start < c < half.stop]
                edges = [half.start] + cuts + [half.stop]
                for a, b in zip(edges, edges[1:]):
                    product(i, side, acc[:, a - half.start :], slice(a, b), side == H and a == half.start, side == G and b == half.stop)

        def gather_words(cols):
            nc.vector.tensor_copy(picked(x_code, cols), table_words[:].bitcast(U32).indirect(entries(offs_sb, cols)))

        def gather_scales(cols):
            nc.vector.tensor_copy(picked(x_scale, cols), table_scales[:].indirect(entries(offs_sb, cols)))

        def evac_s(dd, acc, cols):
            nc.scalar.copy(dd[:, cols], acc[:, : cols.stop - cols.start])

        def evac_v(dd, acc, cols):
            nc.vector.tensor_copy(dd[:, cols], acc[:, : cols.stop - cols.start])

        def fetch_s(dst, dd, lst, pairs):
            nc.scalar.activation(dst[:, pairs], dd[:].indirect(entries(lst, pairs)), ACT.Copy)

        def fetch_v(dst, dd, lst, pairs):
            nc.vector.tensor_copy(dst[:, pairs], dd[:].indirect(entries(lst, pairs)))

        def fetch_sub(dst, dd, lst, pairs, other):
            nc.vector.tensor_tensor(dst[:, pairs], dd[:].indirect(entries(lst, pairs)), other[:, pairs], ALU.subtract)

        def finish(i, margin, pairs, scale=-0.5):
            if i not in w:
                w[i] = sbuf("w%d" % i, U, F32)
            nc.scalar.activation(w[i][:, pairs], margin[:, pairs], ACT.Sigmoid, scale=scale)
            nc.sync.dma_start(out=out[P * i : P * (i + 1), pairs], in_=w[i][:, pairs])

        def clock(name, ap):
            tick = keep.tile([P, 1], ap.dtype, name=name)
            nc.gpsimd.tensor_copy(tick[:], ap)

        stage_together(0)
        stage_together(2)
        stage(3, H)
        stage(3, G)
        nc.vector.memset(table_scales[:].bitcast(I32), 0)
        warm_up()
        sign_g = sbuf("sign_g", 1, F32)
        nc.vector.memset(sign_g[:], SIGNS[G])
        load(H, 0, 256)
        nc.sync.dma_start(offs_sb[:], offs)
        load_scales()
        load(G, 0, 128)
        load_words()
        load(G, 128, 256)
        load(H, 256, 384)
        nc.sync.dma_start(los_sb[:], los)
        load(G, 256, 384)
        load(H, 384, 512)
        load(G, 384, 512)
        nc.sync.dma_start(win_sb[:], win)
        x_scale[0] = shifted("x_scale", S, U8, LEAD_X_SCALE)
        x_code[0] = sbuf("x_code", S, U32)
        gather_scales(WHOLE)
        cast_s(0, H)
        cast_s(0, G)
        quantize_both(0)
        stage_together(1, takes_over="rawg0")
        cast_s(1, H)
        for cols in QUARTERS:
            gather_words(cols)
        acc0 = banks(0, 0, 3)
        places0 = [acc0[0][:, : S // 4], acc0[0][:, S // 4 : S // 2], acc0[1], acc0[2]]
        for acc, cols in zip(places0, QUARTERS):
            for side in (H, G):
                product(0, side, acc, cols, side == H, side == G)
        cast_s(1, G)
        cast_s(2, H)
        dd0 = sbuf("dd0", S, F32, takes_over="rawg128")
        evac_s(dd0, acc0[0], HALVES[0])
        for acc, cols in zip(acc0[1:], QUARTERS[2:]):
            evac_s(dd0, acc, cols)
        acc1 = banks(4, 1, 2)
        acc2 = banks(6, 2, 2)
        acc3 = banks(0, 3, 2)
        rej0 = sbuf("rej0", U, F32)
        fetch_s(rej0, dd0, los_sb, ALL)
        quantize_both(1)
        for acc, half in zip(acc1, HALVES):
            for side in (H, G):
                multiply(1, side, [acc], [half])
        cast_v(2, G)
        dd1 = sbuf("dd1", S, F32, takes_over="rawg256")
        for acc, cols in zip(acc1, HALVES):
            evac_s(dd1, acc, cols)
        quantize_both(2)
        for acc, half in zip(acc2, HALVES):
            for side in (H, G):
                multiply(2, side, [acc], [half])
        cast_v(3, H)
        cast_v(3, G, slice(0, 8), sign=sign_g)
        cast_v(3, G, slice(8, P))
        quantize(3, H, takes_over="sign_g")
        multiply(3, H, acc3)
        quantize(3, G)
        multiply(3, G, acc3)

        dd2 = sbuf("dd2", S, F32)
        for acc, cols in zip(acc2, HALVES):
            evac_s(dd2, acc, cols)
        rej1 = sbuf("rej1", U, F32, takes_over="scales2")
        m0 = sbuf("m0", U, F32, takes_over="rawg384")
        fetch_s(rej1, dd1, los_sb, slice(0, U - 128))
        fetch_sub(m0, dd0, win_sb, ALL, rej0)
        fetch_v(rej1, dd1, los_sb, slice(U - 128, U))
        rej2 = sbuf("rej2", U, F32)
        fetch_s(rej2, dd2, los_sb, ALL)
        finish(0, m0, ALL)
        dd3 = sbuf("dd3", S, F32)
        for acc, cols in zip(acc3, HALVES):
            evac_v(dd3, acc, cols)
        m12 = sbuf("m12", 2 * U, F32, takes_over="scales3g")
        m1, m2 = m12[:, :U], m12[:, U:]
        fetch_sub(m1, dd1, win_sb, ALL, rej1)
        fetch_sub(m2, dd2, win_sb, ALL, rej2)
        rej3 = sbuf("rej3", U, F32)
        for pairs in (FIRST, SECOND):
            fetch_s(rej3, dd3, los_sb, pairs)
        m3 = sbuf("m3", U, F32)
        for pairs in (FIRST, SECOND):
            fetch_sub(m3, dd3, win_sb, pairs, rej3)
        finish(1, m1, ALL)
        finish(2, m2, ALL)
        for pairs in (FIRST, SECOND):
            finish(3, m3, pairs)
